import numpy as np, ml_dtypes
CORES = [48,51,52,55]
N = 4
import mx_ref
BF = ml_dtypes.bfloat16
def tile(rs):
    return np.stack(rs, axis=2).reshape(128, -1).astype(BF)
def pick(q, e):
    c = np.concatenate([q[0].reshape(128, -1, 4), np.zeros((128, 1, 4), np.uint8)], axis=1); s = np.concatenate([q[1], np.ones((16, 1), np.uint8)], axis=1)
    return (np.ascontiguousarray(c[:, e].reshape(128, -1)), np.ascontiguousarray(s[:, e]))
def join(*qs):
    return (np.concatenate([q[0] for q in qs], axis=1), np.concatenate([q[1] for q in qs], axis=1))
def put(q, e, v):
    c, s = q[0].reshape(128, -1, 4).copy(), q[1].copy(); c[:, e] = v[0].reshape(128, -1, 4); s[:, e] = v[1]
    return (c.reshape(128, -1), s)
def pk(c, s):
    return (np.ascontiguousarray(c), mx_ref.live(s))
def emit(q):
    return q[0], q[1]
def packed(v, rng):
    q = [mx_ref.quantize(np.ascontiguousarray(v[r])) for r in range(N)]
    return np.stack([a for a, b in q]), np.stack([mx_ref.plane(b, rng) for a, b in q])
def values_of_codes():
    e, c = np.zeros((128, 128, 4), np.float32), np.zeros((128, 2, 4), np.uint8)
    e[np.arange(128), np.arange(128), 0] = 1
    c[:127, :, 0] = np.arange(256).reshape(2, 128).T[:127]
    return mx_ref.matmul(mx_ref.quantize(e.reshape(128, 512).astype(BF)), (c.reshape(128, 8), np.full((16, 2), 127, np.uint8))).T.reshape(-1).astype(np.float64)
CODE_VALUE, SCALE_VALUE = values_of_codes(), 2.0 ** (np.arange(256) - 127.0)
def decode(q):
    return (CODE_VALUE[q[0]].reshape(16, 8, -1, 4) * SCALE_VALUE[q[1]][:, None, :, None] + 0.0).reshape(128, -1).astype(np.float32)
def f(rng, *shape):
    return mx_ref.flush((rng.standard_normal(shape, dtype=np.float32) * np.exp2(rng.integers(-2, 3, shape[:-1] + (1,)))).astype(BF))
def wide(rng, *shape, cols=0):
    v = rng.standard_normal(shape, dtype=np.float32) * np.exp2(rng.integers(-12, 13, shape)).astype(np.float32)
    if cols: v *= np.repeat(np.exp2(rng.integers(-cols, cols + 1, shape[:-2] + (1, shape[-1] // 4))) * (rng.random(shape[:-2] + (1, shape[-1] // 4)) > 0.0625), 4, axis=-1).astype(np.float32)
    return mx_ref.flush(v.astype(BF))
C, M, P, V, K, R = 448, 14, 32, 6, 24, 3
def numbers_of(rng):
    return {"x": np.array(f(rng, N, 128, 4 * C)), "u": np.array(f(rng, N, 128, 512)), "v": np.array(f(rng, N, 128, 512))}
def weights(rng, w):
    c, p = packed(np.ascontiguousarray(w).reshape(N, 128, 2048), rng)
    return {"wc": c, "ws": p}
def layers(rng, still=[]):
    w = np.array(f(rng, N, 128, 2048)).reshape(N, 8, 16, 4, 8, 16, 4)
    for i in still:
        w[:, :, i] = 0
        w[:, :, :, :, :, i] = 0
    return weights(rng, w)
def setup_inputs(rng):
    return {**numbers_of(rng), **layers(rng)}
def setup_inputs_ties(rng):
    d = numbers_of(rng)
    x = d["x"].reshape(N, 8, 16, C, 4)
    x[:, :, 0] = 0
    x[:, :, 0, :, 0] = rng.integers(1, 4, (N, 8, C)).astype(np.float32).astype(BF)
    u = d["u"].reshape(N, 128, 128, 4)
    u[:, :, ::16] = 0
    o = rng.permutation(N)
    for r in range(N):
        for h in range(0, 128, 16): u[r, h, h, 0] = 0.0 if r == o[0] else -1.0 if r == o[1] else 1.0
    return {"x": x.reshape(N, 128, 4 * C), "u": u.reshape(N, 128, 512), "v": d["v"], **layers(rng, [0])}
def setup_inputs_near(rng):
    d = numbers_of(rng)
    x = d["x"].astype(np.float32).reshape(N, 8, 16, C, 4)
    x[:, :, 0] = 0
    x[:, :, 8:] = 0
    s = rng.integers(0, 16, (N, 8, C))
    x[:, :, 8] = ((s[:, :, :, None] >> np.arange(4)) & 1) * np.exp2(np.arange(4) - 23.0)
    u = d["u"].reshape(N, 128, 128, 4)
    u[:, :, ::16] = 0
    o = rng.permutation(N) % 4
    for r in range(N):
        if o[r] < 2:
            x[r, :, 0, :, 0] = np.repeat(rng.integers(0, 2, P) * 2.0 - 1.0, M)
            x[r, :, 11, :, 0] = 2.0 ** -10
        elif o[r] == 2:
            a = rng.permutation(M)
            x[r, :, 0, int(a[0])::M, 0] = 1.0
            x[r, :, 0, int(a[1])::M, 0] = -1.0
        else:
            x[r, :, 8] = 0
            x[r, :, 10, :, 0] = (1.0 + 0.125 * rng.integers(0, 2, (8, C))) * 2.0 ** -30
            for g in rng.permutation(8)[:4]: x[r, g, 0, rng.integers(C), 0] = 2.0 ** 30
        k = 1.0 if o[r] == 0 else 2.0 ** -30
        for h in range(0, 128, 16):
            u[r, h, h, 0] = k if o[r] < 2 else 1.0
            if o[r] < 3: u[r, h + 8, h] = k
            else: u[r, h + 10, h, 0] = k
            if o[r] < 2: u[r, h + 11, h, 0] = k
    return {"x": x.reshape(N, 128, 4 * C).astype(BF), "u": u.reshape(N, 128, 512), "v": d["v"], **layers(rng, [0, 8, 9, 10, 11, 12, 13, 14, 15])}
def setup_inputs_huge(rng):
    d = numbers_of(rng)
    c = rng.choice([-1.0, 1.0], (N, P, M))
    c[:, ::2] = -1.0
    e = rng.integers(N)
    x = 0.7 + 0.25 * rng.random((N, 8, 16, C, 4))
    x[e] = np.where(x[e] < 0.74, 0.875, 0.9375)
    a = 1.0 - 0.1 * rng.random((N, 128, 8, 4))
    a[e] = 1.0
    u = d["u"].reshape(N, 128, 128, 4)
    u[:, :, ::16] = (2.0 ** 30 * a).astype(np.float32).astype(BF)
    w = np.zeros((N, 128, 4, 128, 4), np.float32)
    i = np.arange(128)
    for b in range(4): w[:, i, b, i, b] = -1
    x = (2.0 ** 30 * x * c.reshape(N, 1, 1, C, 1)).astype(np.float32).astype(BF)
    return {"x": x.reshape(N, 128, 4 * C), "u": u.reshape(N, 128, 512), "v": d["v"], **weights(rng, w.astype(BF))}
def setup_inputs_deep(rng):
    d = numbers_of(rng)
    x = d["x"].reshape(N, 8, 16, C, 4)
    u = d["u"].reshape(N, 128, 128, 4)
    k = rng.integers(-2, 3, (N, 8, 1, C, 1))
    s = rng.choice([-1.0, 1.0], (N, 8, 8, C, 4)) * (1.0 + (2 * rng.integers(0, 64, (N, 8, 8, C, 4)) + 1) * 2.0 ** -7) * np.exp2(k - rng.integers(8, 15, (N, 8, 8, C, 4)))
    s[:, :, 0, :, 0] = 1.96875 * np.exp2(k[:, :, 0, :, 0])
    x[:, :, 8:] = s.astype(np.float32).astype(BF)
    a = 1.0 + 0.125 * rng.integers(0, 8, (8, C))
    g = np.arange(8)[:, None]
    e = rng.permutation(N)
    for i, t in enumerate((np.exp2(g) * a, np.exp2(7 - g) * a, np.exp2(np.arange(C) % M * 8 // M) * a, -np.exp2(g) * a)):
        x[e[i], :, 0] = 0
        x[e[i], :, 0, :, 0] = t.astype(np.float32).astype(BF)
        u[e[i], :, ::16] = 0
        for h in range(0, 128, 16): u[e[i], h, h, 0] = 1
    return {"x": x.reshape(N, 128, 4 * C), "u": u.reshape(N, 128, 512), "v": d["v"], **layers(rng, [0])}
def setup_inputs_spread(rng):
    d = setup_inputs(rng)
    d["x"] = wide(rng, N, 128, 4 * C, cols=6)
    return d
def check_inputs(d):
    b = []
    for k in ("x", "u", "v"):
        a = np.abs(d[k].astype(np.float32))
        if not (np.isfinite(a).all() and ((a == 0) | (a >= 2.0 ** -30) & (a <= 2.0 ** 30)).all()): b.append("a value of " + k)
    none, least, most = [emit(mx_ref.quantize(np.full((128, 16), k, np.float32).astype(BF)))[1][0, 0] for k in (0.0, 2.0 ** -30, 2.0 ** 30)]
    for r in range(N):
        if ((d["wc"][r] == 0x7F) | (d["wc"][r] == 0xFF)).any(): b.append("wc: a code that is no number")
        s = mx_ref.live(d["ws"][r])
        if ((s != none) & ((s < least) | (s > most))).any(): b.append("ws: a scale out of range")
    return b
def parts(t):
    return t.reshape(8, 16, -1, 4).transpose(0, 2, 1, 3)
def laid(a):
    return np.ascontiguousarray(a.transpose(0, 2, 1, 3)).reshape(128, -1)
def voids(key):
    at, out = np.repeat(np.arange(8 * C).reshape(1, 8, P, M), N, axis=0), []
    for n in range(V):
        m = np.argmax(key, axis=3)[:, :, :, None]
        a, b = np.take_along_axis(key, m, axis=3), np.take_along_axis(at, m, axis=3)
        out.append(b[:, 0, :, 0])
        waste = np.repeat((8 * C + P * n + np.arange(P)).reshape(1, 1, P, 1), N, axis=0)
        np.put_along_axis(key, m, np.concatenate([a[:, 1:], np.full((N, 1, P, 1), -np.inf, np.float32)], axis=1), axis=3)
        np.put_along_axis(at, m, np.concatenate([b[:, 1:], waste], axis=1), axis=3)
    return at.reshape(N, 8, C), np.concatenate(out, axis=1)
def reference(x, u, v, wc, ws):
    qu = [mx_ref.quantize(u[r]) for r in range(N)]
    lay = [[pick(pk(wc[r], ws[r]), np.arange(128 * b, 128 * b + 128)) for b in range(4)] for r in range(N)]
    now = [x[r] for r in range(N)]
    for t in range(R):
        key = np.stack([mx_ref.matmul(qu[r], mx_ref.quantize(now[r]))[::16] for r in range(N)]) + np.float32(0.0)
        at, drawn = voids(key.reshape(N, 8, P, M))
        have = [parts(now[r]).reshape(8 * C, 16, 4) for r in range(N)]
        ore = [mx_ref.quantize(laid(have[r][drawn[r]].reshape(K, 8, 16, 4).transpose(1, 0, 2, 3))) for r in range(N)]
        new = []
        for r in range(N):
            q = mx_ref.quantize(decode(ore[(r - t - 1) % N]).astype(BF))
            h = tile([mx_ref.matmul(lay[r][b], q) * np.float32(0.03125) for b in range(4)])
            z = laid(np.concatenate([have[r], parts(h).transpose(1, 0, 2, 3).reshape(8 * K, 16, 4)])[at[r]])
            q = mx_ref.quantize(z)
            new.append(tile([mx_ref.matmul(lay[r][b], q) * np.float32(0.03125) + z[:, b::4].astype(np.float32) for b in range(4)]))
        now = new
    y, og = np.zeros((N, 128, C), np.float32), np.zeros((N, 8, C), np.float32)
    oc, osc = np.zeros((N, 128, 4 * C), np.uint8), np.zeros((N, 16, C), np.uint8)
    for r in range(N):
        q = mx_ref.quantize(now[r])
        y[r] = mx_ref.matmul(mx_ref.quantize(v[r]), q)
        og[r] = at[r]
        oc[r], osc[r] = emit(q)
    return {"y": y, "og": og, "oc": oc, "osc": osc}

@@ -1,0 +1,494 @@
+from concourse.bass import DstId, RemoteDMATransfer
+from concourse.mybir import dt, AluOpType, ActivationFunctionType
+
+A = AluOpType
+AF = ActivationFunctionType
+C, M, P, V, R = 448, 14, 32, 6, 3
+XE = 4 * C
+X0 = 3 * XE
+HB = 11 * XE
+BIG = float(2 ** 96)
+WHOLE = float(3 * 2 ** 22)
+SC = 0.03125
+RW, KW, OW = 72, 132, 68
+QUAD = [0, 2, 1, 3]
+CD, BF, F, U8, U16 = "float8_e4m3fn_x4", "bfloat16", "float32", "uint8", "uint16"
+
+SCRATCH = {"ps": ("psum", [128, 4096], F)}
+for _n, _s, _d in [
+        ("W", [HB + 256], BF), ("x3", [P, 4 * M], BF), ("xl", [16, 112], BF), ("xk", [56, 32], BF), ("x32", [56, 32], BF),
+        ("zz", [XE], BF), ("z32", [XE], BF), ("lt", [C], BF), ("us", [4, 128], BF), ("vs", [512], BF), ("zt", [512], BF),
+        ("one", [516], BF), ("gt", [516], BF), ("bt", [512], BF), ("bu", [128], BF), ("dtl", [640], BF),
+        ("qx", [C], CD), ("sx", [C], U8), ("qz", [C], CD), ("sz", [C], U8), ("qu", [128], CD), ("su", [128], U8),
+        ("qv", [128], CD), ("sv", [128], U8), ("qw", [528], CD), ("sw", [528], U8), ("qg", [512], CD), ("sg", [512], U8),
+        ("qb", [128], CD), ("sb", [256], U8), ("qn", [128], CD), ("qd", [160], CD), ("sd", [160], U8),
+        ("ql0", [160], CD), ("sl0", [256], U8), ("ql1", [160], CD), ("sl1", [256], U8), ("ql2", [160], CD), ("sl2", [256], U8),
+        ("kt", [C], F), ("ys", [C], F), ("rr", [7 * RW], F), ("kb", [7 * KW], F), ("ob", [8 * OW], F), ("oi", [32], F),
+        ("d0", [32], F), ("st", [32], F), ("ff", [64], F), ("nf", [128], F), ("blk", [352], F), ("col", [352], F),
+        ("pat", [48], F), ("sc", [4], F), ("tc", [256], F), ("bx", [64], F), ("tb", [72], F), ("t1", [32], F), ("t7", [32], F),
+        ("a2", [256], F), ("a3", [256], F), ("l2", [64], F), ("l3", [64], F),
+        ("g1", [32], F), ("g2", [32], F), ("g3", [32], F), ("g4", [32], F), ("g5", [32], F), ("g6", [32], F),
+        ("lk", [2], U16), ("lbx", [4], U16), ("lbs", [2], U16), ("la1", [16], U16), ("la2", [8], U16), ("ll1", [4], U16),
+        ("ll2", [2], U16), ("offb", [16], U16), ("offz", [128], U16), ("offl", [32], U16)]:
+    SCRATCH[_n] = ("sbuf", [128] + _s, _d)
+SEMAPHORES = ["v", "s", "t", "g", "lx", "lu", "lw", "lv", "w1", "w2", "sent", "arr0", "arr1", "arr2", "out"]
+
+
+def rank_program(g, core, T, topo):
+    rank = T.rank_of(core)
+    if rank is None:
+        return
+    N = len(T.cores)
+    S = T.sem
+    eng = {"v": g.vector, "s": g.scalar, "t": g.tensor, "g": g, "y": g.sync}
+    count = {}
+    known = {e: {} for e in eng}
+    clock = {}
+    wr, rd = {}, {}
+
+    def wait(e, tok):
+        if known[e].get(tok[0], 0) >= tok[1]:
+            return
+        eng[e].wait_ge(S[tok[0]], tok[1])
+        for k, c in clock.get(tok, {}).items():
+            if known[e].get(k, 0) < c:
+                known[e][k] = c
+        known[e][tok[0]] = tok[1]
+
+    def order(e, reads, writes):
+        need = {}
+        for k in list(reads) + list(writes):
+            toks = [wr[k]] if k in wr else []
+            if k in writes:
+                toks = toks + rd.get(k, [])
+            elif k.startswith("ps"):
+                toks = toks + [t for t in rd.get(k, []) if t[0] != e]
+            for t in toks:
+                need[t[0]] = max(need.get(t[0], 0), t[1])
+        for k in sorted(need, key=lambda k: k != e):
+            wait(e, (k, need[k]))
+
+    def note(e, tok, reads, writes):
+        clock[tok] = dict(known[e])
+        for k in reads:
+            rd.setdefault(k, []).append(tok)
+        for k in writes:
+            wr[k] = tok
+            rd[k] = []
+
+    def do(e, reads, writes, call):
+        order(e, reads, writes)
+        count[e] = count.get(e, 0) + 1
+        call().then_inc(S[e], 1)
+        note(e, (e, count[e]), reads, writes)
+
+    def dmas(sem, items):
+        tok = (sem, count.get(sem, 0) + 16 * len(items))
+        count[sem] = tok[1]
+        seen = {}
+        for e, reads, writes, out, in_ in items:
+            order(e, reads, writes)
+            eng[e].dma_start(out, in_).then_inc(S[sem], 16)
+            for k, c in known[e].items():
+                seen[k] = max(seen.get(k, 0), c)
+        for e, reads, writes, out, in_ in items:
+            note(e, tok, reads, writes)
+        clock[tok] = seen
+
+    vec, act, pe = g.vector, g.scalar, g.tensor
+    W, ps = T.W, T.ps
+    u8 = dt.uint8
+
+    def bank(b, n):
+        return ps[:, 512 * b:512 * b + n]
+
+    def iota(out, pattern, base, cm, key):
+        do("g", [], [key], lambda: g.iota(out, pattern, base, cm, allow_small_or_imprecise_dtypes=True))
+
+    def copy(e, out, in_, reads, writes, scale=None):
+        if e == "s":
+            if scale is None:
+                do(e, reads, writes, lambda: act.activation(out, in_, AF.Copy))
+            else:
+                do(e, reads, writes, lambda: act.activation(out, in_, AF.Identity, scale=scale))
+        elif scale is None:
+            do(e, reads, writes, lambda: vec.tensor_copy(out, in_))
+        else:
+            do(e, reads, writes, lambda: vec.tensor_scalar(out, in_, scale, None, A.mult))
+
+    def ts(out, in0, s1, s2, op0, op1, reads, writes):
+        if s2 is None:
+            do("v", reads, writes, lambda: vec.tensor_scalar(out, in0, s1, None, op0))
+        else:
+            do("v", reads, writes, lambda: vec.tensor_scalar(out, in0, s1, s2, op0, op1))
+
+    def tt(out, in0, in1, op, reads, writes):
+        do("v", reads, writes, lambda: vec.tensor_tensor(out, in0, in1, op))
+
+    def tr(out, in_, reads, writes):
+        do("v", reads, writes, lambda: vec.transpose(out, in_))
+
+    def scan(out, d0, d1, init, op0, op1, reads, writes):
+        do("v", reads, writes, lambda: vec.tensor_tensor_scan(out, d0, d1, init, op0, op1))
+
+    def quant(q, s, in_, reads, writes):
+        do("v", reads, writes, lambda: vec.quantize_mx(q, s, in_))
+
+    def fill(ap, val, key):
+        do("v", [], [key], lambda: vec.memset(ap, val))
+
+    def mm(b, n, pairs, reads):
+        order("t", reads, ["ps%d" % b])
+        for i, (lq, ls, rq, rs) in enumerate(pairs):
+            ins = pe.matmul_mx(bank(b, n), lq, ls, rq, rs, i == 0, i == len(pairs) - 1)
+        count["t"] = count.get("t", 0) + 1
+        ins.then_inc(S.t, 1)
+        note("t", ("t", count["t"]), reads, ["ps%d" % b])
+
+    X32 = [["x32%d%d" % (hf, b) for b in range(4)] for hf in range(2)]
+    XW = X32[0] + X32[1]
+    XK = ["xk%d" % a for a in range(4)]
+    WZ = ["w%d" % d for d in (1, 2, 3, 4, 5, 6)] + ["c4%d" % a for a in range(4)]
+    WB = WZ[0:5] + WZ[6:] + ["w-1", "w-2", "w-3"] + ["c2%d" % a for a in range(4)]
+    spare = []
+
+    def piece():
+        if spare:
+            d, a = spare.pop(0)
+            lo, hi = (0, 64) if d > 0 else (32, 64)
+            s0 = X0 + C * a
+            copy("s", W[lo:hi, s0 + d * XE:s0 + d * XE + C], W[lo + 16 * d:hi + 16 * d, s0:s0 + C], X32[a // 2], ["c%d%d" % (abs(d), a)])
+
+    def windows(first):
+        def shift(d):
+            lo, hi = (0, 128 - 16 * d) if d >= 0 else (-16 * d, 64)
+            s0, n = X0 + d * XE, C if d == 7 and not first else XE
+            if first:
+                return ("y", [], ["w%d" % d] if d else XW, W[lo:hi, s0:s0 + n], T.x[lo + 16 * d:hi + 16 * d, :])
+            return ("y", XW, ["w%d" % d], W[lo:hi, s0:s0 + n], W[lo + 16 * d:hi + 16 * d, X0:X0 + n])
+        dmas("w1", [shift(d) for d in ((0, 1, 2, 3, -1, 4, -2, 5, -3) if first else (1, 2, 3, -1, 5, -3))])
+        dmas("w2", [shift(d) for d in (6, 7)])
+
+    dmas("lx", [("y", [], ["x3"], T.x3[:], T.x[:])])
+    dmas("lu", [("y", [], ["us%d" % k], T.us[:, k:k + 3:2, :], T.u[:, 256 * k:256 * k + 256]) for k in range(2)])
+    windows(True)
+    dmas("lw", [("y", [], ["qw"], T.qw[:, 16:528].bitcast(u8), T.wc[:]),
+                ("y", [], ["sw"], T.sw[:, 16:528], T.ws[:]),
+                ("y", [], ["qw0"], T.qw[:, 0:16].bitcast(u8), T.wc[:, 0:64]),
+                ("y", [], ["sw0"], T.sw[:, 0:16], T.ws[:, 0:16])])
+    dmas("lv", [("y", [], ["vs"], T.vs[:], T.v[:])])
+    WK = ["qw", "sw", "qw0", "sw0"]
+
+    def blk(k, a=0, b=32):
+        return T.blk[:, 32 * k + a:32 * k + b]
+    w0 = 9 * XE + 128
+    o7 = slice(7 * OW + 2, 7 * OW + 66, 2)
+    iota(blk(0), [[32, 4], [2 * XE, 4], [-128, 2]], w0, 0, "blk0")
+    iota(blk(1), [[0, 2], [RW, 4], [0, 4]], 0, 0, "blk1")
+    iota(blk(2, 0, 16), [[64, 2], [128, 4], [512, 2]], 0, 1, "blk2")
+    iota(blk(2, 16, 32), [[64, 2], [128, 4], [512, 2]], 16, 1, "blk2b")
+    iota(blk(3), [[16, 2], [0, 16]], 0, 1, "blk3")
+    iota(T.pat[:, 0:6], [[4, 6]], 0, 0, "pat0")
+    iota(T.pat[:, 6:10], [[4 * RW, 2], [0, 2]], RW + 46, 0, "pat1")
+    iota(T.ob[:, o7], [[XE, 2], [4, 16]], -4, 4 * M, "o7")
+    iota(T.oi[:], [[XE, 2], [32, 16]], -32, 0, "oi")
+    iota(T.tc[:], [[0, 64], [1, 4]], 0, 0, "tc")
+    iota(blk(4), [[8, 4], [C, 4], [4, 2]], 0, 4 * M, "blk4")
+    iota(blk(5), [[16, 2], [1, 8], [32, 2]], 1, 0, "blk5")
+    iota(blk(6, 0, 16), [[128, 2], [16, 2], [0, 4]], 0, 1, "blk6")
+    iota(blk(6, 16, 32), [[128, 2], [16, 2], [0, 4]], 0, 1, "blk6b")
+    iota(blk(7), [[16, 2], [1, 8], [32, 2]], 1, 0, "blk7")
+    iota(blk(8), [[8 - 256, 4], [2 - 16 * XE, 4], [1 + 1024, 2]], 8 * C - 8 * w0, 0, "blk8")
+    iota(blk(9, 0, 16), [[8, 2], [1, 2], [0, 4]], 0, 0, "blk9")
+    iota(blk(9, 16, 32), [[8, 2], [1, 2], [0, 4]], 0, 0, "blk9b")
+    iota(blk(10), [[8 * C - 8, 4], [C, 4], [C - 4, 2]], 0, 0, "blk10")
+    iota(T.pat[:, 10:26], [[2, 4], [16, 2], [0, 2]], 0, 0, "pat2")
+    iota(T.pat[:, 26:34], [[64, 4], [8, 2]], 0, 0, "pat3")
+    iota(T.pat[:, 34:38], [[256, 2], [0, 2]], 0, 0, "pat4")
+
+    fill(T.zt[:], 0.0, "zt")
+    fill(T.one[:], 1.0, "one")
+    fill(T.rr[:, 0:32], -BIG, "rt0")
+    fill(T.rr[96:128, 64:7 * RW:RW], -BIG, "rwi")
+    fill(T.d0[:], BIG, "d0")
+    fill(T.kb[:, 0:66], -BIG, "kb0")
+    fill(T.ff[:], 0.0, "ffi")
+    fill(T.nf[:], 0.0, "nfi")
+    fill(T.lk[:, 0:1], 30, "lk0")
+    fill(T.lk[:, 1:2], 64, "lk1")
+    fill(T.lbs[64:128, 0:1], 64, "lbs2")
+    fill(T.d0[:, 0:32:16], -BIG, "d0")
+    fill(T.nf[:, 1:128:64], 1.0, "nfi")
+    do("g", ["one"], ["gt"], lambda: g.affine_select(T.gt[:], T.one[:], [[1, 516]], A.is_equal, 0.0, -3, -4))
+    copy("s", T.bt[:, 128:512], T.zt[:, 0:384], ["zt"], ["btz"])
+    copy("s", T.dtl[:, 0:128], T.zt[:, 0:128], ["zt"], ["dz0"])
+    copy("s", T.dtl[:, 256:640], T.zt[:, 0:384], ["zt"], ["dz1"])
+    wr["r0"] = wr["rt0"]
+    wr["f0"] = wr["f1"] = wr["ffi"]
+    wr["n0"] = wr["n1"] = wr["nfi"]
+    wr["k0a"] = wr["k0b"] = wr["kb0"]
+    quant(T.qn[:], T.sb[:, 0:128], T.zt[:], ["zt"], ["qb"])
+    for t in range(R):
+        quant(T["ql%d" % t][:, 32:160], T["sl%d" % t][:, 128:256], T.zt[:], ["zt"], ["pad%d" % t])
+
+    def colv(k):
+        return T.col[:, 32 * k:32 * k + 1]
+
+    tr(T.col[:, 0:128], T.blk[:, 0:128], ["blk0", "blk1", "blk2", "blk2b", "blk3"], ["cola"])
+    ts(T.rr[96:128, RW + 65:7 * RW:RW], T.pat[96:128, 0:6], T.col[96:128, 0:1], None, A.add, None, ["pat0", "cola"], ["rwj"])
+    ts(T.lbx[:], T.pat[:, 6:10], colv(1), float(6 * RW + 46), A.add, A.min, ["pat1", "cola"], ["lbx"])
+    ts(T.lbs[0:64, 0:1], T.col[0:64, 64:65], 0.0625, None, A.mult, None, ["cola"], ["lbs"])
+    ts(T.sc[:, 0:1], colv(3), -112.0, None, A.mult, None, ["cola"], ["sc0"])
+    ts(T.sc[:, 1:2], colv(3), -112.0, float(X0), A.mult, A.add, ["cola"], ["sc1"])
+    ts(T.tb[:, 64:65], colv(3), 112.0, None, A.mult, None, ["cola"], ["tb64"])
+    for q0 in (32, 96):
+        ts(T.ob[q0:q0 + 32, o7], T.ob[q0:q0 + 32, o7], float(3 * XE), None, A.add, None, ["o7"], ["o7"])
+        ts(T.oi[q0:q0 + 32, :], T.oi[q0:q0 + 32, :], float(3 * XE), None, A.add, None, ["oi"], ["oi"])
+
+    def keys_half(hf, reads):
+        c0 = 224 * hf
+        quant(T.qx[:, c0:c0 + 224], T.sx[:, c0:c0 + 224], T.xk[:, 28 * hf:28 * hf + 28, :], reads, ["qx%d" % hf])
+        if "qu" not in wr:
+            quant(T.qu[:], T.su[:], T.us[:], ["us0", "us1"], ["qu"])
+        mm(hf, 224, [(T.qu[:], T.su[:], T.qx[:, c0:c0 + 224], T.sx[:, c0:c0 + 224])], ["qu", "qx%d" % hf])
+
+    XJ = ["xj%d" % j for j in range(M)]
+
+    def lay(e, j):
+        copy(e, T.xk[:, 4 * j:4 * j + 4, :], T.x3[:, :, 4 * j:4 * j + 4], ["x3"], [XJ[j]])
+    for j in (5, 6, 10, 11, 12, 13):
+        lay("s", j)
+    for j in range(5):
+        lay("v", j)
+    keys_half(0, XJ[0:7])
+    for j in range(7, 10):
+        lay("v", j)
+    keys_half(1, XJ[7:14])
+    for k in XK:
+        wr[k] = wr["qx1"]
+
+    for t in range(R):
+        last = t == R - 1
+        down = None if t == 0 else SC
+        for hf in range(2):
+            tr(T.kt[:, 224 * hf:224 * hf + 224], bank(hf, 224), ["ps%d" % hf], ["kt%d" % hf])
+        KT = ["kt0", "kt1"]
+        oreg = [7 if t == 0 else 0] + list(range(1, V + 1))
+
+        def origins(n):
+            a, b, pp = OW * oreg[n - 1], OW * oreg[n], (n - 1) % 2
+            scan(T.ob[:, b + 1:b + 65], T.nf[:, 64 * pp:64 * pp + 64], T.ob[:, a + 2:a + 66], 0.0, A.mult, A.add,
+                 ["o%d" % oreg[n - 1], "bo%d" % oreg[n - 1], "bp%d" % oreg[n - 1], "n%d" % pp], ["o%d" % n, "bo%d" % n, "bp%d" % n])
+
+        for n in range(V + 1):
+            r0, k0, k1, o0, pr = RW * n, KW * n, KW * (n + 1), OW * oreg[n], n % 2
+            rn, ro, fn, nn, on = "r%d" % n, "rt%d" % n, "f%d" % pr, "n%d" % pr, "o%d" % oreg[n]
+            kn = ["k0a", "k0b"] if n == 0 else ["k%d" % n]
+            RN = [rn, ro]
+            if n == 0:
+                for h in range(2):
+                    scan(T.rr[:, 16 * h + 1:16 * h + 15], T.d0[:, 1:15], T.kt[:, 16 * h:C:32], -BIG, A.min, A.max, KT + ["d0"], [RN[h]])
+                src, dst = slice(14, 15), slice(64, 65)
+            else:
+                if n < V:
+                    scan(T.rr[:, r0:r0 + 32], T.d0[:], T.kb[:, k0 + 2:k0 + 66:2], -BIG, A.min, A.max, kn + ["d0"], [rn])
+                    src, dst = slice(r0 + 14, r0 + 47, 32), slice(r0 + 64, r0 + 66)
+                else:
+                    src, dst = slice(r0 + 46, r0 + 47), slice(r0 + 65, r0 + 66)
+                scan(T.rr[:, r0 + 32:r0 + 64], T.d0[:], T.kb[:, k0 + 66:k0 + 130:2], -BIG, A.min, A.max, ["t%d" % n, "d0"], [ro])
+            copy("s", T.rr[0:64, dst], T.rr[64:128, src], RN, ["rs%d" % n])
+            copy("s", T.rr[64:96, dst], T.rr[32:64, src], RN, ["ru%d" % n])
+            SH = RN + ["rs%d" % n, "ru%d" % n, "rwi", "rwj"]
+            if n == 0:
+                for h in range(2):
+                    copy("s", T.kb[:, 4 + 32 * h:32 + 32 * h:2], T.kt[:, 16 * h:C:32], KT, [kn[h]])
+            else:
+                pp, a = 1 - pr, OW * oreg[n - 1]
+                copy("s", T.ob[:, a + 3:a + 35:2], T.ff[:, 32 * pp:32 * pp + 16], RN + ["f%d" % pp], ["bo%d" % oreg[n - 1]],
+                     T.rr[:, r0 + 62:r0 + 63])
+                copy("s", T.ob[:, a + 35:a + 67:2], T.ff[:, 32 * pp + 16:32 * pp + 32], SH + ["f%d" % pp], ["bp%d" % oreg[n - 1]],
+                     T.rr[:, r0 + 65:r0 + 66])
+            if n == V:
+                break
+            piece()
+            for h in range(2):
+                c0 = r0 + 16 * h
+                ts(T.st[:, 16 * h:16 * h + 16], T.rr[:, c0:c0 + 16], T.rr[:, c0 + 14:c0 + 15], None, A.is_ge, None,
+                   [RN[h] if n == 0 else rn], ["st%d" % h])
+            tt(T.ff[:, 32 * pr + 1:32 * pr + 32], T.st[:, 1:32], T.st[:, 0:31], A.is_gt, ["st0", "st1"], [fn])
+            tt(T.nf[:, 64 * pr + 3:64 * pr + 64:2], T.st[:, 1:32], T.st[:, 0:31], A.is_le, ["st0", "st1"], [nn])
+            if n < V - 1:
+                tt(T.kb[:, k0 + 3:k0 + 67:2], T.rr[:, r0:r0 + 65].indirect(T.lk[:]), T.ff[:, 32 * pr:32 * pr + 32], A.mult,
+                   SH + ["lk0", "lk1", fn], ["bk%d" % n])
+            if n > 0:
+                origins(n)
+            if n < V - 1:
+                scan(T.kb[:, k1 + 1:k1 + 65], T.nf[:, 64 * pr:64 * pr + 64], T.kb[:, k0 + 2:k0 + 66], 0.0, A.mult, A.add,
+                     kn + ["bk%d" % n, nn], ["k%d" % (n + 1), "bk%d" % (n + 1)])
+            tt(T.kb[:, k1 + 66:k1 + 130:2], T.ob[:, o0 + 2:o0 + 66:2], T.ff[:, 32 * pr:32 * pr + 32], A.mult, [on, fn], ["t%d" % (n + 1)])
+        tt(T.bx[:], T.rr[:, 0:RW * V + 64].indirect(T.lbx[:]), T.tc[:, 0:64], A.add,
+           [k % m for m in range(V) for k in ("r%d", "rt%d", "rs%d", "ru%d")] + ["rt6", "rwi", "rwj", "lbx", "tc"], ["bx"])
+        tr(T.tb[0:32, 0:64], T.bx[0:32, :], ["bx"], ["tba"])
+        tr(T.tb[32:64, 0:64], T.bx[0:32, :], ["bx"], ["tbb"])
+        ts(T.offb[:], T.tb[:, 0:65].indirect(T.lbs[:, 0:1]), T.sc[:, 1:2], None, A.add, None,
+           ["tba", "tbb", "tb64", "lbs", "lbs2", "sc1"], ["offb"])
+        origins(V)
+        wb = W[:, 0:9 * XE]
+        copy("s", T.bu[:], wb.indirect(T.offb[:, 8:16]), XW + WB + ["offb"], ["bu"], down)
+        copy("v", T.bt[:, 0:128], wb.indirect(T.offb[:, 0:8]), XW + WB + ["offb"], ["bt"], down)
+        copy("v", T.bt[64:128, 0:128], T.bu[0:64, :], ["bu"], ["bt"])
+        quant(T.qb[:], T.sb[:, 128:256], T.bt[:], ["bt", "btz"], ["qb"])
+        peer = T.cores[(rank + t + 1) % N]
+        rid, pid = topo.addr(peer)[0:2]
+        es = topo.engines(core, peer)
+        half = len(es) // 2
+        masks = [sum(1 << k for k in es[:half]), sum(1 << k for k in es[half:])]
+        ql, sl, arr = T["ql%d" % t], T["sl%d" % t], "arr%d" % t
+        order("g", ["qb"], [])
+        g.remote_dma_fused([
+            RemoteDMATransfer(dst_ids=[DstId(rid=rid, pnc=pid)], dma_engine_mask=masks[0], remote_sem=S[arr],
+                              src=T.qb[:, 0:32].bitcast(u8), dst=ql[:, 0:32].bitcast(u8)),
+            RemoteDMATransfer(dst_ids=[DstId(rid=rid, pnc=pid)], dma_engine_mask=masks[1], remote_sem=S[arr],
+                              src=T.sb[:, 32:160], dst=sl[:, 0:128])], local_sem=S.sent)
+        count["sent"] = count.get("sent", 0) + 2 * half
+        note("g", ("sent", count["sent"]), ["qb"], [])
+        count[arr] = 2 * (len(topo.engines(T.cores[(rank - t - 1) % N], core)) // 2)
+        wr["land%d" % t] = (arr, count[arr])
+
+        if t == 0:
+            ts(T.blk[96:128, 176:192], T.blk[96:128, 176:192], -16.0, None, A.add, None, ["blk5"], ["blk5"])
+        of = slice(OW * V + 2, OW * V + 66, 2)
+        o6 = T.ob[:, of]
+        for a in range(4):
+            tr(T.t1[32 * a:32 * a + 32, :], T.ob[32 * QUAD[a]:32 * QUAD[a] + 32, of], ["o6"], ["t1%d" % a])
+            if t == 0 and a == 0:
+                tr(T.col[:, 128:352], T.blk[:, 128:352],
+                   ["blk4", "blk5", "blk6", "blk6b", "blk7", "blk8", "blk9", "blk9b", "blk10"], ["colb"])
+        if t == 0:
+            ts(T.la1[:], T.pat[:, 10:26], colv(9), None, A.add, None, ["pat2", "colb"], ["la1"])
+            ts(T.la2[:], T.pat[:, 26:34], colv(5), 255.0, A.add, A.min, ["pat3", "colb"], ["la2"])
+        tt(T.a2[:], T.t1[:].indirect(T.la1[:]), T.tc[:], A.add, ["t1%d" % a for a in range(4)] + ["la1", "tc"], ["a2"])
+        tr(T.t7[0:32, :], T.ob[96:128, of], ["o6"], ["t70"])
+        tr(T.a3[:], T.a2[:], ["a2"], ["a3"])
+        tr(T.t7[32:64, :], T.ob[96:128, of], ["o6"], ["t71"])
+        ts(T.offz[:], T.a3[:].indirect(T.la2[:]), T.sc[:, 0:1], None, A.add, None, ["a3", "la2", "sc0"], ["offz"])
+        wz = W[:, X0:X0 + 7 * XE]
+        ZA = ["z%d" % a for a in range(4)]
+
+        def early(e, c0, c1, key):
+            z0 = C * (c0 // 32) + 16 * (c0 % 32)
+            copy(e, T.zz[:, z0:z0 + 16 * (c1 - c0)], wz.indirect(T.offz[:, c0:c1]), XW + WZ + ["offz"], key, down)
+        for a in range(3):
+            early("s", 32 * a, 32 * a + 28, [ZA[a]])
+        tr(T.t7[64:96, :], T.ob[96:128, of], ["o6"], ["t72"])
+        tr(T.t7[96:128, :], T.ob[96:128, of], ["o6"], ["t73"])
+        if t == 0:
+            ts(T.ll1[:], T.pat[:, 34:38], colv(6), 0.0625, A.add, A.mult, ["pat4", "colb"], ["ll1"])
+            ts(T.ll2[:], T.pat[:, 26:28], colv(7), 63.0, A.add, A.min, ["pat3", "colb"], ["ll2"])
+            for b in range(4):
+                quant(T.qg[:, 128 * b:128 * b + 128], T.sg[:, 128 * b:128 * b + 128], T.gt[:, 3 - b:515 - b], ["gt"], ["qg%d" % b])
+        tt(T.l2[:], T.t7[:].indirect(T.ll1[:]), T.tc[:, 0:64], A.add, ["t7%d" % a for a in range(4)] + ["ll1", "tc"], ["l2"])
+        if t > 0:
+            early("v", 96, 110, [ZA[3]])
+        else:
+            ts(T.ob[:, 2:66:2], T.oi[:], colv(4), None, A.add, None, ["oi", "colb"], ["o0"])
+        tr(T.l3[:], T.l2[:], ["l2"], ["l3"])
+        if t == 1:
+            quant(T.qv[:], T.sv[:], T.vs[:], ["vs"], ["qv"])
+            ts(T.sc[:, 2:3], colv(10), XE // 2 - 0.5, SC, A.add, A.mult, ["colb"], ["sc2"])
+        if last:
+            ts(T.g1[:], o6, float(8 * XE - 1), 0.5 - XE // 2, A.min, A.add, ["o6"], ["g1"])
+
+        for b in range(4):
+            mm(4 + b, 128, [(T.qg[:, 128 * b:128 * b + 128], T.sg[:, 128 * b:128 * b + 128], ql[:, 0:128], sl[:, 96:224])],
+               ["qg%d" % b, "land%d" % t, "pad%d" % t])
+        for b in range(4):
+            copy("v", T.dtl[:, 128 + b:256:4], bank(4 + b, 32), ["ps%d" % (4 + b)], ["d%d_" % b])
+        quant(T.qd[:], T.sd[:], T.dtl[:], ["d%d_" % b for b in range(4)] + ["dz0", "dz1"], ["qd"])
+        for b in range(4):
+            lo, hi = 16 + 128 * b, 128 * b
+            mm(b, 128, [(T.qw[:, lo:lo + 128], T.sw[:, lo:lo + 128], T.qd[:, 32:160], T.sd[:, 32:160]),
+                        (T.qw[:, hi:hi + 128], T.sw[:, hi:hi + 128], T.qd[:, 0:128], T.sd[:, 0:128])], WK + ["qd"])
+        ts(T.offl[:], T.l3[:].indirect(T.ll2[:]), T.sc[:, 0:1], None, A.add, None, ["l3", "ll2", "sc0"], ["offl"])
+        if t == 0:
+            early("v", 96, 124, [ZA[3]])
+        else:
+            early("v", 110, 124, ["z3b"])
+        for b in range(4):
+            copy("v", W[:, HB + b:HB + 256:4], bank(b, 64), ["ps%d" % b], ["h%d" % b], SC if t == 0 else None)
+        wl = W[:, X0:HB + 256]
+        LR = XW + WZ + ["w7", "offl"] + ["h%d" % b for b in range(4)]
+        copy("s", T.lt[:, 224:448], wl.indirect(T.offl[:, 14:28]), LR, ["lt1"], down)
+        copy("v", T.lt[:, 0:224], wl.indirect(T.offl[:, 0:14]), LR, ["lt0"], down)
+
+        def place(e, a):
+            copy(e, T.zz[96:128, C * a:C * a + C], T.lt[32 * a:32 * a + 32, :], ["lt0", "lt1"], [ZA[a]] + (["z3b"] if a == 3 else []))
+
+        def layer(hf):
+            c0 = 224 * hf
+            quant(T.qz[:, c0:c0 + 224], T.sz[:, c0:c0 + 224], T.zz[:, 896 * hf:896 * hf + 896], ZA[2 * hf:2 * hf + 2], ["qz%d" % hf])
+            for b in range(4):
+                lo = 16 + 128 * b
+                mm(4 * hf + b, 224, [(T.qw[:, lo:lo + 128], T.sw[:, lo:lo + 128], T.qz[:, c0:c0 + 224], T.sz[:, c0:c0 + 224])],
+                   WK + ["qz%d" % hf])
+        place("s", 3)
+        place("v", 0)
+        place("v", 1)
+        layer(0)
+        place("v", 2)
+        layer(1)
+        for hf in range(2):
+            for b in range(4):
+                z0 = 896 * hf + 224 * b
+                copy("s", T.z32[:, z0:z0 + 224], T.zz[:, 896 * hf + b:896 * hf + 896:4], ZA[2 * hf:2 * hf + 2], ["z32%d%d" % (hf, b)], 32.0)
+        if last:
+            do("s", ["g1", "sc2"], ["g4"], lambda: act.activation(T.g4[:], T.g1[:], AF.Identity, bias=T.sc[:, 2:3], scale=SC))
+            do("s", ["o6", "colb"], ["g5"], lambda: act.activation(T.g5[:], o6, AF.Identity, bias=colv(8), scale=8.0))
+        for hf in range(2):
+            for b in range(4):
+                z0 = 896 * hf + 224 * b
+                out = T.x32[:, 28 * hf:28 * hf + 28, b:32:4] if last else W[:, X0 + 896 * hf + b:X0 + 896 * hf + 896:4]
+                tt(out, bank(4 * hf + b, 224), T.z32[:, z0:z0 + 224], A.add, ["ps%d" % (4 * hf + b), "z32%d%d" % (hf, b)], [X32[hf][b]])
+        if not last:
+            windows(False)
+            for a in range(4):
+                copy("s" if a < 2 else "v", T.xk[:, :, 8 * a:8 * a + 8], W[:, X0 + C * a:X0 + C * a + C], X32[a // 2], [XK[a]], SC)
+            spare.extend((d, a) for a in range(4) for d in (4, -2))
+            for k in range(3):
+                piece()
+            keys_half(0, XK)
+            keys_half(1, XK)
+
+    def unlay(hf, q, e):
+        copy("v" if hf else "s", T.xl[:, 4 * q + 2 * hf:4 * q + 2 * hf + 2, 56 * e:56 * e + 56],
+             T.x32[:, 28 * hf:28 * hf + 28, 8 * q + 4 * e:8 * q + 4 * e + 4], X32[hf], ["xl%d%d%d" % (hf, q, e)], SC)
+    for q in range(4):
+        for e in range(2):
+            unlay(0, q, e)
+    ts(T.g2[:], T.g1[:], 1.0 / XE, WHOLE, A.mult, A.add, ["g1"], ["g2"])
+    for k in range(2):
+        c0 = 224 * k
+        for q in (2 * k, 2 * k + 1):
+            for e in range(2):
+                unlay(1, q, e)
+        quant(T.qx[:, c0:c0 + 224], T.sx[:, c0:c0 + 224], T.xl[:, 8 * k:8 * k + 8, :],
+              ["xl%d%d%d" % (hf, q, e) for hf in range(2) for q in (2 * k, 2 * k + 1) for e in range(2)], ["qx%d" % k])
+        mm(k, 224, [(T.qv[:], T.sv[:], T.qx[:, c0:c0 + 224], T.sx[:, c0:c0 + 224])], ["qv", "qx%d" % k])
+        if k == 0:
+            ts(T.g3[:], T.g2[:], -WHOLE, float(C - 56), A.add, A.mult, ["g2"], ["g3"])
+    tt(T.g2[:], T.g3[:], T.g4[:], A.add, ["g3", "g4"], ["g2"])
+    tt(T.g6[:], T.g2[:], T.g5[:], A.max, ["g2", "g5"], ["g6"])
+    QX = ["qx0", "qx1"]
+    copy("s", T.ys[:, 0:224], bank(0, 224), ["ps0"], ["ys0"])
+    copy("v", T.ys[:, 224:448], bank(1, 224), ["ps1"], ["ys1"])
+
+    def og(e, a, h):
+        return (e, ["g6"], [], T.og[2 * a + h:2 * a + h + 1, :], T.g6[32 * QUAD[a]:32 * QUAD[a] + 32, 16 * h + 1:16 * h + 15])
+    dmas("out", [("y", ["qx0"], [], T.oc[:, 0:896], T.qx[:, 0:224].bitcast(u8)),
+                 ("y", ["qx1"], [], T.oc[:, 896:XE], T.qx[:, 224:C].bitcast(u8)),
+                 ("s", ["ys0"], [], T.y[:, 0:224], T.ys[:, 0:224])]
+         + [("y", QX, [], T.osc[4 * k:4 * k + 4, :], T.sx[32 * k:32 * k + 4, :]) for k in range(4)]
+         + [og("s", a, h) for a in range(3) for h in range(2)]
+         + [("y", ["ys1"], [], T.y[:, 224:C], T.ys[:, 224:C]), og("y", 3, 0), og("y", 3, 1)])
+    for k in count:
+        wait("y", (k, count[k]))

@@ -10,7 +10,7 @@ HB = 11 * XE
 BIG = float(2 ** 96)
 WHOLE = float(3 * 2 ** 22)
 SC = 0.03125
-RW, KW, OW = 72, 132, 68
+L = 96
 QUAD = [0, 2, 1, 3]
 CD, BF, F, U8, U16 = "float8_e4m3fn_x4", "bfloat16", "float32", "uint8", "uint16"
 
@@ -23,12 +23,14 @@ for _n, _s, _d in [
         ("qv", [128], CD), ("sv", [128], U8), ("qw", [528], CD), ("sw", [528], U8), ("qg", [512], CD), ("sg", [512], U8),
         ("qb", [128], CD), ("sb", [256], U8), ("qn", [128], CD), ("qd", [160], CD), ("sd", [160], U8),
         ("ql0", [160], CD), ("sl0", [256], U8), ("ql1", [160], CD), ("sl1", [256], U8), ("ql2", [160], CD), ("sl2", [256], U8),
-        ("kt", [C], F), ("ys", [C], F), ("rr", [7 * RW], F), ("kb", [7 * KW], F), ("ob", [8 * OW], F), ("oi", [32], F),
-        ("d0", [32], F), ("st", [32], F), ("ff", [64], F), ("nf", [128], F), ("blk", [352], F), ("col", [352], F),
+        ("kt", [C], F), ("ys", [C], F), ("rb", [2 * L], F), ("kb", [2 * L], F), ("sq", [2 * L], F), ("yy", [66], F),
+        ("dk", [200], F), ("dl", [200], F), ("dr", [L], F), ("df", [L], F), ("ff", [33], F), ("gg", [64], F), ("uu", [32], F),
+        ("tn", [8 * L], F), ("lb", [V * L], F), ("of", [L + 1], F), ("oa", [33], F), ("oi", [33], F), ("wt", [V], F),
+        ("blk", [352], F), ("col", [352], F),
         ("pat", [48], F), ("sc", [4], F), ("tc", [256], F), ("bx", [64], F), ("tb", [72], F), ("t1", [32], F), ("t7", [32], F),
         ("a2", [256], F), ("a3", [256], F), ("l2", [64], F), ("l3", [64], F),
         ("g1", [32], F), ("g2", [32], F), ("g3", [32], F), ("g4", [32], F), ("g5", [32], F), ("g6", [32], F),
-        ("lk", [2], U16), ("lbx", [4], U16), ("lbs", [2], U16), ("la1", [16], U16), ("la2", [8], U16), ("ll1", [4], U16),
+        ("lbx", [4], U16), ("lbs", [2], U16), ("la1", [16], U16), ("la2", [8], U16), ("ll1", [4], U16),
         ("ll2", [2], U16), ("offb", [16], U16), ("offz", [128], U16), ("offl", [32], U16)]:
     SCRATCH[_n] = ("sbuf", [128] + _s, _d)
 SEMAPHORES = ["v", "s", "t", "g", "lx", "lu", "lw", "lv", "w1", "w2", "sent", "arr0", "arr1", "arr2", "out"]
@@ -148,16 +150,8 @@ def rank_program(g, core, T, topo):
     X32 = [["x32%d%d" % (hf, b) for b in range(4)] for hf in range(2)]
     XW = X32[0] + X32[1]
     XK = ["xk%d" % a for a in range(4)]
-    WZ = ["w%d" % d for d in (1, 2, 3, 4, 5, 6)] + ["c4%d" % a for a in range(4)]
-    WB = WZ[0:5] + WZ[6:] + ["w-1", "w-2", "w-3"] + ["c2%d" % a for a in range(4)]
-    spare = []
-
-    def piece():
-        if spare:
-            d, a = spare.pop(0)
-            lo, hi = (0, 64) if d > 0 else (32, 64)
-            s0 = X0 + C * a
-            copy("s", W[lo:hi, s0 + d * XE:s0 + d * XE + C], W[lo + 16 * d:hi + 16 * d, s0:s0 + C], X32[a // 2], ["c%d%d" % (abs(d), a)])
+    WZ = ["w%d" % d for d in (1, 2, 3, 4, 5, 6)]
+    WB = WZ[0:5] + ["w-1", "w-2", "w-3"]
 
     def windows(first):
         def shift(d):
@@ -166,7 +160,7 @@ def rank_program(g, core, T, topo):
             if first:
                 return ("y", [], ["w%d" % d] if d else XW, W[lo:hi, s0:s0 + n], T.x[lo + 16 * d:hi + 16 * d, :])
             return ("y", XW, ["w%d" % d], W[lo:hi, s0:s0 + n], W[lo + 16 * d:hi + 16 * d, X0:X0 + n])
-        dmas("w1", [shift(d) for d in ((0, 1, 2, 3, -1, 4, -2, 5, -3) if first else (1, 2, 3, -1, 5, -3))])
+        dmas("w1", [shift(d) for d in (0, 1, 2, 3, -1, 4, -2, 5, -3)[0 if first else 1:]])
         dmas("w2", [shift(d) for d in (6, 7)])
 
     dmas("lx", [("y", [], ["x3"], T.x3[:], T.x[:])])
@@ -182,16 +176,15 @@ def rank_program(g, core, T, topo):
     def blk(k, a=0, b=32):
         return T.blk[:, 32 * k + a:32 * k + b]
     w0 = 9 * XE + 128
-    o7 = slice(7 * OW + 2, 7 * OW + 66, 2)
     iota(blk(0), [[32, 4], [2 * XE, 4], [-128, 2]], w0, 0, "blk0")
-    iota(blk(1), [[0, 2], [RW, 4], [0, 4]], 0, 0, "blk1")
+    iota(blk(1), [[0, 2], [L, 4], [0, 4]], 0, 0, "blk1")
     iota(blk(2, 0, 16), [[64, 2], [128, 4], [512, 2]], 0, 1, "blk2")
     iota(blk(2, 16, 32), [[64, 2], [128, 4], [512, 2]], 16, 1, "blk2b")
     iota(blk(3), [[16, 2], [0, 16]], 0, 1, "blk3")
     iota(T.pat[:, 0:6], [[4, 6]], 0, 0, "pat0")
-    iota(T.pat[:, 6:10], [[4 * RW, 2], [0, 2]], RW + 46, 0, "pat1")
-    iota(T.ob[:, o7], [[XE, 2], [4, 16]], -4, 4 * M, "o7")
-    iota(T.oi[:], [[XE, 2], [32, 16]], -32, 0, "oi")
+    iota(T.pat[:, 6:10], [[4 * L, 2], [0, 2]], 45, 0, "pat1")
+    iota(T.oa[:, 0:32], [[XE, 2], [4, 16]], -4, 4 * M, "oa")
+    iota(T.oi[:, 0:32], [[XE, 2], [32, 16]], -32, 0, "oi")
     iota(T.tc[:], [[0, 64], [1, 4]], 0, 0, "tc")
     iota(blk(4), [[8, 4], [C, 4], [4, 2]], 0, 4 * M, "blk4")
     iota(blk(5), [[16, 2], [1, 8], [32, 2]], 1, 0, "blk5")
@@ -208,25 +201,38 @@ def rank_program(g, core, T, topo):
 
     fill(T.zt[:], 0.0, "zt")
     fill(T.one[:], 1.0, "one")
-    fill(T.rr[:, 0:32], -BIG, "rt0")
-    fill(T.rr[96:128, 64:7 * RW:RW], -BIG, "rwi")
-    fill(T.d0[:], BIG, "d0")
-    fill(T.kb[:, 0:66], -BIG, "kb0")
-    fill(T.ff[:], 0.0, "ffi")
-    fill(T.nf[:], 0.0, "nfi")
-    fill(T.lk[:, 0:1], 30, "lk0")
-    fill(T.lk[:, 1:2], 64, "lk1")
+    fill(T.rb[:, 0:L], -BIG, "r0")
+    fill(T.kb[:, 0:L], -BIG, "k0")
+    fill(T.dr[:], 0.0, "dr")
+    fill(T.yy[:], 0.0, "yi")
+    fill(T.dk[:], 0.0, "dk")
+    fill(T.sq[96:128, :], -BIG, "si")
+    fill(T.dl[:], 1.0, "dl")
+    fill(T.df[:], 1.0, "df")
+    fill(T.tn[:, 0:L], 0.0, "t0")
+    fill(T.tn[:, 7 * L:8 * L], 0.0, "t7")
+    fill(T.ff[:], 0.0, "f")
+    fill(T.of[:, 0:1], 0.0, "ofi")
+    fill(T.dr[:, 0:L:48], -BIG, "dr")
+    fill(T.df[:, 0:L:48], 0.0, "df")
     fill(T.lbs[64:128, 0:1], 64, "lbs2")
-    fill(T.d0[:, 0:32:16], -BIG, "d0")
-    fill(T.nf[:, 1:128:64], 1.0, "nfi")
+    order("v", ["dk", "dl"], [])
+    for k in range(2):
+        fill(T.dk[:, 100 * k:100 * k + L:3], -BIG, "dk%d" % k)
+        fill(T.dl[:, 100 * k:100 * k + 1], 0.0, "dl%d" % k)
+        fill(T.dl[:, 100 * k + 46:100 * k + L:48], -1.0, "dm%d" % k)
+    wr["dk"] = wr["dl"] = wr["dm1"]
     do("g", ["one"], ["gt"], lambda: g.affine_select(T.gt[:], T.one[:], [[1, 516]], A.is_equal, 0.0, -3, -4))
     copy("s", T.bt[:, 128:512], T.zt[:, 0:384], ["zt"], ["btz"])
     copy("s", T.dtl[:, 0:128], T.zt[:, 0:128], ["zt"], ["dz0"])
     copy("s", T.dtl[:, 256:640], T.zt[:, 0:384], ["zt"], ["dz1"])
-    wr["r0"] = wr["rt0"]
-    wr["f0"] = wr["f1"] = wr["ffi"]
-    wr["n0"] = wr["n1"] = wr["nfi"]
-    wr["k0a"] = wr["k0b"] = wr["kb0"]
+    for k in range(2):
+        for h in range(2):
+            wr["z%d%d" % (k, h)], wr["st%d%d" % (k, h)], wr["y%d%d" % (k, h)] = wr["dk"], wr["dl"], wr["yi"]
+            wr["r%d%d" % (0, h)], wr["k%d%d" % (0, h)] = wr["r0"], wr["k0"]
+        for c in "AC":
+            wr["s%d%s" % (k, c)] = wr["si"]
+        wr["s%da" % k] = wr["si"]
     quant(T.qn[:], T.sb[:, 0:128], T.zt[:], ["zt"], ["qb"])
     for t in range(R):
         quant(T["ql%d" % t][:, 32:160], T["sl%d" % t][:, 128:256], T.zt[:], ["zt"], ["pad%d" % t])
@@ -235,15 +241,21 @@ def rank_program(g, core, T, topo):
         return T.col[:, 32 * k:32 * k + 1]
 
     tr(T.col[:, 0:128], T.blk[:, 0:128], ["blk0", "blk1", "blk2", "blk2b", "blk3"], ["cola"])
-    ts(T.rr[96:128, RW + 65:7 * RW:RW], T.pat[96:128, 0:6], T.col[96:128, 0:1], None, A.add, None, ["pat0", "cola"], ["rwj"])
-    ts(T.lbx[:], T.pat[:, 6:10], colv(1), float(6 * RW + 46), A.add, A.min, ["pat1", "cola"], ["lbx"])
+    ts(T.wt[96:128, :], T.pat[96:128, 0:6], T.col[96:128, 0:1], None, A.add, None, ["pat0", "cola"], ["wt"])
+    ts(T.lbx[:], T.pat[:, 6:10], colv(1), float(5 * L + 45), A.add, A.min, ["pat1", "cola"], ["lbx"])
     ts(T.lbs[0:64, 0:1], T.col[0:64, 64:65], 0.0625, None, A.mult, None, ["cola"], ["lbs"])
     ts(T.sc[:, 0:1], colv(3), -112.0, None, A.mult, None, ["cola"], ["sc0"])
     ts(T.sc[:, 1:2], colv(3), -112.0, float(X0), A.mult, A.add, ["cola"], ["sc1"])
     ts(T.tb[:, 64:65], colv(3), 112.0, None, A.mult, None, ["cola"], ["tb64"])
     for q0 in (32, 96):
-        ts(T.ob[q0:q0 + 32, o7], T.ob[q0:q0 + 32, o7], float(3 * XE), None, A.add, None, ["o7"], ["o7"])
-        ts(T.oi[q0:q0 + 32, :], T.oi[q0:q0 + 32, :], float(3 * XE), None, A.add, None, ["oi"], ["oi"])
+        ts(T.oa[q0:q0 + 32, 0:32], T.oa[q0:q0 + 32, 0:32], float(3 * XE), None, A.add, None, ["oa"], ["oa"])
+        ts(T.oi[q0:q0 + 32, 0:32], T.oi[q0:q0 + 32, 0:32], float(3 * XE), None, A.add, None, ["oi"], ["oi"])
+
+    def steps(o, key, k):
+        fill(o[:, 0:33:16], 0.0, key)
+        fill(o[:, 15:32:16], 0.0, key)
+        tt(T.tn[:, L * k:L * k + L:3], o[:, 0:32], o[:, 1:33], A.subtract, [key], ["t%d" % k])
+    steps(T.oa, "oa", 0)
 
     def keys_half(hf, reads):
         c0 = 224 * hf
@@ -273,70 +285,137 @@ def rank_program(g, core, T, topo):
         for hf in range(2):
             tr(T.kt[:, 224 * hf:224 * hf + 224], bank(hf, 224), ["ps%d" % hf], ["kt%d" % hf])
         KT = ["kt0", "kt1"]
-        oreg = [7 if t == 0 else 0] + list(range(1, V + 1))
+        treg = [0 if t == 0 else 7] + list(range(1, V + 1))
 
-        def origins(n):
-            a, b, pp = OW * oreg[n - 1], OW * oreg[n], (n - 1) % 2
-            scan(T.ob[:, b + 1:b + 65], T.nf[:, 64 * pp:64 * pp + 64], T.ob[:, a + 2:a + 66], 0.0, A.mult, A.add,
-                 ["o%d" % oreg[n - 1], "bo%d" % oreg[n - 1], "bp%d" % oreg[n - 1], "n%d" % pp], ["o%d" % n, "bo%d" % n, "bp%d" % n])
+        def two(k, n):
+            return ["%s%d%d" % (k, n % 2, h) for h in range(2)]
 
-        for n in range(V + 1):
-            r0, k0, k1, o0, pr = RW * n, KW * n, KW * (n + 1), OW * oreg[n], n % 2
-            rn, ro, fn, nn, on = "r%d" % n, "rt%d" % n, "f%d" % pr, "n%d" % pr, "o%d" % oreg[n]
-            kn = ["k0a", "k0b"] if n == 0 else ["k%d" % n]
-            RN = [rn, ro]
-            if n == 0:
-                for h in range(2):
-                    scan(T.rr[:, 16 * h + 1:16 * h + 15], T.d0[:, 1:15], T.kt[:, 16 * h:C:32], -BIG, A.min, A.max, KT + ["d0"], [RN[h]])
-                src, dst = slice(14, 15), slice(64, 65)
+        def tkeys(n):
+            return ["t%d" % treg[n]] + (["t%d%s" % (n, k) for k in "abcdef"] if n else [])
+
+        def run(buf, n, h, a, b, step=1, size=L):
+            o = size * (n % 2) + 48 * h
+            return buf[:, o + a:o + b:step]
+
+        def gate(n, h, kind):
+            r, m = run(T.rb, n, h, 2, 48, 3), run(T.rb, n, h, 44, 45)
+            key, rk = ["%s%d%d" % (kind, n % 2, h)], ["r%d%d" % (n % 2, h)]
+            if kind == "y":
+                o = 33 * (n % 2) + 1 + 16 * h
+                ts(T.yy[:, o:o + 16], r, m, -BIG, A.is_lt, A.mult, rk, key)
+            elif kind == "z":
+                ts(run(T.dk, n, h, 4, 50, 3, 100), r, m, -BIG, A.is_ge, A.mult, rk, key)
             else:
-                if n < V:
-                    scan(T.rr[:, r0:r0 + 32], T.d0[:], T.kb[:, k0 + 2:k0 + 66:2], -BIG, A.min, A.max, kn + ["d0"], [rn])
-                    src, dst = slice(r0 + 14, r0 + 47, 32), slice(r0 + 64, r0 + 66)
-                else:
-                    src, dst = slice(r0 + 46, r0 + 47), slice(r0 + 65, r0 + 66)
-                scan(T.rr[:, r0 + 32:r0 + 64], T.d0[:], T.kb[:, k0 + 66:k0 + 130:2], -BIG, A.min, A.max, ["t%d" % n, "d0"], [ro])
-            copy("s", T.rr[0:64, dst], T.rr[64:128, src], RN, ["rs%d" % n])
-            copy("s", T.rr[64:96, dst], T.rr[32:64, src], RN, ["ru%d" % n])
-            SH = RN + ["rs%d" % n, "ru%d" % n, "rwi", "rwj"]
-            if n == 0:
-                for h in range(2):
-                    copy("s", T.kb[:, 4 + 32 * h:32 + 32 * h:2], T.kt[:, 16 * h:C:32], KT, [kn[h]])
+                ts(run(T.dl, n, h, 3, 46, 3, 100), run(T.rb, n, h, 2, 45, 3), m, None, A.is_ge, None, rk, key)
+
+        def latch(n, hs):
+            a, b, o = 48 * hs[0], 48 * hs[-1] + 48, L * treg[n]
+            skip = "" if len(hs) == 2 else "cdef" if hs[0] == 0 else "ab"
+            scan(T.lb[:, L * n + a:L * n + b], T.dl[:, 100 * (n % 2) + a:100 * (n % 2) + b], T.tn[:, o + a:o + b], 0.0, A.mult, A.add,
+                 ["st%d%d" % (n % 2, h) for h in hs] + [k for k in tkeys(n) if k[-1] not in skip], ["l%d%d" % (n, h) for h in hs])
+
+        def hot(n):
+            o = 100 * (n % 2)
+            tt(T.ff[:, 0:32], T.dk[:, o + 4:o + 98:3], T.dk[:, o + 1:o + 95:3], A.is_lt, two("z", n), ["f"])
+
+        def edge(n):
+            tt(T.gg[:, 32 * (n % 2):32 * (n % 2) + 32], T.ff[:, 0:32], T.ff[:, 1:33], A.subtract, ["f"], ["g%d_" % (n % 2)])
+
+        def carry(n, part):
+            o, o1 = L * treg[n], L * (n + 1)
+            if part == 0:
+                if n:
+                    tt(T.uu[:], T.tn[:, o + 1:o + L:3], T.tn[:, o + 2:o + L:3], A.add, tkeys(n)[1:], ["u"])
             else:
-                pp, a = 1 - pr, OW * oreg[n - 1]
-                copy("s", T.ob[:, a + 3:a + 35:2], T.ff[:, 32 * pp:32 * pp + 16], RN + ["f%d" % pp], ["bo%d" % oreg[n - 1]],
-                     T.rr[:, r0 + 62:r0 + 63])
-                copy("s", T.ob[:, a + 35:a + 67:2], T.ff[:, 32 * pp + 16:32 * pp + 32], SH + ["f%d" % pp], ["bp%d" % oreg[n - 1]],
-                     T.rr[:, r0 + 65:r0 + 66])
-            if n == V:
+                tt(T.tn[:, o1:o1 + L:3], T.tn[:, o:o + L:3], T.uu[:] if n else T.tn[:, o + 1:o + L:3], A.add,
+                   tkeys(n)[0:1] + ["u"], ["t%d" % (n + 1)])
+
+        def moved(n, which, e="s"):
+            o1, l0, g0 = L * (n + 1), L * n, 32 * (n % 2)
+            jobs = {"a": (0, 1, 0, 128, T.lb[:, l0 + 93:l0 + 94], 1), "b": (0, 2, 0, 128, T.lb[:, l0 + 46:l0 + 47], 0),
+                    "c": (1, 1, 0, 64, T.lb[64:128, l0 + 45:l0 + 46], 0), "d": (1, 1, 64, 96, T.lb[32:64, l0 + 45:l0 + 46], 0),
+                    "e": (1, 2, 0, 128, T.lb[:, l0 + 94:l0 + 95], 1), "f": (1, 1, 96, 128, T.wt[96:128, n:n + 1], None)}
+            for k in which:
+                h, slot, lo, hi, col, src = jobs[k]
+                a = o1 + 48 * h + slot
+                copy(e, T.tn[lo:hi, a:o1 + 48 * h + 48:3], T.gg[lo:hi, g0 + 16 * h:g0 + 16 * h + 16],
+                     ["g%d_" % (n % 2), "wt" if src is None else "l%d%d" % (n, src)], ["t%d%s" % (n + 1, k)], col)
+
+        def enter(n):
+            o, y0 = L * (n % 2), 33 * (n % 2) + 1
+            for k, h, lo, hi, col, src in (("b", 1, 0, 64, T.rb[64:128, o + 44:o + 45], 0), ("c", 1, 64, 96, T.rb[32:64, o + 44:o + 45], 0),
+                                           ("a", 0, 0, 128, T.rb[:, o + 92:o + 93], 1)):
+                out, in_ = T.sq[lo:hi, o + 48 * h:o + 48 * h + 48:3], T.yy[lo:hi, y0 + 16 * h:y0 + 16 * h + 16]
+                do("s", ["y%d%d" % (n % 2, h), "r%d%d" % (n % 2, src)], ["s%d%s" % (n % 2, k)],
+                   lambda: act.activation(out, in_, AF.Identity, bias=col))
+
+        for n in range(V):
+            o, oq, pr = L * (n % 2), L * (1 - n % 2), n % 2
+            SK = ["s%d%s" % (1 - pr, k) for k in "abcAC"] + ["si"]
+            if n == 0:
+                for h in (1, 0):
+                    scan(run(T.rb, 0, h, 5, 45, 3), T.dr[:, 1:15], T.kt[:, 16 * h:C:32], -BIG, A.add, A.max, KT + ["dr"], ["r0%d" % h])
+                for h in range(2):
+                    copy("s", run(T.kb, 0, h, 5, 45, 3), T.kt[:, 16 * h:C:32], KT, ["k0%d" % h])
+            else:
+                scan(T.rb[:, o:o + L], T.dr[:], T.sq[:, oq:oq + L], -BIG, A.add, A.max, SK + ["dr"], two("r", n))
+                edge(n - 1)
+                if n < V - 1:
+                    scan(T.kb[:, o:o + L], T.dk[:, 100 * (1 - pr):100 * (1 - pr) + L], T.sq[:, oq:oq + L], -BIG, A.add, A.max,
+                         SK + two("z", n - 1), two("k", n))
+            if n == V - 1:
                 break
-            piece()
-            for h in range(2):
-                c0 = r0 + 16 * h
-                ts(T.st[:, 16 * h:16 * h + 16], T.rr[:, c0:c0 + 16], T.rr[:, c0 + 14:c0 + 15], None, A.is_ge, None,
-                   [RN[h] if n == 0 else rn], ["st%d" % h])
-            tt(T.ff[:, 32 * pr + 1:32 * pr + 32], T.st[:, 1:32], T.st[:, 0:31], A.is_gt, ["st0", "st1"], [fn])
-            tt(T.nf[:, 64 * pr + 3:64 * pr + 64:2], T.st[:, 1:32], T.st[:, 0:31], A.is_le, ["st0", "st1"], [nn])
-            if n < V - 1:
-                tt(T.kb[:, k0 + 3:k0 + 67:2], T.rr[:, r0:r0 + 65].indirect(T.lk[:]), T.ff[:, 32 * pr:32 * pr + 32], A.mult,
-                   SH + ["lk0", "lk1", fn], ["bk%d" % n])
-            if n > 0:
-                origins(n)
-            if n < V - 1:
-                scan(T.kb[:, k1 + 1:k1 + 65], T.nf[:, 64 * pr:64 * pr + 64], T.kb[:, k0 + 2:k0 + 66], 0.0, A.mult, A.add,
-                     kn + ["bk%d" % n, nn], ["k%d" % (n + 1), "bk%d" % (n + 1)])
-            tt(T.kb[:, k1 + 66:k1 + 130:2], T.ob[:, o0 + 2:o0 + 66:2], T.ff[:, 32 * pr:32 * pr + 32], A.mult, [on, fn], ["t%d" % (n + 1)])
-        tt(T.bx[:], T.rr[:, 0:RW * V + 64].indirect(T.lbx[:]), T.tc[:, 0:64], A.add,
-           [k % m for m in range(V) for k in ("r%d", "rt%d", "rs%d", "ru%d")] + ["rt6", "rwi", "rwj", "lbx", "tc"], ["bx"])
+            gate(n, 1, "y")
+            gate(n, 0, "y")
+            enter(n)
+            gate(n, 0, "z")
+            gate(n, 1, "z")
+            if n:
+                latch(n - 1, [0, 1])
+            keys = T.kb[:, o + 2:o + L:3]
+            tt(T.sq[:, o + 1:o + L:3], keys, T.yy[:, 33 * pr:33 * pr + 32], A.add, two("k", n) + two("y", n), ["s%dA" % pr])
+            if n:
+                carry(n - 1, 0)
+            tt(T.sq[:, o + 2:o + L:3], keys, T.dk[:, 100 * pr + 4:100 * pr + 98:3], A.add, two("k", n) + two("z", n), ["s%dC" % pr])
+            copy("s", T.dl[:, 100 * pr + 3:100 * pr + 94:3], T.dk[:, 100 * pr + 4:100 * pr + 95:3], two("z", n), two("st", n), -1.0 / BIG)
+            if n:
+                moved(n - 1, "abcdef")
+            hot(n)
+            if n:
+                carry(n - 1, 1)
+        n = V - 1
+        gate(n, 0, "st")
+        latch(n - 1, [0, 1])
+        carry(n - 1, 0)
+        gate(n, 0, "z")
+        gate(n, 1, "z")
+        moved(n - 1, "a", "v")
+        moved(n - 1, "b", "s")
+        carry(n - 1, 1)
+        moved(n - 1, "cdef")
+        gate(n, 1, "st")
+        hot(n)
+        latch(n, [0])
+        edge(n)
+        tt(T.bx[:], T.lb[:, 0:L * n + 48].indirect(T.lbx[:]), T.tc[:, 0:64], A.add,
+           [k % m for m in range(V) for k in ("l%d0", "l%d1")][:-1] + ["lbx", "tc"], ["bx"])
+        latch(n, [1])
+        carry(n, 0)
         tr(T.tb[0:32, 0:64], T.bx[0:32, :], ["bx"], ["tba"])
         tr(T.tb[32:64, 0:64], T.bx[0:32, :], ["bx"], ["tbb"])
+        carry(n, 1)
+        moved(n, "abcdef")
         ts(T.offb[:], T.tb[:, 0:65].indirect(T.lbs[:, 0:1]), T.sc[:, 1:2], None, A.add, None,
            ["tba", "tbb", "tb64", "lbs", "lbs2", "sc1"], ["offb"])
-        origins(V)
         wb = W[:, 0:9 * XE]
         copy("s", T.bu[:], wb.indirect(T.offb[:, 8:16]), XW + WB + ["offb"], ["bu"], down)
         copy("v", T.bt[:, 0:128], wb.indirect(T.offb[:, 0:8]), XW + WB + ["offb"], ["bt"], down)
+        scan(T.of[:, 1:L + 1], T.df[:], T.tn[:, L * V:L * V + L], 0.0, A.mult, A.subtract, tkeys(V) + ["df", "ofi"], ["o6"])
         copy("v", T.bt[64:128, 0:128], T.bu[0:64, :], ["bu"], ["bt"])
+        of = slice(0, L, 3)
+        o6 = T.of[:, of]
+        for a in range(2):
+            tr(T.t1[32 * a:32 * a + 32, :], T.of[32 * QUAD[a]:32 * QUAD[a] + 32, of], ["o6"], ["t1%d" % a])
         quant(T.qb[:], T.sb[:, 128:256], T.bt[:], ["bt", "btz"], ["qb"])
         peer = T.cores[(rank + t + 1) % N]
         rid, pid = topo.addr(peer)[0:2]
@@ -357,20 +436,23 @@ def rank_program(g, core, T, topo):
 
         if t == 0:
             ts(T.blk[96:128, 176:192], T.blk[96:128, 176:192], -16.0, None, A.add, None, ["blk5"], ["blk5"])
-        of = slice(OW * V + 2, OW * V + 66, 2)
-        o6 = T.ob[:, of]
-        for a in range(4):
-            tr(T.t1[32 * a:32 * a + 32, :], T.ob[32 * QUAD[a]:32 * QUAD[a] + 32, of], ["o6"], ["t1%d" % a])
-            if t == 0 and a == 0:
+        for a in range(2, 4):
+            tr(T.t1[32 * a:32 * a + 32, :], T.of[32 * QUAD[a]:32 * QUAD[a] + 32, of], ["o6"], ["t1%d" % a])
+            if t == 0 and a == 2:
                 tr(T.col[:, 128:352], T.blk[:, 128:352],
                    ["blk4", "blk5", "blk6", "blk6b", "blk7", "blk8", "blk9", "blk9b", "blk10"], ["colb"])
         if t == 0:
             ts(T.la1[:], T.pat[:, 10:26], colv(9), None, A.add, None, ["pat2", "colb"], ["la1"])
             ts(T.la2[:], T.pat[:, 26:34], colv(5), 255.0, A.add, A.min, ["pat3", "colb"], ["la2"])
         tt(T.a2[:], T.t1[:].indirect(T.la1[:]), T.tc[:], A.add, ["t1%d" % a for a in range(4)] + ["la1", "tc"], ["a2"])
-        tr(T.t7[0:32, :], T.ob[96:128, of], ["o6"], ["t70"])
+        tr(T.t7[0:32, :], T.of[96:128, of], ["o6"], ["t70"])
+        tr(T.t7[32:64, :], T.of[96:128, of], ["o6"], ["t71"])
+        tr(T.t7[64:96, :], T.of[96:128, of], ["o6"], ["t72"])
         tr(T.a3[:], T.a2[:], ["a2"], ["a3"])
-        tr(T.t7[32:64, :], T.ob[96:128, of], ["o6"], ["t71"])
+        tr(T.t7[96:128, :], T.of[96:128, of], ["o6"], ["t73"])
+        if t == 0:
+            ts(T.ll1[:], T.pat[:, 34:38], colv(6), 0.0625, A.add, A.mult, ["pat4", "colb"], ["ll1"])
+            ts(T.ll2[:], T.pat[:, 26:28], colv(7), 63.0, A.add, A.min, ["pat3", "colb"], ["ll2"])
         ts(T.offz[:], T.a3[:].indirect(T.la2[:]), T.sc[:, 0:1], None, A.add, None, ["a3", "la2", "sc0"], ["offz"])
         wz = W[:, X0:X0 + 7 * XE]
         ZA = ["z%d" % a for a in range(4)]
@@ -380,19 +462,17 @@ def rank_program(g, core, T, topo):
             copy(e, T.zz[:, z0:z0 + 16 * (c1 - c0)], wz.indirect(T.offz[:, c0:c1]), XW + WZ + ["offz"], key, down)
         for a in range(3):
             early("s", 32 * a, 32 * a + 28, [ZA[a]])
-        tr(T.t7[64:96, :], T.ob[96:128, of], ["o6"], ["t72"])
-        tr(T.t7[96:128, :], T.ob[96:128, of], ["o6"], ["t73"])
+        tt(T.l2[:], T.t7[:].indirect(T.ll1[:]), T.tc[:, 0:64], A.add, ["t7%d" % a for a in range(4)] + ["ll1", "tc"], ["l2"])
         if t == 0:
-            ts(T.ll1[:], T.pat[:, 34:38], colv(6), 0.0625, A.add, A.mult, ["pat4", "colb"], ["ll1"])
-            ts(T.ll2[:], T.pat[:, 26:28], colv(7), 63.0, A.add, A.min, ["pat3", "colb"], ["ll2"])
             for b in range(4):
                 quant(T.qg[:, 128 * b:128 * b + 128], T.sg[:, 128 * b:128 * b + 128], T.gt[:, 3 - b:515 - b], ["gt"], ["qg%d" % b])
-        tt(T.l2[:], T.t7[:].indirect(T.ll1[:]), T.tc[:, 0:64], A.add, ["t7%d" % a for a in range(4)] + ["ll1", "tc"], ["l2"])
         if t > 0:
             early("v", 96, 110, [ZA[3]])
         else:
-            ts(T.ob[:, 2:66:2], T.oi[:], colv(4), None, A.add, None, ["oi", "colb"], ["o0"])
+            ts(T.oi[:, 0:32], T.oi[:, 0:32], colv(4), None, A.add, None, ["oi", "colb"], ["oi"])
         tr(T.l3[:], T.l2[:], ["l2"], ["l3"])
+        if t == 0:
+            steps(T.oi, "oi", 7)
         if t == 1:
             quant(T.qv[:], T.sv[:], T.vs[:], ["vs"], ["qv"])
             ts(T.sc[:, 2:3], colv(10), XE // 2 - 0.5, SC, A.add, A.mult, ["colb"], ["sc2"])
@@ -453,9 +533,6 @@ def rank_program(g, core, T, topo):
             windows(False)
             for a in range(4):
                 copy("s" if a < 2 else "v", T.xk[:, :, 8 * a:8 * a + 8], W[:, X0 + C * a:X0 + C * a + C], X32[a // 2], [XK[a]], SC)
-            spare.extend((d, a) for a in range(4) for d in (4, -2))
-            for k in range(3):
-                piece()
             keys_half(0, XK)
             keys_half(1, XK)
 

@@ -11,29 +11,33 @@ BIG = float(2 ** 96)
 WHOLE = float(3 * 2 ** 22)
 SC = 0.03125
 L = 96
+DL = 132
 QUAD = [0, 2, 1, 3]
+TREG = [0, 1, 2, 3, 4, 7, 5]
+KB = 48
 CD, BF, F, U8, U16 = "float8_e4m3fn_x4", "bfloat16", "float32", "uint8", "uint16"
 
 SCRATCH = {"ps": ("psum", [128, 4096], F)}
 for _n, _s, _d in [
-        ("W", [HB + 256], BF), ("x3", [P, 4 * M], BF), ("xl", [16, 112], BF), ("xk", [56, 32], BF), ("x32", [56, 32], BF),
-        ("zz", [XE], BF), ("z32", [XE], BF), ("lt", [C], BF), ("us", [4, 128], BF), ("vs", [512], BF), ("zt", [512], BF),
-        ("one", [516], BF), ("gt", [516], BF), ("bt", [512], BF), ("bu", [128], BF), ("dtl", [640], BF),
+        ("W", [HB + 384], BF), ("x3", [P, 4 * M], BF), ("xl", [4, 4, 2, 4 * M], BF), ("xk", [56, 32], BF), ("x32", [112, 16], BF),
+        ("zz", [XE], BF), ("z32", [XE], BF), ("lt", [C], BF), ("us", [4, 128], BF), ("vs", [512], BF), ("zt", [576], BF),
+        ("one", [516], BF), ("gt", [516], BF), ("bt", [512], BF), ("bu", [192], BF), ("dtl", [704], BF),
         ("qx", [C], CD), ("sx", [C], U8), ("qz", [C], CD), ("sz", [C], U8), ("qu", [128], CD), ("su", [128], U8),
         ("qv", [128], CD), ("sv", [128], U8), ("qw", [528], CD), ("sw", [528], U8), ("qg", [512], CD), ("sg", [512], U8),
-        ("qb", [128], CD), ("sb", [256], U8), ("qn", [128], CD), ("qd", [160], CD), ("sd", [160], U8),
-        ("ql0", [160], CD), ("sl0", [256], U8), ("ql1", [160], CD), ("sl1", [256], U8), ("ql2", [160], CD), ("sl2", [256], U8),
+        ("qb", [128], CD), ("sb", [272], U8), ("qn", [144], CD), ("qd", [176], CD), ("sd", [176], U8),
+        ("ql0", [176], CD), ("sl0", [320], U8), ("ql1", [176], CD), ("sl1", [320], U8), ("ql2", [176], CD), ("sl2", [320], U8),
         ("kt", [C], F), ("ys", [C], F), ("rb", [2 * L], F), ("kb", [2 * L], F), ("sq", [2 * L], F), ("yy", [66], F),
-        ("dk", [200], F), ("dl", [200], F), ("dr", [L], F), ("df", [L], F), ("ff", [33], F), ("gg", [64], F), ("uu", [32], F),
-        ("tn", [8 * L], F), ("lb", [V * L], F), ("of", [L + 1], F), ("oa", [33], F), ("oi", [33], F), ("wt", [V], F),
-        ("blk", [352], F), ("col", [352], F),
-        ("pat", [48], F), ("sc", [4], F), ("tc", [256], F), ("bx", [64], F), ("tb", [72], F), ("t1", [32], F), ("t7", [32], F),
+        ("dk", [200], F), ("dl", [2 * DL], F), ("dr", [L], F), ("df", [L], F), ("ff", [33], F), ("gg", [64], F), ("uu", [32], F),
+        ("tn", [8 * L + 32], F), ("lb", [V * L + 32], F), ("of", [L + 1], F), ("wt", [V], F),
+        ("blk", [512], F), ("col", [512], F), ("stg", [7, 2, 16], F), ("stc", [224], F), ("g7", [32], F), ("g8", [32], F),
+        ("pat", [64], F), ("sc", [10], F), ("tc", [256], F), ("bx", [64], F), ("tb", [104], F), ("t1", [32], F), ("t7", [32], F),
         ("a2", [256], F), ("a3", [256], F), ("l2", [64], F), ("l3", [64], F),
         ("g1", [32], F), ("g2", [32], F), ("g3", [32], F), ("g4", [32], F), ("g5", [32], F), ("g6", [32], F),
-        ("lbx", [4], U16), ("lbs", [2], U16), ("la1", [16], U16), ("la2", [8], U16), ("ll1", [4], U16),
-        ("ll2", [2], U16), ("offb", [16], U16), ("offz", [128], U16), ("offl", [32], U16)]:
+        ("lbx", [4], U16), ("lbs", [2], U16), ("lbl", [2], U16), ("la1", [16], U16), ("la2", [8], U16), ("la3", [8], U16),
+        ("ll1", [4], U16), ("ll2", [2], U16), ("ll3", [2], U16),
+        ("offb", [16], U16), ("offc", [16], U16), ("offz", [128], U16), ("offl", [32], U16)]:
     SCRATCH[_n] = ("sbuf", [128] + _s, _d)
-SEMAPHORES = ["v", "s", "t", "g", "lx", "lu", "lw", "lv", "w1", "w2", "sent", "arr0", "arr1", "arr2", "out"]
+SEMAPHORES = ["v", "s", "t", "g", "lx", "lu", "lw", "lv", "w1", "w2", "sent", "arr0", "arr1", "arr2", "og", "out"]
 
 
 def rank_program(g, core, T, topo):
@@ -104,6 +108,9 @@ def rank_program(g, core, T, topo):
     def bank(b, n):
         return ps[:, 512 * b:512 * b + n]
 
+    def alone():
+        wait("g", ("g", count["g"]))
+
     def iota(out, pattern, base, cm, key):
         do("g", [], [key], lambda: g.iota(out, pattern, base, cm, allow_small_or_imprecise_dtypes=True))
 
@@ -136,8 +143,8 @@ def rank_program(g, core, T, topo):
     def quant(q, s, in_, reads, writes):
         do("v", reads, writes, lambda: vec.quantize_mx(q, s, in_))
 
-    def fill(ap, val, key):
-        do("v", [], [key], lambda: vec.memset(ap, val))
+    def fill(ap, val, key, after=()):
+        do("v", list(after), [key], lambda: vec.memset(ap, val))
 
     def mm(b, n, pairs, reads):
         order("t", reads, ["ps%d" % b])
@@ -147,205 +154,303 @@ def rank_program(g, core, T, topo):
         ins.then_inc(S.t, 1)
         note("t", ("t", count["t"]), reads, ["ps%d" % b])
 
-    X32 = [["x32%d%d" % (hf, b) for b in range(4)] for hf in range(2)]
-    XW = X32[0] + X32[1]
-    XK = ["xk%d" % a for a in range(4)]
+    CH = [(0, 128), (128, 320), (320, 448)]
+    CL = [(0, 224), (224, 448)]
+    XW = ["x%d%d" % (c, b) for c in range(3) for b in range(4)]
     WZ = ["w%d" % d for d in (1, 2, 3, 4, 5, 6)]
     WB = WZ[0:5] + ["w-1", "w-2", "w-3"]
 
-    def windows(first):
+    def windows():
         def shift(d):
             lo, hi = (0, 128 - 16 * d) if d >= 0 else (-16 * d, 64)
-            s0, n = X0 + d * XE, C if d == 7 and not first else XE
-            if first:
-                return ("y", [], ["w%d" % d] if d else XW, W[lo:hi, s0:s0 + n], T.x[lo + 16 * d:hi + 16 * d, :])
-            return ("y", XW, ["w%d" % d], W[lo:hi, s0:s0 + n], W[lo + 16 * d:hi + 16 * d, X0:X0 + n])
-        dmas("w1", [shift(d) for d in (0, 1, 2, 3, -1, 4, -2, 5, -3)[0 if first else 1:]])
+            s0 = X0 + d * XE
+            return ("y", XW, ["w%d" % d], W[lo:hi, s0:s0 + XE], W[lo + 16 * d:hi + 16 * d, X0:X0 + XE])
+        dmas("w1", [shift(d) for d in (1, 2, 3, -1, 4, -2, 5, -3)])
         dmas("w2", [shift(d) for d in (6, 7)])
 
     dmas("lx", [("y", [], ["x3"], T.x3[:], T.x[:])])
     dmas("lu", [("y", [], ["us%d" % k], T.us[:, k:k + 3:2, :], T.u[:, 256 * k:256 * k + 256]) for k in range(2)])
-    windows(True)
+    WK = ["qw", "sw", "qw0", "sw0"]
+
+    def blk(k, a=0, b=32):
+        return T.blk[:, 32 * k + a:32 * k + b]
+    w0 = 9 * XE + 4 * KB
+    BK = ["blk%d" % k for k in range(19)]
+    iota(blk(0), [[32, 4], [2 * XE, 4], [-4 * KB, 2]], w0, 0, BK[0])
+    iota(blk(1), [[0, 2], [1, 4], [0, 4]], 0, 0, BK[1])
+    iota(blk(2, 0, 16), [[64, 2], [128, 4], [512, 2]], 0, 1, BK[2])
+    iota(blk(2, 16, 32), [[64, 2], [128, 4], [512, 2]], 16, 1, BK[16])
+    iota(blk(3), [[16, 2], [0, 16]], 0, 1, BK[3])
+    iota(blk(4), [[0, 4], [64, 2], [128, 4]], 0, 0, BK[4])
+    iota(blk(5), [[16, 4], [2 * XE, 4], [-4 * KB, 2]], w0 + 128, 0, BK[5])
+    iota(T.pat[:, 0:16], [[4, 8], [0, 2]], 0, 0, "pat0")
+
+    def more():
+        iota(blk(6, 0, 16), [[128, 2], [16, 2], [0, 4]], 0, 1, BK[6])
+        iota(blk(6, 16, 32), [[128, 2], [16, 2], [0, 4]], 0, 1, BK[17])
+        iota(blk(7), [[-16, 2], [1, 8], [32, 2]], 17, 0, BK[7])
+        iota(blk(8), [[8 - 256, 4], [2 - 16 * XE, 4], [1 + 32 * KB, 2]], 8 * C - 8 * w0, 0, BK[8])
+        iota(blk(9, 0, 16), [[8, 2], [1, 2], [0, 4]], 0, 0, BK[9])
+        iota(blk(9, 16, 32), [[8, 2], [1, 2], [0, 4]], 0, 0, BK[18])
+        iota(blk(10), [[1, 32]], 0, 0, BK[10])
+        iota(blk(11), [[-16, 2], [1, 16]], 17, 0, BK[11])
+        iota(blk(12), [[-16, 2], [1, 16]], 17, 0, BK[12])
+        iota(blk(13), [[0, 4], [2, 4], [0, 2]], 0, 0, BK[13])
+        iota(blk(14), [[8 - 32, 4], [128 - 8, 4], [0, 2]], 0, 0, BK[14])
+        iota(blk(15), [[8, 4], [128, 4], [4, 2]], 0, 0, BK[15])
+        iota(T.pat[:, 16:32], [[2, 4], [16, 2], [0, 2]], 0, 0, "pat1")
+        iota(T.pat[:, 32:40], [[32, 2], [64, 4]], 0, 0, "pat2")
+        for h, lo in ((0, 0), (1, 0), (1, 96)):
+            if lo:
+                alone()
+                iota(T.blk[96:128, 400:416], [[1, 16]], 17, 0, BK[12])
+            for c0, c1 in CH:
+                k0 = c0 // 64
+                iota(T.stg[lo:128, k0:c1 // 64, h, :], [[64, 4], [1, (c1 - c0) // 32], [32, 2]], (1 if h and not lo else 17) + c0 // 32, 0,
+                     "stg%d%d" % (h, k0))
+    T0 = ["t0"] + ["t0%d%d" % (a, k) for a in range(4) for k in range(2)]
+
+    def put(ap, n, val, key, after=()):
+        do("s", ["zt"] + list(after), [key], lambda: act.activation(ap, T.zt[:, 0:n], AF.Identity, bias=val))
+    fill(T.zt[:], 0.0, "zt")
+    fill(T.tn[:, 0:L], 0.0, "t0z")
+    fill(T.dk[:], 0.0, "dk")
+    fill(T.dl[:], 1.0, "dl")
+    fill(T.dr[:], 0.0, "dr")
+    fill(T.df[:], 1.0, "df")
+    fill(T.tn[:, 8 * L:8 * L + 32], 1.0, "tail")
+    fill(T.rb[:, 0:L], -BIG, "r0")
+    fill(T.kb[:, 0:L], -BIG, "k0")
+    fill(T.yy[:], 0.0, "yi")
+    fill(T.sq[96:128, :], -BIG, "si")
+    fill(T.one[:], 1.0, "one")
+    quant(T.qn[:], T.sb[:, 0:3 * KB], T.zt[:], ["zt"], ["qb"])
+    for t in range(R):
+        quant(T["ql%d" % t][:, KB:KB + 128], T["sl%d" % t][:, 4 * KB:4 * KB + 128], T.zt[:, 0:512], ["zt"], ["pad%d" % t])
+    for k in range(2):
+        put(T.tn[:, 48 * k + 3:48 * k + 42:3], 13, -128.0, "t0" if k else "t0y", ["t0z"])
+    put(T.ff[:], 33, 0.0, "f")
+    put(T.of[:, 0:1], 1, 0.0, "ofi")
+    for k in range(2):
+        put(T.dk[:, 100 * k:100 * k + L:3], 32, -BIG, "dk%d" % k, ["dk"])
+    for k in range(2):
+        put(T.dl[:, DL * k:DL * k + 1], 1, 0.0, "dl%d" % k, ["dl"])
+        for c in (46, 47):
+            put(T.dl[:, DL * k + c:DL * k + L:48], 2, -1.0, "dm%d%d" % (k, c))
+    put(T.dr[:, 0:L:48], 2, -BIG, "dr")
+    put(T.df[:, 0:L:48], 2, 0.0, "df")
+    put(T.tn[:, 6 * L:7 * L], L, 0.0, "pz")
+    put(T.tn[:, 8 * L + 4:8 * L + 32:4], 7, -3.0, "tail3", ["tail"])
+    for k in range(2):
+        put(T.tn[:, 6 * L + 48 * k + 3:6 * L + 48 * k + 42:3], 13, -32.0, "py%d" % k, ["pz"])
+    put(T.tn[:, 8 * L:8 * L + 1], 1, 0.0, "tail")
+    wr["dk"] = wr["dl"] = wr["tail"]
+    order("g", ["t0z"], [])
+    for a in range(4):
+        q0 = 32 * QUAD[a]
+        if a == 1:
+            alone()
+        iota(T.tn[q0:q0 + 32, 0:L:48], [[XE, 2]], -(2 * a + 1) * XE, -4, T0[1 + 2 * a])
+        iota(T.tn[q0:q0 + 32, 42:L:48], [[-XE, 2]], (2 * a + 1) * XE + 128 * (M - 1), 4, T0[2 + 2 * a])
+    alone()
+    iota(T.tc[:], [[0, 64], [1, 4]], 0, 0, "tc")
+    iota(T.bt[:, 4 * KB:512], [[0, 512 - 4 * KB]], 0, 0, "btz")
+    more()
+    alone()
+    do("g", ["one"], ["gt"], lambda: g.affine_select(T.gt[:], T.one[:], [[1, 516]], A.is_equal, 0.0, -3, -4))
+    for k in range(2):
+        for h in range(2):
+            wr["z%d%d" % (k, h)], wr["st%d%d" % (k, h)], wr["y%d%d" % (k, h)] = wr["dk"], wr["dl"], wr["yi"]
+            wr["r%d%d" % (0, h)], wr["k%d%d" % (0, h)] = wr["r0"], wr["k0"]
+        for c in "ACa":
+            wr["s%d%s" % (k, c)] = wr["si"]
+
+    def colv(k):
+        return T.col[:, 32 * k:32 * k + 1]
+
+    def lists():
+        fill(T.lbs[64:128, 0:1], 64, "lbs2")
+        fill(T.lbl[64:128, 0:1], 64, "lbl2")
+        fill(T.lbx[:, 2:4], 4 * L + 93, "lbx2")
+        fill(T.dtl[:, 0:4 * KB], 0.0, "dz0")
+        fill(T.dtl[:, 8 * KB:704], 0.0, "dz1")
+        yield
+        tr(T.col[:, 0:192], T.blk[:, 0:192], BK[0:6] + BK[16:17], ["cola"])
+        yield
+        ts(T.wt[96:128, 0:5], T.pat[96:128, 0:10:2], T.col[96:128, 0:1], None, A.add, None, ["pat0", "cola"], ["wt"])
+        copy("v", T.wt[96:128, 5:6], T.col[96:128, 160:161], ["cola"], ["wt5"])
+        ts(T.sc[:, 2:3], colv(1), float(L), 93.0, A.mult, A.add, ["cola"], ["sc2"])
+        ts(T.sc[0:64, 3:4], T.col[0:64, 96:97], T.col[0:64, 128:129], None, A.add, None, ["cola"], ["sc3"])
+        yield
+        ts(T.sc[:, 0:1], colv(3), -112.0, None, A.mult, None, ["cola"], ["sc0"])
+        ts(T.sc[:, 1:2], colv(3), -112.0, float(X0), A.mult, A.add, ["cola"], ["sc1"])
+        ts(T.tb[:, 64:65], colv(3), 112.0, None, A.mult, None, ["cola"], ["tb64"])
+        yield
+        ts(T.lbs[0:64, 0:1], T.col[0:64, 64:65], 0.0625, None, A.mult, None, ["cola"], ["lbs"])
+        ts(T.lbx[:, 0:2], T.pat[:, 0:2], T.sc[:, 2:3], None, A.add, None, ["pat0", "sc2"], ["lbx"])
+        yield
+        ts(T.lbl[0:64, 0:1], T.sc[0:64, 3:4], 0.0625, 72.0, A.mult, A.add, ["sc3"], ["lbl"])
+        yield
+        tr(T.col[:, 192:352], T.blk[:, 192:352], BK[6:11] + BK[17:19], ["col"])
+        yield
+        ts(T.la1[:], T.pat[:, 16:32], colv(9), None, A.add, None, ["pat1", "col"], ["la1"])
+        ts(T.ll1[:], T.pat[:, 0:4], 64.0, colv(6), A.mult, A.add, ["pat0", "col"], ["ll1"])
+        ts(T.ll2[:], T.pat[:, 0:4:2], 2.0, colv(7), A.mult, A.add, ["pat0", "col"], ["ll2"])
+        yield
+        tr(T.stc[:], T.stg[:], ["stg%d%d" % (h, c0 // 64) for h in range(2) for c0, c1 in CH], ["stc"])
+        yield
+        ts(T.ll1[:], T.ll1[:], 0.0625, None, A.mult, None, ["ll1"], ["ll1"])
+        ts(T.ll2[:], T.ll2[:], 63.0, None, A.min, None, ["ll2"], ["ll2"])
+        copy("v", T.la2[:, 0:7], T.stc[:, 0:224:32], ["stc"], ["la2"])
+        yield
+        for b in range(4):
+            quant(T.qg[:, 128 * b:128 * b + 128], T.sg[:, 128 * b:128 * b + 128], T.gt[:, 3 - b:515 - b], ["gt"], ["qg%d" % b])
+            yield
+        tr(T.col[:, 352:512], T.blk[:, 352:512], BK[11:16], ["colc"])
+        yield
+        o = 6 * L
+        ts(T.tn[:, o:o + L:48], T.tn[:, 0:L:48], colv(14), None, A.subtract, None, T0 + ["colc", "pz"], ["pa"])
+        ts(T.tn[:, o + 42:o + L:48], T.tn[:, 42:L:48], colv(14), -288.0, A.add, A.add, T0 + ["colc", "pz"], ["pb"])
+        ts(T.sc[:, 4:5], colv(13), 32.0, None, A.mult, None, ["colc"], ["sc4"])
+        yield
+        ts(T.tn[:, o + 12:o + L:48], T.tn[:, o + 13:o + L:48], T.sc[:, 4:5], -416.0, A.subtract, A.add, ["sc4", "py0", "py1"], ["pc"])
+        ts(T.tn[:, o + 30:o + L:48], T.tn[:, o + 31:o + L:48], T.sc[:, 4:5], -608.0, A.add, A.add, ["sc4", "py0", "py1"], ["pd"])
+        yield
+        quant(T.qv[:], T.sv[:], T.vs[:], ["vs"], ["qv"])
+        yield
+        ts(T.la3[:], T.pat[:, 32:40], colv(12), 255.0, A.add, A.min, ["pat2", "colc"], ["la3"])
+        ts(T.ll3[:], T.pat[:, 0:4:2], 8.0, colv(11), A.mult, A.add, ["pat0", "colc"], ["ll3"])
+        ts(T.sc[:, 5:6], colv(10), float(32 * M), colv(15), A.mult, A.subtract, ["col", "colc"], ["sc5"])
+        ts(T.sc[:, 6:7], colv(10), float(M), 3.0, A.mult, A.add, ["col"], ["sc6"])
+        yield
+        ts(T.ll3[:], T.ll3[:], 63.0, None, A.min, None, ["ll3"], ["ll3"])
+        ts(T.sc[:, 5:6], T.sc[:, 5:6], XE // 2 - 0.5, SC, A.add, A.mult, ["sc5"], ["sc5"])
+        ts(T.sc[:, 7:8], colv(10), float(M), 9.0, A.mult, A.add, ["col"], ["sc7"])
+        ts(T.sc[:, 8:9], colv(13), 12.0, None, A.add, None, ["colc"], ["sc8"])
+        yield
+        ts(T.sc[:, 9:10], colv(10), float(8 * C + 5 * P), None, A.add, None, ["col"], ["sc9"])
+        yield
+    todo = [lists()]
+
+    def spare(k=1):
+        for _ in range(k):
+            next(todo[0], None)
+
+    def keys(c, src, reads):
+        c0, c1 = CH[c]
+        quant(T.qx[:, c0:c1], T.sx[:, c0:c1], src, reads, ["qx%d" % c])
+        if "qu" not in wr:
+            spare()
+            quant(T.qu[:], T.su[:], T.us[:], ["us0", "us1"], ["qu"])
+        mm(4 + c, c1 - c0, [(T.qu[:], T.su[:], T.qx[:, c0:c1], T.sx[:, c0:c1])], ["qu", "qx%d" % c])
+
+    def turn(c):
+        c0, c1 = CH[c]
+        tr(T.kt[:, c0:c1], bank(4 + c, c1 - c0), ["ps%d" % (4 + c)], ["kt%d" % c])
+
+    XJ = ["xj%d" % j for j in range(M)]
+
+    def lay(e, j):
+        copy(e, W[:, X0 + 128 * j:X0 + 128 * j + 128], T.x3[:, :, 4 * j:4 * j + 4], ["x3"], [XJ[j]])
+
+    def first(c):
+        c0, c1 = CH[c]
+        keys(c, W[:, X0 + 4 * c0:X0 + 4 * c1], XJ[c0 // 32:c1 // 32])
+    for j in (8, 9, 10, 11, 12, 13):
+        lay("s", j)
+    for j in range(8):
+        lay("v", j)
+    XW0, XW[:] = list(XW), XJ
+    windows()
     dmas("lw", [("y", [], ["qw"], T.qw[:, 16:528].bitcast(u8), T.wc[:]),
                 ("y", [], ["sw"], T.sw[:, 16:528], T.ws[:]),
                 ("y", [], ["qw0"], T.qw[:, 0:16].bitcast(u8), T.wc[:, 0:64]),
                 ("y", [], ["sw0"], T.sw[:, 0:16], T.ws[:, 0:16])])
     dmas("lv", [("y", [], ["vs"], T.vs[:], T.v[:])])
-    WK = ["qw", "sw", "qw0", "sw0"]
-
-    def blk(k, a=0, b=32):
-        return T.blk[:, 32 * k + a:32 * k + b]
-    w0 = 9 * XE + 128
-    iota(blk(0), [[32, 4], [2 * XE, 4], [-128, 2]], w0, 0, "blk0")
-    iota(blk(1), [[0, 2], [L, 4], [0, 4]], 0, 0, "blk1")
-    iota(blk(2, 0, 16), [[64, 2], [128, 4], [512, 2]], 0, 1, "blk2")
-    iota(blk(2, 16, 32), [[64, 2], [128, 4], [512, 2]], 16, 1, "blk2b")
-    iota(blk(3), [[16, 2], [0, 16]], 0, 1, "blk3")
-    iota(T.pat[:, 0:6], [[4, 6]], 0, 0, "pat0")
-    iota(T.pat[:, 6:10], [[4 * L, 2], [0, 2]], 45, 0, "pat1")
-    iota(T.oa[:, 0:32], [[XE, 2], [4, 16]], -4, 4 * M, "oa")
-    iota(T.oi[:, 0:32], [[XE, 2], [32, 16]], -32, 0, "oi")
-    iota(T.tc[:], [[0, 64], [1, 4]], 0, 0, "tc")
-    iota(blk(4), [[8, 4], [C, 4], [4, 2]], 0, 4 * M, "blk4")
-    iota(blk(5), [[16, 2], [1, 8], [32, 2]], 1, 0, "blk5")
-    iota(blk(6, 0, 16), [[128, 2], [16, 2], [0, 4]], 0, 1, "blk6")
-    iota(blk(6, 16, 32), [[128, 2], [16, 2], [0, 4]], 0, 1, "blk6b")
-    iota(blk(7), [[16, 2], [1, 8], [32, 2]], 1, 0, "blk7")
-    iota(blk(8), [[8 - 256, 4], [2 - 16 * XE, 4], [1 + 1024, 2]], 8 * C - 8 * w0, 0, "blk8")
-    iota(blk(9, 0, 16), [[8, 2], [1, 2], [0, 4]], 0, 0, "blk9")
-    iota(blk(9, 16, 32), [[8, 2], [1, 2], [0, 4]], 0, 0, "blk9b")
-    iota(blk(10), [[8 * C - 8, 4], [C, 4], [C - 4, 2]], 0, 0, "blk10")
-    iota(T.pat[:, 10:26], [[2, 4], [16, 2], [0, 2]], 0, 0, "pat2")
-    iota(T.pat[:, 26:34], [[64, 4], [8, 2]], 0, 0, "pat3")
-    iota(T.pat[:, 34:38], [[256, 2], [0, 2]], 0, 0, "pat4")
-
-    fill(T.zt[:], 0.0, "zt")
-    fill(T.one[:], 1.0, "one")
-    fill(T.rb[:, 0:L], -BIG, "r0")
-    fill(T.kb[:, 0:L], -BIG, "k0")
-    fill(T.dr[:], 0.0, "dr")
-    fill(T.yy[:], 0.0, "yi")
-    fill(T.dk[:], 0.0, "dk")
-    fill(T.sq[96:128, :], -BIG, "si")
-    fill(T.dl[:], 1.0, "dl")
-    fill(T.df[:], 1.0, "df")
-    fill(T.tn[:, 0:L], 0.0, "t0")
-    fill(T.tn[:, 7 * L:8 * L], 0.0, "t7")
-    fill(T.ff[:], 0.0, "f")
-    fill(T.of[:, 0:1], 0.0, "ofi")
-    fill(T.dr[:, 0:L:48], -BIG, "dr")
-    fill(T.df[:, 0:L:48], 0.0, "df")
-    fill(T.lbs[64:128, 0:1], 64, "lbs2")
-    order("v", ["dk", "dl"], [])
-    for k in range(2):
-        fill(T.dk[:, 100 * k:100 * k + L:3], -BIG, "dk%d" % k)
-        fill(T.dl[:, 100 * k:100 * k + 1], 0.0, "dl%d" % k)
-        fill(T.dl[:, 100 * k + 46:100 * k + L:48], -1.0, "dm%d" % k)
-    wr["dk"] = wr["dl"] = wr["dm1"]
-    do("g", ["one"], ["gt"], lambda: g.affine_select(T.gt[:], T.one[:], [[1, 516]], A.is_equal, 0.0, -3, -4))
-    copy("s", T.bt[:, 128:512], T.zt[:, 0:384], ["zt"], ["btz"])
-    copy("s", T.dtl[:, 0:128], T.zt[:, 0:128], ["zt"], ["dz0"])
-    copy("s", T.dtl[:, 256:640], T.zt[:, 0:384], ["zt"], ["dz1"])
-    for k in range(2):
-        for h in range(2):
-            wr["z%d%d" % (k, h)], wr["st%d%d" % (k, h)], wr["y%d%d" % (k, h)] = wr["dk"], wr["dl"], wr["yi"]
-            wr["r%d%d" % (0, h)], wr["k%d%d" % (0, h)] = wr["r0"], wr["k0"]
-        for c in "AC":
-            wr["s%d%s" % (k, c)] = wr["si"]
-        wr["s%da" % k] = wr["si"]
-    quant(T.qn[:], T.sb[:, 0:128], T.zt[:], ["zt"], ["qb"])
-    for t in range(R):
-        quant(T["ql%d" % t][:, 32:160], T["sl%d" % t][:, 128:256], T.zt[:], ["zt"], ["pad%d" % t])
-
-    def colv(k):
-        return T.col[:, 32 * k:32 * k + 1]
-
-    tr(T.col[:, 0:128], T.blk[:, 0:128], ["blk0", "blk1", "blk2", "blk2b", "blk3"], ["cola"])
-    ts(T.wt[96:128, :], T.pat[96:128, 0:6], T.col[96:128, 0:1], None, A.add, None, ["pat0", "cola"], ["wt"])
-    ts(T.lbx[:], T.pat[:, 6:10], colv(1), float(5 * L + 45), A.add, A.min, ["pat1", "cola"], ["lbx"])
-    ts(T.lbs[0:64, 0:1], T.col[0:64, 64:65], 0.0625, None, A.mult, None, ["cola"], ["lbs"])
-    ts(T.sc[:, 0:1], colv(3), -112.0, None, A.mult, None, ["cola"], ["sc0"])
-    ts(T.sc[:, 1:2], colv(3), -112.0, float(X0), A.mult, A.add, ["cola"], ["sc1"])
-    ts(T.tb[:, 64:65], colv(3), 112.0, None, A.mult, None, ["cola"], ["tb64"])
-    for q0 in (32, 96):
-        ts(T.oa[q0:q0 + 32, 0:32], T.oa[q0:q0 + 32, 0:32], float(3 * XE), None, A.add, None, ["oa"], ["oa"])
-        ts(T.oi[q0:q0 + 32, 0:32], T.oi[q0:q0 + 32, 0:32], float(3 * XE), None, A.add, None, ["oi"], ["oi"])
-
-    def steps(o, key, k):
-        fill(o[:, 0:33:16], 0.0, key)
-        fill(o[:, 15:32:16], 0.0, key)
-        tt(T.tn[:, L * k:L * k + L:3], o[:, 0:32], o[:, 1:33], A.subtract, [key], ["t%d" % k])
-    steps(T.oa, "oa", 0)
-
-    def keys_half(hf, reads):
-        c0 = 224 * hf
-        quant(T.qx[:, c0:c0 + 224], T.sx[:, c0:c0 + 224], T.xk[:, 28 * hf:28 * hf + 28, :], reads, ["qx%d" % hf])
-        if "qu" not in wr:
-            quant(T.qu[:], T.su[:], T.us[:], ["us0", "us1"], ["qu"])
-        mm(hf, 224, [(T.qu[:], T.su[:], T.qx[:, c0:c0 + 224], T.sx[:, c0:c0 + 224])], ["qu", "qx%d" % hf])
-
-    XJ = ["xj%d" % j for j in range(M)]
-
-    def lay(e, j):
-        copy(e, T.xk[:, 4 * j:4 * j + 4, :], T.x3[:, :, 4 * j:4 * j + 4], ["x3"], [XJ[j]])
-    for j in (5, 6, 10, 11, 12, 13):
-        lay("s", j)
-    for j in range(5):
-        lay("v", j)
-    keys_half(0, XJ[0:7])
-    for j in range(7, 10):
-        lay("v", j)
-    keys_half(1, XJ[7:14])
-    for k in XK:
-        wr[k] = wr["qx1"]
+    first(0)
+    first(1)
+    first(2)
+    spare()
+    turn(0)
+    turn(1)
+    turn(2)
+    spare()
 
     for t in range(R):
         last = t == R - 1
         down = None if t == 0 else SC
-        for hf in range(2):
-            tr(T.kt[:, 224 * hf:224 * hf + 224], bank(hf, 224), ["ps%d" % hf], ["kt%d" % hf])
-        KT = ["kt0", "kt1"]
-        treg = [0 if t == 0 else 7] + list(range(1, V + 1))
+        KT = ["kt0", "kt1", "kt2"]
+        treg = [6 if t else 0] + TREG[1:]
 
         def two(k, n):
             return ["%s%d%d" % (k, n % 2, h) for h in range(2)]
 
         def tkeys(n):
-            return ["t%d" % treg[n]] + (["t%d%s" % (n, k) for k in "abcdef"] if n else [])
+            if n:
+                return ["t%d" % n] + ["t%d%s" % (n, k) for k in "abcdef"]
+            return ["py0", "py1", "pa", "pb", "pc", "pd"] if t else T0
 
         def run(buf, n, h, a, b, step=1, size=L):
-            o = size * (n % 2) + 48 * h
+            o = size * (n % 2) + 48 * (1 - h)
             return buf[:, o + a:o + b:step]
 
         def gate(n, h, kind):
             r, m = run(T.rb, n, h, 2, 48, 3), run(T.rb, n, h, 44, 45)
             key, rk = ["%s%d%d" % (kind, n % 2, h)], ["r%d%d" % (n % 2, h)]
             if kind == "y":
-                o = 33 * (n % 2) + 1 + 16 * h
+                o = 33 * (n % 2) + 17 - 16 * h
                 ts(T.yy[:, o:o + 16], r, m, -BIG, A.is_lt, A.mult, rk, key)
             elif kind == "z":
                 ts(run(T.dk, n, h, 4, 50, 3, 100), r, m, -BIG, A.is_ge, A.mult, rk, key)
             else:
-                ts(run(T.dl, n, h, 3, 46, 3, 100), run(T.rb, n, h, 2, 45, 3), m, None, A.is_ge, None, rk, key)
+                ts(run(T.dl, n, h, 3, 46, 3, DL), run(T.rb, n, h, 2, 45, 3), m, None, A.is_ge, None, rk, key)
 
         def latch(n, hs):
-            a, b, o = 48 * hs[0], 48 * hs[-1] + 48, L * treg[n]
-            skip = "" if len(hs) == 2 else "cdef" if hs[0] == 0 else "ab"
-            scan(T.lb[:, L * n + a:L * n + b], T.dl[:, 100 * (n % 2) + a:100 * (n % 2) + b], T.tn[:, o + a:o + b], 0.0, A.mult, A.add,
-                 ["st%d%d" % (n % 2, h) for h in hs] + [k for k in tkeys(n) if k[-1] not in skip], ["l%d%d" % (n, h) for h in hs])
+            a, b = (0, L) if len(hs) == 2 else (0, 48) if hs[0] else (48, L + 32)
+            o, d = L * treg[n], DL * (n % 2)
+            skip = "" if len(hs) == 2 else "ab" if hs[0] else "cdef"
+            scan(T.lb[:, L * n + a:L * n + b], T.dl[:, d + a:d + b], T.tn[:, o + a:o + b], 0.0, A.mult, A.add,
+                 ["st%d%d" % (n % 2, h) for h in hs] + [k for k in tkeys(n) if k[-1] not in skip] + ["tail"],
+                 ["l%d%d" % (n, h) for h in hs])
 
         def hot(n):
-            o = 100 * (n % 2)
-            tt(T.ff[:, 0:32], T.dk[:, o + 4:o + 98:3], T.dk[:, o + 1:o + 95:3], A.is_lt, two("z", n), ["f"])
+            if n < V - 1:
+                o = 33 * (n % 2)
+                tt(T.ff[:, 0:32], T.yy[:, o + 1:o + 33], T.yy[:, o:o + 32], A.is_gt, two("y", n), ["f"])
+            else:
+                o = DL * (n % 2)
+                tt(T.ff[:, 0:32], T.dl[:, o + 3:o + 97:3], T.dl[:, o:o + 94:3], A.is_gt, two("st", n), ["f"])
 
         def edge(n):
             tt(T.gg[:, 32 * (n % 2):32 * (n % 2) + 32], T.ff[:, 0:32], T.ff[:, 1:33], A.subtract, ["f"], ["g%d_" % (n % 2)])
 
         def carry(n, part):
-            o, o1 = L * treg[n], L * (n + 1)
+            o, o1 = L * treg[n], L * treg[n + 1]
             if part == 0:
                 if n:
                     tt(T.uu[:], T.tn[:, o + 1:o + L:3], T.tn[:, o + 2:o + L:3], A.add, tkeys(n)[1:], ["u"])
-            else:
-                tt(T.tn[:, o1:o1 + L:3], T.tn[:, o:o + L:3], T.uu[:] if n else T.tn[:, o + 1:o + L:3], A.add,
-                   tkeys(n)[0:1] + ["u"], ["t%d" % (n + 1)])
+            elif n:
+                tt(T.tn[:, o1:o1 + L:3], T.tn[:, o:o + L:3], T.uu[:], A.add, tkeys(n)[0:1] + ["u"], ["t%d" % (n + 1)])
+            elif t < 2:
+                copy("v", T.tn[:, o1:o1 + L:3], T.tn[:, o:o + L:3], tkeys(0), ["t1"])
 
         def moved(n, which, e="s"):
-            o1, l0, g0 = L * (n + 1), L * n, 32 * (n % 2)
-            jobs = {"a": (0, 1, 0, 128, T.lb[:, l0 + 93:l0 + 94], 1), "b": (0, 2, 0, 128, T.lb[:, l0 + 46:l0 + 47], 0),
-                    "c": (1, 1, 0, 64, T.lb[64:128, l0 + 45:l0 + 46], 0), "d": (1, 1, 64, 96, T.lb[32:64, l0 + 45:l0 + 46], 0),
-                    "e": (1, 2, 0, 128, T.lb[:, l0 + 94:l0 + 95], 1), "f": (1, 1, 96, 128, T.wt[96:128, n:n + 1], None)}
+            o1, l0, g0 = L * TREG[n + 1], L * n, 32 * (n % 2)
+            jobs = {"a": (0, 1, 0, 128, T.lb[:, l0 + 45:l0 + 46], 1), "b": (0, 2, 0, 128, T.lb[:, l0 + 94:l0 + 95], 0),
+                    "c": (1, 1, 0, 64, T.lb[64:128, l0 + 93:l0 + 94], 0), "d": (1, 1, 64, 96, T.lb[32:64, l0 + 93:l0 + 94], 0),
+                    "e": (1, 2, 0, 128, T.lb[:, l0 + 46:l0 + 47], 1), "f": (1, 1, 96, 128, T.wt[96:128, n:n + 1], None)}
             for k in which:
                 h, slot, lo, hi, col, src = jobs[k]
-                a = o1 + 48 * h + slot
-                copy(e, T.tn[lo:hi, a:o1 + 48 * h + 48:3], T.gg[lo:hi, g0 + 16 * h:g0 + 16 * h + 16],
-                     ["g%d_" % (n % 2), "wt" if src is None else "l%d%d" % (n, src)], ["t%d%s" % (n + 1, k)], col)
+                a = o1 + 48 * (1 - h)
+                copy(e, T.tn[lo:hi, a + slot:a + 48:3], T.gg[lo:hi, g0 + 16 - 16 * h:g0 + 32 - 16 * h],
+                     ["g%d_" % (n % 2), ("wt5" if n == 5 else "wt") if src is None else "l%d%d" % (n, src)], ["t%d%s" % (n + 1, k)], col)
 
         def enter(n):
-            o, y0 = L * (n % 2), 33 * (n % 2) + 1
-            for k, h, lo, hi, col, src in (("b", 1, 0, 64, T.rb[64:128, o + 44:o + 45], 0), ("c", 1, 64, 96, T.rb[32:64, o + 44:o + 45], 0),
-                                           ("a", 0, 0, 128, T.rb[:, o + 92:o + 93], 1)):
-                out, in_ = T.sq[lo:hi, o + 48 * h:o + 48 * h + 48:3], T.yy[lo:hi, y0 + 16 * h:y0 + 16 * h + 16]
+            o, y0 = L * (n % 2), 33 * (n % 2) + 17
+            for k, h, lo, hi, col, src in (("b", 1, 0, 64, T.rb[64:128, o + 92:o + 93], 0), ("c", 1, 64, 96, T.rb[32:64, o + 92:o + 93], 0),
+                                           ("a", 0, 0, 128, T.rb[:, o + 44:o + 45], 1)):
+                a = o + 48 * (1 - h)
+                out, in_ = T.sq[lo:hi, a:a + 48:3], T.yy[lo:hi, y0 - 16 * h:y0 - 16 * h + 16]
                 do("s", ["y%d%d" % (n % 2, h), "r%d%d" % (n % 2, src)], ["s%d%s" % (n % 2, k)],
                    lambda: act.activation(out, in_, AF.Identity, bias=col))
 
@@ -357,66 +462,78 @@ def rank_program(g, core, T, topo):
                     scan(run(T.rb, 0, h, 5, 45, 3), T.dr[:, 1:15], T.kt[:, 16 * h:C:32], -BIG, A.add, A.max, KT + ["dr"], ["r0%d" % h])
                 for h in range(2):
                     copy("s", run(T.kb, 0, h, 5, 45, 3), T.kt[:, 16 * h:C:32], KT, ["k0%d" % h])
+                spare()
             else:
                 scan(T.rb[:, o:o + L], T.dr[:], T.sq[:, oq:oq + L], -BIG, A.add, A.max, SK + ["dr"], two("r", n))
-                edge(n - 1)
+                latch(n - 1, [0, 1])
                 if n < V - 1:
                     scan(T.kb[:, o:o + L], T.dk[:, 100 * (1 - pr):100 * (1 - pr) + L], T.sq[:, oq:oq + L], -BIG, A.add, A.max,
                          SK + two("z", n - 1), two("k", n))
+                carry(n - 1, 1)
             if n == V - 1:
                 break
+            if n:
+                moved(n - 1, "acd")
             gate(n, 1, "y")
             gate(n, 0, "y")
             enter(n)
             gate(n, 0, "z")
             gate(n, 1, "z")
             if n:
-                latch(n - 1, [0, 1])
-            keys = T.kb[:, o + 2:o + L:3]
-            tt(T.sq[:, o + 1:o + L:3], keys, T.yy[:, 33 * pr:33 * pr + 32], A.add, two("k", n) + two("y", n), ["s%dA" % pr])
-            if n:
-                carry(n - 1, 0)
-            tt(T.sq[:, o + 2:o + L:3], keys, T.dk[:, 100 * pr + 4:100 * pr + 98:3], A.add, two("k", n) + two("z", n), ["s%dC" % pr])
-            copy("s", T.dl[:, 100 * pr + 3:100 * pr + 94:3], T.dk[:, 100 * pr + 4:100 * pr + 95:3], two("z", n), two("st", n), -1.0 / BIG)
-            if n:
-                moved(n - 1, "abcdef")
+                moved(n - 1, "be", "v")
+            else:
+                spare()
             hot(n)
-            if n:
-                carry(n - 1, 1)
+            kk = T.kb[:, o + 2:o + L:3]
+            tt(T.sq[:, o + 1:o + L:3], kk, T.yy[:, 33 * pr:33 * pr + 32], A.add, two("k", n) + two("y", n), ["s%dA" % pr])
+            tt(T.sq[:, o + 2:o + L:3], kk, T.dk[:, 100 * pr + 4:100 * pr + 98:3], A.add, two("k", n) + two("z", n), ["s%dC" % pr])
+            copy("s", T.dl[:, DL * pr + 3:DL * pr + 94:3], T.dk[:, 100 * pr + 4:100 * pr + 95:3], two("z", n), two("st", n), -1.0 / BIG)
+            if n == 0:
+                spare()
+            carry(n, 0)
+            edge(n)
+            moved(n, "f")
         n = V - 1
+        wb = W[:, 0:9 * XE]
+        moved(n - 1, "acd")
         gate(n, 0, "st")
-        latch(n - 1, [0, 1])
-        carry(n - 1, 0)
-        gate(n, 0, "z")
-        gate(n, 1, "z")
-        moved(n - 1, "a", "v")
-        moved(n - 1, "b", "s")
-        carry(n - 1, 1)
-        moved(n - 1, "cdef")
+        moved(n - 1, "b", "v")
+        tt(T.bx[:], T.lb[:, 0:L * n].indirect(T.lbx[:]), T.tc[:, 0:64], A.add,
+           [k % m for m in range(n) for k in ("l%d0", "l%d1")] + ["lbx", "lbx2", "tc"], ["bx"])
         gate(n, 1, "st")
-        hot(n)
         latch(n, [0])
-        edge(n)
-        tt(T.bx[:], T.lb[:, 0:L * n + 48].indirect(T.lbx[:]), T.tc[:, 0:64], A.add,
-           [k % m for m in range(V) for k in ("l%d0", "l%d1")][:-1] + ["lbx", "tc"], ["bx"])
-        latch(n, [1])
-        carry(n, 0)
+        moved(n - 1, "e", "v")
         tr(T.tb[0:32, 0:64], T.bx[0:32, :], ["bx"], ["tba"])
         tr(T.tb[32:64, 0:64], T.bx[0:32, :], ["bx"], ["tbb"])
-        carry(n, 1)
-        moved(n, "abcdef")
+        hot(n)
+        tr(T.tb[0:32, 72:104], T.lb[0:32, V * L:V * L + 32], ["l50"], ["tbc"])
+        tr(T.tb[32:64, 72:104], T.lb[0:32, V * L:V * L + 32], ["l50"], ["tbd"])
+        latch(n, [1])
         ts(T.offb[:], T.tb[:, 0:65].indirect(T.lbs[:, 0:1]), T.sc[:, 1:2], None, A.add, None,
            ["tba", "tbb", "tb64", "lbs", "lbs2", "sc1"], ["offb"])
-        wb = W[:, 0:9 * XE]
-        copy("s", T.bu[:], wb.indirect(T.offb[:, 8:16]), XW + WB + ["offb"], ["bu"], down)
-        copy("v", T.bt[:, 0:128], wb.indirect(T.offb[:, 0:8]), XW + WB + ["offb"], ["bt"], down)
-        scan(T.of[:, 1:L + 1], T.df[:], T.tn[:, L * V:L * V + L], 0.0, A.mult, A.subtract, tkeys(V) + ["df", "ofi"], ["o6"])
-        copy("v", T.bt[64:128, 0:128], T.bu[0:64, :], ["bu"], ["bt"])
+        edge(n)
+        ts(T.offc[:], T.tb[:, 0:104].indirect(T.lbl[:, 0:1]), T.sc[:, 1:2], None, A.add, None,
+           ["tba", "tbb", "tbc", "tbd", "tb64", "lbl", "lbl2", "sc1"], ["offc"])
+        carry(n, 0)
+        for e, k, dst in (("v", 0, T.bt), ("s", 1, T.bu)):
+            copy(e, dst[:, 0:128], wb.indirect(T.offb[:, 8 * k:8 * k + 8]), XW + WB + ["offb"], ["be%d" % k], down)
+        for e, k, dst in (("v", 0, T.bt), ("s", 1, T.bu)):
+            copy(e, dst[:, 128:192], wb.indirect(T.offc[:, 4 * k:4 * k + 4]), XW + WB + ["offc"], ["bl%d" % k], down)
+        moved(n, "bea", "v")
+        moved(n, "cdf")
+        carry(n, 1)
+        copy("v", T.bt[64:128, 0:192], T.bu[0:64, :], ["be1", "bl1"], ["be0", "bl0"])
+        o = L * TREG[V]
+        if t == 0:
+            spare()
+        scan(T.of[:, 1:L + 1], T.df[:], T.tn[:, o:o + L], 0.0, A.mult, A.subtract, tkeys(V) + ["df", "ofi"], ["o6"])
+        quant(T.qb[:], T.sb[:, 3 * KB:3 * KB + 128], T.bt[:], ["be0", "bl0", "btz"], ["qb"])
+        if t == 0:
+            spare()
         of = slice(0, L, 3)
         o6 = T.of[:, of]
-        for a in range(2):
+        for a in range(4):
             tr(T.t1[32 * a:32 * a + 32, :], T.of[32 * QUAD[a]:32 * QUAD[a] + 32, of], ["o6"], ["t1%d" % a])
-        quant(T.qb[:], T.sb[:, 128:256], T.bt[:], ["bt", "btz"], ["qb"])
         peer = T.cores[(rank + t + 1) % N]
         rid, pid = topo.addr(peer)[0:2]
         es = topo.engines(core, peer)
@@ -426,146 +543,214 @@ def rank_program(g, core, T, topo):
         order("g", ["qb"], [])
         g.remote_dma_fused([
             RemoteDMATransfer(dst_ids=[DstId(rid=rid, pnc=pid)], dma_engine_mask=masks[0], remote_sem=S[arr],
-                              src=T.qb[:, 0:32].bitcast(u8), dst=ql[:, 0:32].bitcast(u8)),
+                              src=T.qb[:, 0:KB].bitcast(u8), dst=ql[:, 0:KB].bitcast(u8)),
             RemoteDMATransfer(dst_ids=[DstId(rid=rid, pnc=pid)], dma_engine_mask=masks[1], remote_sem=S[arr],
-                              src=T.sb[:, 32:160], dst=sl[:, 0:128])], local_sem=S.sent)
+                              src=T.sb[:, 0:4 * KB], dst=sl[:, 0:4 * KB])], local_sem=S.sent)
         count["sent"] = count.get("sent", 0) + 2 * half
         note("g", ("sent", count["sent"]), ["qb"], [])
         count[arr] = 2 * (len(topo.engines(T.cores[(rank - t - 1) % N], core)) // 2)
         wr["land%d" % t] = (arr, count[arr])
 
-        if t == 0:
-            ts(T.blk[96:128, 176:192], T.blk[96:128, 176:192], -16.0, None, A.add, None, ["blk5"], ["blk5"])
-        for a in range(2, 4):
-            tr(T.t1[32 * a:32 * a + 32, :], T.of[32 * QUAD[a]:32 * QUAD[a] + 32, of], ["o6"], ["t1%d" % a])
-            if t == 0 and a == 2:
-                tr(T.col[:, 128:352], T.blk[:, 128:352],
-                   ["blk4", "blk5", "blk6", "blk6b", "blk7", "blk8", "blk9", "blk9b", "blk10"], ["colb"])
-        if t == 0:
-            ts(T.la1[:], T.pat[:, 10:26], colv(9), None, A.add, None, ["pat2", "colb"], ["la1"])
-            ts(T.la2[:], T.pat[:, 26:34], colv(5), 255.0, A.add, A.min, ["pat3", "colb"], ["la2"])
+        chunks = CL if last else CH
         tt(T.a2[:], T.t1[:].indirect(T.la1[:]), T.tc[:], A.add, ["t1%d" % a for a in range(4)] + ["la1", "tc"], ["a2"])
-        tr(T.t7[0:32, :], T.of[96:128, of], ["o6"], ["t70"])
-        tr(T.t7[32:64, :], T.of[96:128, of], ["o6"], ["t71"])
-        tr(T.t7[64:96, :], T.of[96:128, of], ["o6"], ["t72"])
+        if t == 0:
+            spare()
+        for a in range(4):
+            tr(T.t7[32 * a:32 * a + 32, :], T.of[96:128, of], ["o6"], ["t7%d" % a])
         tr(T.a3[:], T.a2[:], ["a2"], ["a3"])
-        tr(T.t7[96:128, :], T.of[96:128, of], ["o6"], ["t73"])
         if t == 0:
-            ts(T.ll1[:], T.pat[:, 34:38], colv(6), 0.0625, A.add, A.mult, ["pat4", "colb"], ["ll1"])
-            ts(T.ll2[:], T.pat[:, 26:28], colv(7), 63.0, A.add, A.min, ["pat3", "colb"], ["ll2"])
-        ts(T.offz[:], T.a3[:].indirect(T.la2[:]), T.sc[:, 0:1], None, A.add, None, ["a3", "la2", "sc0"], ["offz"])
-        wz = W[:, X0:X0 + 7 * XE]
-        ZA = ["z%d" % a for a in range(4)]
-
-        def early(e, c0, c1, key):
-            z0 = C * (c0 // 32) + 16 * (c0 % 32)
-            copy(e, T.zz[:, z0:z0 + 16 * (c1 - c0)], wz.indirect(T.offz[:, c0:c1]), XW + WZ + ["offz"], key, down)
-        for a in range(3):
-            early("s", 32 * a, 32 * a + 28, [ZA[a]])
+            spare()
         tt(T.l2[:], T.t7[:].indirect(T.ll1[:]), T.tc[:, 0:64], A.add, ["t7%d" % a for a in range(4)] + ["ll1", "tc"], ["l2"])
-        if t == 0:
-            for b in range(4):
-                quant(T.qg[:, 128 * b:128 * b + 128], T.sg[:, 128 * b:128 * b + 128], T.gt[:, 3 - b:515 - b], ["gt"], ["qg%d" % b])
-        if t > 0:
-            early("v", 96, 110, [ZA[3]])
-        else:
-            ts(T.oi[:, 0:32], T.oi[:, 0:32], colv(4), None, A.add, None, ["oi", "colb"], ["oi"])
-        tr(T.l3[:], T.l2[:], ["l2"], ["l3"])
-        if t == 0:
-            steps(T.oi, "oi", 7)
-        if t == 1:
-            quant(T.qv[:], T.sv[:], T.vs[:], ["vs"], ["qv"])
-            ts(T.sc[:, 2:3], colv(10), XE // 2 - 0.5, SC, A.add, A.mult, ["colb"], ["sc2"])
         if last:
+            ts(T.offz[:], T.a3[:].indirect(T.la3[:]), T.sc[:, 0:1], None, A.add, None, ["a3", "la3", "sc0"], ["offz"])
+        else:
+            ts(T.offz[:, 0:112], T.a3[:].indirect(T.la2[:, 0:7]), T.sc[:, 0:1], None, A.add, None, ["a3", "la2", "sc0"], ["offz"])
+        wz = W[:, X0:X0 + 7 * XE]
+        ZE = ["ze%d" % k for k in range(56)]
+        ZP = [["zp%d%d" % (c, a) for a in range(4)] for c in range(3)]
+
+        def early(e, c0, c1):
+            f0 = c0 // 56 * 16 if last else c0 // 4
+            copy(e, T.zz[:, 4 * c0:4 * c1], wz.indirect(T.offz[:, f0:f0 + (c1 - c0) // 4]), XW + WZ + ["offz"], ZE[c0 // 8:c1 // 8], down)
+
+        def numbers():
             ts(T.g1[:], o6, float(8 * XE - 1), 0.5 - XE // 2, A.min, A.add, ["o6"], ["g1"])
+            ts(T.g5[:], o6, 8.0, colv(8), A.mult, A.add, ["o6", "col"], ["g5"])
+            yield
+            ts(T.g2[:], T.g1[:], 1.0 / XE, WHOLE, A.mult, A.add, ["g1"], ["g2"])
+            ts(T.g4[:], T.g1[:], SC, T.sc[:, 5:6], A.mult, A.add, ["g1", "sc5"], ["g4"])
+            ts(T.g5[:], T.g5[:], T.sc[:, 9:10], None, A.min, None, ["g5", "sc9"], ["g5"])
+            yield
+            ts(T.g3[:], T.g2[:], -WHOLE, -56.0, A.add, A.mult, ["g2"], ["g3"])
+            ts(T.g7[:], T.g2[:], -WHOLE, float(C), A.add, A.mult, ["g2"], ["g7"])
+            yield
+            tt(T.g3[:], T.g3[:], T.g4[:], A.add, ["g3", "g4"], ["g3"])
+            yield
+            ts(T.g1[:], T.g3[:], T.sc[:, 6:7], None, A.min, None, ["g3", "sc6"], ["g1"])
+            ts(T.g2[:], T.g3[:], T.sc[:, 8:9], T.sc[:, 7:8], A.subtract, A.min, ["g3", "sc7", "sc8"], ["g2"])
+            ts(T.g4[:], T.g3[:], -30.0, None, A.add, None, ["g3"], ["g4"])
+            yield
+            tt(T.g1[:], T.g1[:], T.g2[:], A.max, ["g1", "g2"], ["g1"])
+            yield
+            tt(T.g1[:], T.g1[:], T.g4[:], A.max, ["g1", "g4"], ["g1"])
+            yield
+            tt(T.g1[:], T.g1[:], T.g7[:], A.add, ["g1", "g7"], ["g1"])
+            yield
+            tt(T.g6[:], T.g1[:], T.g5[:], A.max, ["g1", "g5"], ["g6"])
+            dmas("og", [("y", ["g6"], [], T.og[2 * a + h:2 * a + h + 1, :], T.g6[32 * QUAD[a]:32 * QUAD[a] + 32, 17 - 16 * h:31 - 16 * h])
+                        for a in range(4) for h in range(2)])
+            yield
+        if last:
+            todo[0] = numbers()
+        cuts = list(range(0, 337, 56)) if last else [0, 128, 336]
+        for c0, c1 in zip(cuts, cuts[1:]):
+            early("s", c0, c1)
+        tr(T.l3[:], T.l2[:], ["l2"], ["l3"])
+        spare(4 if t == 0 else 1)
+        early("v", 336, 392)
+        ts(T.offl[:], T.l3[:].indirect((T.ll3 if last else T.ll2)[:]), T.sc[:, 0:1], None, A.add, None, ["l3", "ll2", "ll3", "sc0"], ["offl"])
+        spare()
 
         for b in range(4):
-            mm(4 + b, 128, [(T.qg[:, 128 * b:128 * b + 128], T.sg[:, 128 * b:128 * b + 128], ql[:, 0:128], sl[:, 96:224])],
+            mm(4 + b, 128, [(T.qg[:, 128 * b:128 * b + 128], T.sg[:, 128 * b:128 * b + 128], ql[:, 0:128], sl[:, 3 * KB:3 * KB + 128])],
                ["qg%d" % b, "land%d" % t, "pad%d" % t])
         for b in range(4):
-            copy("v", T.dtl[:, 128 + b:256:4], bank(4 + b, 32), ["ps%d" % (4 + b)], ["d%d_" % b])
+            copy("v", T.dtl[:, 4 * KB + b:8 * KB:4], bank(4 + b, KB), ["ps%d" % (4 + b)], ["d%d_" % b])
+        spare()
         quant(T.qd[:], T.sd[:], T.dtl[:], ["d%d_" % b for b in range(4)] + ["dz0", "dz1"], ["qd"])
         for b in range(4):
             lo, hi = 16 + 128 * b, 128 * b
-            mm(b, 128, [(T.qw[:, lo:lo + 128], T.sw[:, lo:lo + 128], T.qd[:, 32:160], T.sd[:, 32:160]),
+            mm(b, 128, [(T.qw[:, lo:lo + 128], T.sw[:, lo:lo + 128], T.qd[:, KB:KB + 128], T.sd[:, KB:KB + 128]),
                         (T.qw[:, hi:hi + 128], T.sw[:, hi:hi + 128], T.qd[:, 0:128], T.sd[:, 0:128])], WK + ["qd"])
-        ts(T.offl[:], T.l3[:].indirect(T.ll2[:]), T.sc[:, 0:1], None, A.add, None, ["l3", "ll2", "sc0"], ["offl"])
-        if t == 0:
-            early("v", 96, 124, [ZA[3]])
-        else:
-            early("v", 110, 124, ["z3b"])
+        spare()
+        early("v", 392, C)
         for b in range(4):
-            copy("v", W[:, HB + b:HB + 256:4], bank(b, 64), ["ps%d" % b], ["h%d" % b], SC if t == 0 else None)
-        wl = W[:, X0:HB + 256]
+            if last:
+                spare()
+            copy("v", W[:, HB + b:HB + 8 * KB:4], bank(b, 2 * KB), ["ps%d" % b], ["h%d" % b], SC if t == 0 else None)
+        if last:
+            spare()
+        wl = W[:, X0:HB + 8 * KB]
         LR = XW + WZ + ["w7", "offl"] + ["h%d" % b for b in range(4)]
-        copy("s", T.lt[:, 224:448], wl.indirect(T.offl[:, 14:28]), LR, ["lt1"], down)
-        copy("v", T.lt[:, 0:224], wl.indirect(T.offl[:, 0:14]), LR, ["lt0"], down)
+        if t == 0:
+            XW[:] = XW0
+            for k in XW:
+                wr[k] = wr["h3"]
+                rd[k] = []
+            OLD = XJ
+        else:
+            OLD = []
 
-        def place(e, a):
-            copy(e, T.zz[96:128, C * a:C * a + C], T.lt[32 * a:32 * a + 32, :], ["lt0", "lt1"], [ZA[a]] + (["z3b"] if a == 3 else []))
+        def late(e, c):
+            c0, c1 = chunks[c]
+            f0 = 16 * c if last else c0 // 16
+            copy(e, T.lt[:, c0:c1], wl.indirect(T.offl[:, f0:f0 + (c1 - c0) // 16]), LR, ["lt%d" % c], down)
 
-        def layer(hf):
-            c0 = 224 * hf
-            quant(T.qz[:, c0:c0 + 224], T.sz[:, c0:c0 + 224], T.zz[:, 896 * hf:896 * hf + 896], ZA[2 * hf:2 * hf + 2], ["qz%d" % hf])
+        def place(e, c, a):
+            c0, c1 = chunks[c]
+            z0 = 4 * c0 + a * (c1 - c0)
+            copy(e, T.zz[96:128, z0:z0 + c1 - c0], T.lt[32 * a:32 * a + 32, c0:c1], ["lt%d" % c] + ZE[c0 // 8:c1 // 8], [ZP[c][a]])
+
+        def layer(c):
+            c0, c1 = chunks[c]
+            zk = ZE[c0 // 8:c1 // 8] + ZP[c]
+            quant(T.qz[:, c0:c1], T.sz[:, c0:c1], T.zz[:, 4 * c0:4 * c1], zk, ["qz%d" % c])
             for b in range(4):
                 lo = 16 + 128 * b
-                mm(4 * hf + b, 224, [(T.qw[:, lo:lo + 128], T.sw[:, lo:lo + 128], T.qz[:, c0:c0 + 224], T.sz[:, c0:c0 + 224])],
-                   WK + ["qz%d" % hf])
-        place("s", 3)
-        place("v", 0)
-        place("v", 1)
-        layer(0)
-        place("v", 2)
-        layer(1)
-        for hf in range(2):
+                mm(4 * (c % 2) + b, c1 - c0, [(T.qw[:, lo:lo + 128], T.sw[:, lo:lo + 128], T.qz[:, c0:c1], T.sz[:, c0:c1])],
+                   WK + ["qz%d" % c])
+
+        def times32(c):
+            c0, c1 = chunks[c]
+            copy("s", T.z32[:, 4 * c0:4 * c1], T.zz[:, 4 * c0:4 * c1], ZE[c0 // 8:c1 // 8] + ZP[c], ["z32%d" % c], 32.0)
+
+        def state(c):
+            c0, c1 = chunks[c]
+            order("v", [], OLD)
             for b in range(4):
-                z0 = 896 * hf + 224 * b
-                copy("s", T.z32[:, z0:z0 + 224], T.zz[:, 896 * hf + b:896 * hf + 896:4], ZA[2 * hf:2 * hf + 2], ["z32%d%d" % (hf, b)], 32.0)
-        if last:
-            do("s", ["g1", "sc2"], ["g4"], lambda: act.activation(T.g4[:], T.g1[:], AF.Identity, bias=T.sc[:, 2:3], scale=SC))
-            do("s", ["o6", "colb"], ["g5"], lambda: act.activation(T.g5[:], o6, AF.Identity, bias=colv(8), scale=8.0))
-        for hf in range(2):
-            for b in range(4):
-                z0 = 896 * hf + 224 * b
-                out = T.x32[:, 28 * hf:28 * hf + 28, b:32:4] if last else W[:, X0 + 896 * hf + b:X0 + 896 * hf + 896:4]
-                tt(out, bank(4 * hf + b, 224), T.z32[:, z0:z0 + 224], A.add, ["ps%d" % (4 * hf + b), "z32%d%d" % (hf, b)], [X32[hf][b]])
+                out = T.x32[:, c0 // 4:c1 // 4, b:16:4] if last else W[:, X0 + 4 * c0 + b:X0 + 4 * c1:4]
+                k = 4 * (c % 2) + b
+                tt(out, bank(k, c1 - c0), T.z32[:, 4 * c0 + b:4 * c1:4], A.add, ["ps%d" % k, "z32%d" % c],
+                   ["o%d%d" % (c, b)] if last else [XW[4 * c + b]])
+
+        def scaled(es, c):
+            c0, c1 = chunks[c]
+            for a, e in enumerate(es):
+                z0 = X0 + 4 * c0 + a * (c1 - c0)
+                copy(e, T.xk[:, c0 // 8:c1 // 8, 8 * a:8 * a + 8], W[:, z0:z0 + c1 - c0], XW[4 * c:4 * c + 4], ["xk%d%d" % (c, a)], SC)
+
+        def rekey(c):
+            c0, c1 = chunks[c]
+            keys(c, T.xk[:, c0 // 8:c1 // 8], ["xk%d%d" % (c, a) for a in range(4)])
+        late("v", 0)
+        late("s", 1)
         if not last:
-            windows(False)
+            late("s", 2)
             for a in range(4):
-                copy("s" if a < 2 else "v", T.xk[:, :, 8 * a:8 * a + 8], W[:, X0 + C * a:X0 + C * a + C], X32[a // 2], [XK[a]], SC)
-            keys_half(0, XK)
-            keys_half(1, XK)
+                place("v", 0, a)
+            for a in range(4):
+                place("v" if a < 2 else "s", 1, a)
+            for a in range(2):
+                place("v", 2, a)
+            times32(0)
+            layer(0)
+            for a in range(2, 4):
+                place("v", 2, a)
+            times32(1)
+            layer(1)
+            times32(2)
+            c0, c1 = chunks[2]
+            quant(T.qz[:, c0:c1], T.sz[:, c0:c1], T.zz[:, 4 * c0:4 * c1], ZE[c0 // 8:c1 // 8] + ZP[2], ["qz2"])
+            state(0)
+            for b in range(4):
+                lo = 16 + 128 * b
+                mm(b, c1 - c0, [(T.qw[:, lo:lo + 128], T.sw[:, lo:lo + 128], T.qz[:, c0:c1], T.sz[:, c0:c1])], WK + ["qz2"])
+            scaled("ssss", 0)
+            state(1)
+            scaled("ssss", 1)
+            state(2)
+            windows()
+            rekey(0)
+            scaled("vvvv", 2)
+            rekey(1)
+            rekey(2)
+            turn(0)
+            turn(1)
+            turn(2)
 
-    def unlay(hf, q, e):
-        copy("v" if hf else "s", T.xl[:, 4 * q + 2 * hf:4 * q + 2 * hf + 2, 56 * e:56 * e + 56],
-             T.x32[:, 28 * hf:28 * hf + 28, 8 * q + 4 * e:8 * q + 4 * e + 4], X32[hf], ["xl%d%d%d" % (hf, q, e)], SC)
-    for q in range(4):
-        for e in range(2):
-            unlay(0, q, e)
-    ts(T.g2[:], T.g1[:], 1.0 / XE, WHOLE, A.mult, A.add, ["g1"], ["g2"])
-    for k in range(2):
-        c0 = 224 * k
-        for q in (2 * k, 2 * k + 1):
-            for e in range(2):
-                unlay(1, q, e)
-        quant(T.qx[:, c0:c0 + 224], T.sx[:, c0:c0 + 224], T.xl[:, 8 * k:8 * k + 8, :],
-              ["xl%d%d%d" % (hf, q, e) for hf in range(2) for q in (2 * k, 2 * k + 1) for e in range(2)], ["qx%d" % k])
-        mm(k, 224, [(T.qv[:], T.sv[:], T.qx[:, c0:c0 + 224], T.sx[:, c0:c0 + 224])], ["qv", "qx%d" % k])
-        if k == 0:
-            ts(T.g3[:], T.g2[:], -WHOLE, float(C - 56), A.add, A.mult, ["g2"], ["g3"])
-    tt(T.g2[:], T.g3[:], T.g4[:], A.add, ["g3", "g4"], ["g2"])
-    tt(T.g6[:], T.g2[:], T.g5[:], A.max, ["g2", "g5"], ["g6"])
-    QX = ["qx0", "qx1"]
+    def unlay(e, c, j):
+        copy(e, T.xl[:, 2 * c + j // 2, :, j % 2, :], T.x32[:, 56 * c:56 * c + 56, 4 * j:4 * j + 4],
+             ["o%d%d" % (c, b) for b in range(4)], ["xl%d%d" % (c, j)], SC)
+
+    def result(c):
+        c0 = 224 * c
+        quant(T.qx[:, c0:c0 + 224], T.sx[:, c0:c0 + 224], T.xl[:, 2 * c:2 * c + 2], ["xl%d%d" % (c, j) for j in range(4)], ["qx0", "qx1", "qx2"][c:])
+        mm(4 * c, 224, [(T.qv[:], T.sv[:], T.qx[:, c0:c0 + 224], T.sx[:, c0:c0 + 224])], ["qv", "qx%d" % c])
+    for a in range(4):
+        place("v", 0, a)
+    place("s", 1, 3)
+    times32(0)
+    place("v", 1, 0)
+    layer(0)
+    place("v", 1, 1)
+    place("v", 1, 2)
+    times32(1)
+    layer(1)
+    state(0)
+    for j in range(4):
+        unlay("s", 0, j)
+    state(1)
+    result(0)
+    wr["qx1"] = wr["qx2"] = wr["xl00"]
+    for j in range(4):
+        unlay("v" if j < 3 else "s", 1, j)
     copy("s", T.ys[:, 0:224], bank(0, 224), ["ps0"], ["ys0"])
-    copy("v", T.ys[:, 224:448], bank(1, 224), ["ps1"], ["ys1"])
-
-    def og(e, a, h):
-        return (e, ["g6"], [], T.og[2 * a + h:2 * a + h + 1, :], T.g6[32 * QUAD[a]:32 * QUAD[a] + 32, 16 * h + 1:16 * h + 15])
+    result(1)
+    copy("v", T.ys[:, 224:448], bank(4, 224), ["ps4"], ["ys1"])
     dmas("out", [("y", ["qx0"], [], T.oc[:, 0:896], T.qx[:, 0:224].bitcast(u8)),
-                 ("y", ["qx1"], [], T.oc[:, 896:XE], T.qx[:, 224:C].bitcast(u8)),
-                 ("s", ["ys0"], [], T.y[:, 0:224], T.ys[:, 0:224])]
-         + [("y", QX, [], T.osc[4 * k:4 * k + 4, :], T.sx[32 * k:32 * k + 4, :]) for k in range(4)]
-         + [og("s", a, h) for a in range(3) for h in range(2)]
-         + [("y", ["ys1"], [], T.y[:, 224:C], T.ys[:, 224:C]), og("y", 3, 0), og("y", 3, 1)])
+                 ("s", ["ys0"], [], T.y[:, 0:224], T.ys[:, 0:224]),
+                 ("y", ["qx1"], [], T.oc[:, 896:XE], T.qx[:, 224:C].bitcast(u8))]
+         + [("s", ["qx0", "qx1"], [], T.osc[4 * k:4 * k + 4, :], T.sx[32 * k:32 * k + 4, :]) for k in range(4)]
+         + [("y", ["ys1"], [], T.y[:, 224:C], T.ys[:, 224:C])])
     for k in count:
         wait("y", (k, count[k]))

@@ -13,24 +13,25 @@ SC = 0.03125
 L = 96
 DL = 132
 QUAD = [0, 2, 1, 3]
-TREG = [0, 1, 2, 3, 4, 7, 5]
-KB = 48
+TREG = [0, 100, 200, 300, 400, 700, 500]
+T1, TAIL = 600, 700 + L
+KB = 24
 CD, BF, F, U8, U16 = "float8_e4m3fn_x4", "bfloat16", "float32", "uint8", "uint16"
 
 SCRATCH = {"ps": ("psum", [128, 4096], F)}
 for _n, _s, _d in [
         ("W", [HB + 384], BF), ("x3", [P, 4 * M], BF), ("xl", [4, 4, 2, 4 * M], BF), ("xk", [56, 32], BF), ("x32", [112, 16], BF),
-        ("zz", [XE], BF), ("z32", [XE], BF), ("lt", [C], BF), ("us", [4, 128], BF), ("vs", [512], BF), ("zt", [576], BF),
-        ("one", [516], BF), ("gt", [516], BF), ("bt", [512], BF), ("bu", [192], BF), ("dtl", [704], BF),
+        ("zz", [XE], BF), ("z32", [XE], BF), ("lt", [C], BF), ("us", [4, 128], BF), ("vs", [512], BF), ("zt", [512], BF),
+        ("one", [516], BF), ("gt", [516], BF), ("bt", [576], BF), ("bu", [128], BF), ("bl", [128], BF), ("dtl", [608], BF),
         ("qx", [C], CD), ("sx", [C], U8), ("qz", [C], CD), ("sz", [C], U8), ("qu", [128], CD), ("su", [128], U8),
         ("qv", [128], CD), ("sv", [128], U8), ("qw", [528], CD), ("sw", [528], U8), ("qg", [512], CD), ("sg", [512], U8),
-        ("qb", [128], CD), ("sb", [272], U8), ("qn", [144], CD), ("qd", [176], CD), ("sd", [176], U8),
-        ("ql0", [176], CD), ("sl0", [320], U8), ("ql1", [176], CD), ("sl1", [320], U8), ("ql2", [176], CD), ("sl2", [320], U8),
+        ("qb", [128], CD), ("sb", [256], U8), ("qn", [128], CD), ("qd", [152], CD), ("sd", [152], U8),
+        ("ql0", [152], CD), ("sl0", [224], U8), ("ql1", [152], CD), ("sl1", [224], U8), ("ql2", [152], CD), ("sl2", [224], U8),
         ("kt", [C], F), ("ys", [C], F), ("rb", [2 * L], F), ("kb", [2 * L], F), ("sq", [2 * L], F), ("yy", [66], F),
         ("dk", [200], F), ("dl", [2 * DL], F), ("dr", [L], F), ("df", [L], F), ("ff", [33], F), ("gg", [64], F), ("uu", [32], F),
-        ("tn", [8 * L + 32], F), ("lb", [V * L + 32], F), ("of", [L + 1], F), ("wt", [V], F),
+        ("tn", [TAIL + 32], F), ("dd", [L], F), ("lb", [V * L + 32], F), ("of", [L + 1], F), ("wt", [V], F),
         ("blk", [512], F), ("col", [512], F), ("stg", [7, 2, 16], F), ("stc", [224], F), ("g7", [32], F), ("g8", [32], F),
-        ("pat", [64], F), ("sc", [10], F), ("tc", [256], F), ("bx", [64], F), ("tb", [104], F), ("t1", [32], F), ("t7", [32], F),
+        ("pat", [64], F), ("sc", [12], F), ("tq", [64], F), ("tc", [256], F), ("bx", [64], F), ("tb", [104], F), ("t1", [64], F),
         ("a2", [256], F), ("a3", [256], F), ("l2", [64], F), ("l3", [64], F),
         ("g1", [32], F), ("g2", [32], F), ("g3", [32], F), ("g4", [32], F), ("g5", [32], F), ("g6", [32], F),
         ("lbx", [4], U16), ("lbs", [2], U16), ("lbl", [2], U16), ("la1", [16], U16), ("la2", [8], U16), ("la3", [8], U16),
@@ -176,20 +177,20 @@ def rank_program(g, core, T, topo):
         return T.blk[:, 32 * k + a:32 * k + b]
     w0 = 9 * XE + 4 * KB
     BK = ["blk%d" % k for k in range(19)]
-    iota(blk(0), [[32, 4], [2 * XE, 4], [-4 * KB, 2]], w0, 0, BK[0])
+    iota(blk(0), [[16, 4], [2 * XE, 4], [-4 * KB, 2]], w0, 0, BK[0])
     iota(blk(1), [[0, 2], [1, 4], [0, 4]], 0, 0, BK[1])
-    iota(blk(2, 0, 16), [[64, 2], [128, 4], [512, 2]], 0, 1, BK[2])
-    iota(blk(2, 16, 32), [[64, 2], [128, 4], [512, 2]], 16, 1, BK[16])
+    iota(blk(2, 0, 16), [[64, 2], [-512, 2], [128, 4]], 512, 1, BK[2])
+    iota(blk(2, 16, 32), [[64, 2], [-512, 2], [128, 4]], 528, 1, BK[16])
     iota(blk(3), [[16, 2], [0, 16]], 0, 1, BK[3])
     iota(blk(4), [[0, 4], [64, 2], [128, 4]], 0, 0, BK[4])
-    iota(blk(5), [[16, 4], [2 * XE, 4], [-4 * KB, 2]], w0 + 128, 0, BK[5])
+    iota(blk(5), [[4, 4], [2 * XE, 4], [-4 * KB, 2]], w0, 0, BK[5])
     iota(T.pat[:, 0:16], [[4, 8], [0, 2]], 0, 0, "pat0")
 
     def more():
         iota(blk(6, 0, 16), [[128, 2], [16, 2], [0, 4]], 0, 1, BK[6])
         iota(blk(6, 16, 32), [[128, 2], [16, 2], [0, 4]], 0, 1, BK[17])
         iota(blk(7), [[-16, 2], [1, 8], [32, 2]], 17, 0, BK[7])
-        iota(blk(8), [[8 - 256, 4], [2 - 16 * XE, 4], [1 + 32 * KB, 2]], 8 * C - 8 * w0, 0, BK[8])
+        iota(blk(8), [[8 - 128, 4], [2 - 16 * XE, 4], [1 + 32 * KB, 2]], 8 * C - 8 * w0, 0, BK[8])
         iota(blk(9, 0, 16), [[8, 2], [1, 2], [0, 4]], 0, 0, BK[9])
         iota(blk(9, 16, 32), [[8, 2], [1, 2], [0, 4]], 0, 0, BK[18])
         iota(blk(10), [[1, 32]], 0, 0, BK[10])
@@ -200,14 +201,16 @@ def rank_program(g, core, T, topo):
         iota(blk(15), [[8, 4], [128, 4], [4, 2]], 0, 0, BK[15])
         iota(T.pat[:, 16:32], [[2, 4], [16, 2], [0, 2]], 0, 0, "pat1")
         iota(T.pat[:, 32:40], [[32, 2], [64, 4]], 0, 0, "pat2")
-        for h, lo in ((0, 0), (1, 0), (1, 96)):
-            if lo:
-                alone()
-                iota(T.blk[96:128, 400:416], [[1, 16]], 17, 0, BK[12])
-            for c0, c1 in CH:
-                k0 = c0 // 64
-                iota(T.stg[lo:128, k0:c1 // 64, h, :], [[64, 4], [1, (c1 - c0) // 32], [32, 2]], (1 if h and not lo else 17) + c0 // 32, 0,
-                     "stg%d%d" % (h, k0))
+        for c0, c1 in CH:
+            iota(T.stg[:, c0 // 64:c1 // 64, 0, :], [[64, 4], [1, (c1 - c0) // 32], [32, 2]], 17 + c0 // 32, 0, "stg%d" % c0)
+
+    def rest():
+        sk = ["stg%d" % c0 for c0, c1 in CH]
+        do("s", sk, ["stga"], lambda: act.activation(T.stg[0:96, :, 1, :], T.stg[0:96, :, 0, :], AF.Identity, bias=-16.0))
+        copy("s", T.stg[96:128, :, 1, :], T.stg[96:128, :, 0, :], sk, ["stgb"])
+        copy("s", T.blk[96:128, 400:416], T.blk[96:128, 384:400], [BK[12]], [BK[12]])
+        put(T.dtl[:, 0:4 * KB], 4 * KB, 0.0, "dz0")
+        put(T.dtl[:, 8 * KB:608], 608 - 8 * KB, 0.0, "dz1")
     T0 = ["t0"] + ["t0%d%d" % (a, k) for a in range(4) for k in range(2)]
 
     def put(ap, n, val, key, after=()):
@@ -218,15 +221,13 @@ def rank_program(g, core, T, topo):
     fill(T.dl[:], 1.0, "dl")
     fill(T.dr[:], 0.0, "dr")
     fill(T.df[:], 1.0, "df")
-    fill(T.tn[:, 8 * L:8 * L + 32], 1.0, "tail")
+    fill(T.tn[:, TAIL:TAIL + 32], 0.0, "tail")
+    fill(T.dd[:], 1.0, "dd")
     fill(T.rb[:, 0:L], -BIG, "r0")
     fill(T.kb[:, 0:L], -BIG, "k0")
     fill(T.yy[:], 0.0, "yi")
     fill(T.sq[96:128, :], -BIG, "si")
     fill(T.one[:], 1.0, "one")
-    quant(T.qn[:], T.sb[:, 0:3 * KB], T.zt[:], ["zt"], ["qb"])
-    for t in range(R):
-        quant(T["ql%d" % t][:, KB:KB + 128], T["sl%d" % t][:, 4 * KB:4 * KB + 128], T.zt[:, 0:512], ["zt"], ["pad%d" % t])
     for k in range(2):
         put(T.tn[:, 48 * k + 3:48 * k + 42:3], 13, -128.0, "t0" if k else "t0y", ["t0z"])
     put(T.ff[:], 33, 0.0, "f")
@@ -239,11 +240,12 @@ def rank_program(g, core, T, topo):
             put(T.dl[:, DL * k + c:DL * k + L:48], 2, -1.0, "dm%d%d" % (k, c))
     put(T.dr[:, 0:L:48], 2, -BIG, "dr")
     put(T.df[:, 0:L:48], 2, 0.0, "df")
-    put(T.tn[:, 6 * L:7 * L], L, 0.0, "pz")
-    put(T.tn[:, 8 * L + 4:8 * L + 32:4], 7, -3.0, "tail3", ["tail"])
+    put(T.tn[:, T1:T1 + L], L, 0.0, "pz")
+    put(T.dd[:, 0:L:3], 32, 0.0, "dd")
+    put(T.tn[:, TAIL + 4:TAIL + 32:4], 7, 1.0, "tail")
     for k in range(2):
-        put(T.tn[:, 6 * L + 48 * k + 3:6 * L + 48 * k + 42:3], 13, -32.0, "py%d" % k, ["pz"])
-    put(T.tn[:, 8 * L:8 * L + 1], 1, 0.0, "tail")
+        put(T.tn[:, T1 + 48 * k + 3:T1 + 48 * k + 42:3], 13, -32.0, "py%d" % k, ["pz"])
+    put(T.tn[:, TAIL + 16:TAIL + 17], 1, -3.0, "tail")
     wr["dk"] = wr["dl"] = wr["tail"]
     order("g", ["t0z"], [])
     for a in range(4):
@@ -254,9 +256,10 @@ def rank_program(g, core, T, topo):
         iota(T.tn[q0:q0 + 32, 42:L:48], [[-XE, 2]], (2 * a + 1) * XE + 128 * (M - 1), 4, T0[2 + 2 * a])
     alone()
     iota(T.tc[:], [[0, 64], [1, 4]], 0, 0, "tc")
-    iota(T.bt[:, 4 * KB:512], [[0, 512 - 4 * KB]], 0, 0, "btz")
+    iota(T.tq[:, 0:32], [[0, 8], [1, 4]], 0, 0, "tq0")
+    iota(T.tq[:, 32:64], [[0, 2], [1, 4], [0, 4]], 0, 0, "tq1")
+    iota(T.bt[:, 160:576], [[0, 416]], 0, 0, "btz")
     more()
-    alone()
     do("g", ["one"], ["gt"], lambda: g.affine_select(T.gt[:], T.one[:], [[1, 516]], A.is_equal, 0.0, -3, -4))
     for k in range(2):
         for h in range(2):
@@ -268,17 +271,19 @@ def rank_program(g, core, T, topo):
     def colv(k):
         return T.col[:, 32 * k:32 * k + 1]
 
+    def pad(t):
+        quant(T["ql%d" % t][:, KB:KB + 128], T["sl%d" % t][:, 4 * KB:4 * KB + 128], T.zt[:, 0:512], ["zt"], ["pad%d" % t])
+
     def lists():
         fill(T.lbs[64:128, 0:1], 64, "lbs2")
         fill(T.lbl[64:128, 0:1], 64, "lbl2")
         fill(T.lbx[:, 2:4], 4 * L + 93, "lbx2")
-        fill(T.dtl[:, 0:4 * KB], 0.0, "dz0")
-        fill(T.dtl[:, 8 * KB:704], 0.0, "dz1")
+        quant(T.qn[:], T.sb[:, 0:128], T.zt[:], ["zt"], ["qb"])
         yield
         tr(T.col[:, 0:192], T.blk[:, 0:192], BK[0:6] + BK[16:17], ["cola"])
         yield
-        ts(T.wt[96:128, 0:5], T.pat[96:128, 0:10:2], T.col[96:128, 0:1], None, A.add, None, ["pat0", "cola"], ["wt"])
-        copy("v", T.wt[96:128, 5:6], T.col[96:128, 160:161], ["cola"], ["wt5"])
+        ts(T.wt[96:128, 0:4], T.pat[96:128, 0:8:2], T.col[96:128, 0:1], None, A.add, None, ["pat0", "cola"], ["wt"])
+        ts(T.wt[96:128, 4:6], T.pat[96:128, 8:12:2], 4.0, T.col[96:128, 160:161], A.mult, A.add, ["pat0", "cola"], ["wt5"])
         ts(T.sc[:, 2:3], colv(1), float(L), 93.0, A.mult, A.add, ["cola"], ["sc2"])
         ts(T.sc[0:64, 3:4], T.col[0:64, 96:97], T.col[0:64, 128:129], None, A.add, None, ["cola"], ["sc3"])
         yield
@@ -297,18 +302,20 @@ def rank_program(g, core, T, topo):
         ts(T.ll1[:], T.pat[:, 0:4], 64.0, colv(6), A.mult, A.add, ["pat0", "col"], ["ll1"])
         ts(T.ll2[:], T.pat[:, 0:4:2], 2.0, colv(7), A.mult, A.add, ["pat0", "col"], ["ll2"])
         yield
-        tr(T.stc[:], T.stg[:], ["stg%d%d" % (h, c0 // 64) for h in range(2) for c0, c1 in CH], ["stc"])
+        tr(T.stc[:], T.stg[:], ["stga", "stgb"], ["stc"])
         yield
-        ts(T.ll1[:], T.ll1[:], 0.0625, None, A.mult, None, ["ll1"], ["ll1"])
+        ts(T.ll1[96:128, :], T.ll1[96:128, :], 0.0625, None, A.mult, None, ["ll1"], ["ll1b"])
+        ts(T.ll1[0:96, :], T.ll1[0:96, :], 0.0625, 32.0, A.mult, A.add, ["ll1"], ["ll1a"])
         ts(T.ll2[:], T.ll2[:], 63.0, None, A.min, None, ["ll2"], ["ll2"])
         copy("v", T.la2[:, 0:7], T.stc[:, 0:224:32], ["stc"], ["la2"])
         yield
         for b in range(4):
             quant(T.qg[:, 128 * b:128 * b + 128], T.sg[:, 128 * b:128 * b + 128], T.gt[:, 3 - b:515 - b], ["gt"], ["qg%d" % b])
             yield
+        yield
         tr(T.col[:, 352:512], T.blk[:, 352:512], BK[11:16], ["colc"])
         yield
-        o = 6 * L
+        o = T1
         ts(T.tn[:, o:o + L:48], T.tn[:, 0:L:48], colv(14), None, A.subtract, None, T0 + ["colc", "pz"], ["pa"])
         ts(T.tn[:, o + 42:o + L:48], T.tn[:, 42:L:48], colv(14), -288.0, A.add, A.add, T0 + ["colc", "pz"], ["pb"])
         ts(T.sc[:, 4:5], colv(13), 32.0, None, A.mult, None, ["colc"], ["sc4"])
@@ -316,19 +323,24 @@ def rank_program(g, core, T, topo):
         ts(T.tn[:, o + 12:o + L:48], T.tn[:, o + 13:o + L:48], T.sc[:, 4:5], -416.0, A.subtract, A.add, ["sc4", "py0", "py1"], ["pc"])
         ts(T.tn[:, o + 30:o + L:48], T.tn[:, o + 31:o + L:48], T.sc[:, 4:5], -608.0, A.add, A.add, ["sc4", "py0", "py1"], ["pd"])
         yield
-        quant(T.qv[:], T.sv[:], T.vs[:], ["vs"], ["qv"])
-        yield
         ts(T.la3[:], T.pat[:, 32:40], colv(12), 255.0, A.add, A.min, ["pat2", "colc"], ["la3"])
         ts(T.ll3[:], T.pat[:, 0:4:2], 8.0, colv(11), A.mult, A.add, ["pat0", "colc"], ["ll3"])
+        yield
         ts(T.sc[:, 5:6], colv(10), float(32 * M), colv(15), A.mult, A.subtract, ["col", "colc"], ["sc5"])
         ts(T.sc[:, 6:7], colv(10), float(M), 3.0, A.mult, A.add, ["col"], ["sc6"])
         yield
+        quant(T.qv[:], T.sv[:], T.vs[:], ["vs"], ["qv"])
+        yield
         ts(T.ll3[:], T.ll3[:], 63.0, None, A.min, None, ["ll3"], ["ll3"])
         ts(T.sc[:, 5:6], T.sc[:, 5:6], XE // 2 - 0.5, SC, A.add, A.mult, ["sc5"], ["sc5"])
+        yield
         ts(T.sc[:, 7:8], colv(10), float(M), 9.0, A.mult, A.add, ["col"], ["sc7"])
         ts(T.sc[:, 8:9], colv(13), 12.0, None, A.add, None, ["colc"], ["sc8"])
         yield
-        ts(T.sc[:, 9:10], colv(10), float(8 * C + 5 * P), None, A.add, None, ["col"], ["sc9"])
+        ts(T.sc[:, 9:10], colv(5), -2.0, colv(10), A.mult, A.add, ["col", "cola"], ["sc9"])
+        ts(T.sc[:, 10:11], colv(10), float(8 * C + 4 * P), None, A.add, None, ["col"], ["sc10"])
+        yield
+        ts(T.sc[:, 9:10], T.sc[:, 9:10], float(8 * C), None, A.add, None, ["sc9"], ["sc9"])
         yield
     todo = [lists()]
 
@@ -339,9 +351,11 @@ def rank_program(g, core, T, topo):
     def keys(c, src, reads):
         c0, c1 = CH[c]
         quant(T.qx[:, c0:c1], T.sx[:, c0:c1], src, reads, ["qx%d" % c])
-        if "qu" not in wr:
-            spare()
-            quant(T.qu[:], T.su[:], T.us[:], ["us0", "us1"], ["qu"])
+        if "qu" in wr:
+            score(c)
+
+    def score(c):
+        c0, c1 = CH[c]
         mm(4 + c, c1 - c0, [(T.qu[:], T.su[:], T.qx[:, c0:c1], T.sx[:, c0:c1])], ["qu", "qx%d" % c])
 
     def turn(c):
@@ -356,9 +370,9 @@ def rank_program(g, core, T, topo):
     def first(c):
         c0, c1 = CH[c]
         keys(c, W[:, X0 + 4 * c0:X0 + 4 * c1], XJ[c0 // 32:c1 // 32])
-    for j in (8, 9, 10, 11, 12, 13):
+    for j in range(9, M):
         lay("s", j)
-    for j in range(8):
+    for j in range(9):
         lay("v", j)
     XW0, XW[:] = list(XW), XJ
     windows()
@@ -369,8 +383,11 @@ def rank_program(g, core, T, topo):
     dmas("lv", [("y", [], ["vs"], T.vs[:], T.v[:])])
     first(0)
     first(1)
+    quant(T.qu[:], T.su[:], T.us[:], ["us0", "us1"], ["qu"])
+    score(0)
+    score(1)
     first(2)
-    spare()
+    spare(2)
     turn(0)
     turn(1)
     turn(2)
@@ -380,7 +397,7 @@ def rank_program(g, core, T, topo):
         last = t == R - 1
         down = None if t == 0 else SC
         KT = ["kt0", "kt1", "kt2"]
-        treg = [6 if t else 0] + TREG[1:]
+        treg = [T1 if t else 0] + TREG[1:]
 
         def two(k, n):
             return ["%s%d%d" % (k, n % 2, h) for h in range(2)]
@@ -407,7 +424,7 @@ def rank_program(g, core, T, topo):
 
         def latch(n, hs):
             a, b = (0, L) if len(hs) == 2 else (0, 48) if hs[0] else (48, L + 32)
-            o, d = L * treg[n], DL * (n % 2)
+            o, d = treg[n], DL * (n % 2)
             skip = "" if len(hs) == 2 else "ab" if hs[0] else "cdef"
             scan(T.lb[:, L * n + a:L * n + b], T.dl[:, d + a:d + b], T.tn[:, o + a:o + b], 0.0, A.mult, A.add,
                  ["st%d%d" % (n % 2, h) for h in hs] + [k for k in tkeys(n) if k[-1] not in skip] + ["tail"],
@@ -424,18 +441,15 @@ def rank_program(g, core, T, topo):
         def edge(n):
             tt(T.gg[:, 32 * (n % 2):32 * (n % 2) + 32], T.ff[:, 0:32], T.ff[:, 1:33], A.subtract, ["f"], ["g%d_" % (n % 2)])
 
-        def carry(n, part):
-            o, o1 = L * treg[n], L * treg[n + 1]
-            if part == 0:
-                if n:
-                    tt(T.uu[:], T.tn[:, o + 1:o + L:3], T.tn[:, o + 2:o + L:3], A.add, tkeys(n)[1:], ["u"])
-            elif n:
-                tt(T.tn[:, o1:o1 + L:3], T.tn[:, o:o + L:3], T.uu[:], A.add, tkeys(n)[0:1] + ["u"], ["t%d" % (n + 1)])
+        def carry(n):
+            o, o1 = treg[n], treg[n + 1]
+            if n:
+                scan(T.tn[:, o1 - 2:o1 + L - 2], T.dd[:], T.tn[:, o:o + L], 0.0, A.mult, A.add, tkeys(n) + ["dd"], tkeys(n + 1))
             elif t < 2:
                 copy("v", T.tn[:, o1:o1 + L:3], T.tn[:, o:o + L:3], tkeys(0), ["t1"])
 
         def moved(n, which, e="s"):
-            o1, l0, g0 = L * TREG[n + 1], L * n, 32 * (n % 2)
+            o1, l0, g0 = TREG[n + 1], L * n, 32 * (n % 2)
             jobs = {"a": (0, 1, 0, 128, T.lb[:, l0 + 45:l0 + 46], 1), "b": (0, 2, 0, 128, T.lb[:, l0 + 94:l0 + 95], 0),
                     "c": (1, 1, 0, 64, T.lb[64:128, l0 + 93:l0 + 94], 0), "d": (1, 1, 64, 96, T.lb[32:64, l0 + 93:l0 + 94], 0),
                     "e": (1, 2, 0, 128, T.lb[:, l0 + 46:l0 + 47], 1), "f": (1, 1, 96, 128, T.wt[96:128, n:n + 1], None)}
@@ -443,7 +457,7 @@ def rank_program(g, core, T, topo):
                 h, slot, lo, hi, col, src = jobs[k]
                 a = o1 + 48 * (1 - h)
                 copy(e, T.tn[lo:hi, a + slot:a + 48:3], T.gg[lo:hi, g0 + 16 - 16 * h:g0 + 32 - 16 * h],
-                     ["g%d_" % (n % 2), ("wt5" if n == 5 else "wt") if src is None else "l%d%d" % (n, src)], ["t%d%s" % (n + 1, k)], col)
+                     ["g%d_" % (n % 2), ("wt5" if n > 3 else "wt") if src is None else "l%d%d" % (n, src)], ["t%d%s" % (n + 1, k)], col)
 
         def enter(n):
             o, y0 = L * (n % 2), 33 * (n % 2) + 17
@@ -462,14 +476,16 @@ def rank_program(g, core, T, topo):
                     scan(run(T.rb, 0, h, 5, 45, 3), T.dr[:, 1:15], T.kt[:, 16 * h:C:32], -BIG, A.add, A.max, KT + ["dr"], ["r0%d" % h])
                 for h in range(2):
                     copy("s", run(T.kb, 0, h, 5, 45, 3), T.kt[:, 16 * h:C:32], KT, ["k0%d" % h])
-                spare()
+                if t:
+                    pad(t)
+                else:
+                    spare()
             else:
                 scan(T.rb[:, o:o + L], T.dr[:], T.sq[:, oq:oq + L], -BIG, A.add, A.max, SK + ["dr"], two("r", n))
                 latch(n - 1, [0, 1])
                 if n < V - 1:
                     scan(T.kb[:, o:o + L], T.dk[:, 100 * (1 - pr):100 * (1 - pr) + L], T.sq[:, oq:oq + L], -BIG, A.add, A.max,
                          SK + two("z", n - 1), two("k", n))
-                carry(n - 1, 1)
             if n == V - 1:
                 break
             if n:
@@ -490,7 +506,7 @@ def rank_program(g, core, T, topo):
             copy("s", T.dl[:, DL * pr + 3:DL * pr + 94:3], T.dk[:, 100 * pr + 4:100 * pr + 95:3], two("z", n), two("st", n), -1.0 / BIG)
             if n == 0:
                 spare()
-            carry(n, 0)
+            carry(n)
             edge(n)
             moved(n, "f")
         n = V - 1
@@ -498,8 +514,8 @@ def rank_program(g, core, T, topo):
         moved(n - 1, "acd")
         gate(n, 0, "st")
         moved(n - 1, "b", "v")
-        tt(T.bx[:], T.lb[:, 0:L * n].indirect(T.lbx[:]), T.tc[:, 0:64], A.add,
-           [k % m for m in range(n) for k in ("l%d0", "l%d1")] + ["lbx", "lbx2", "tc"], ["bx"])
+        tt(T.bx[:], T.lb[:, 0:L * n].indirect(T.lbx[:]), T.tq[:], A.add,
+           [k % m for m in range(n) for k in ("l%d0", "l%d1")] + ["lbx", "lbx2", "tq0", "tq1"], ["bx"])
         gate(n, 1, "st")
         latch(n, [0])
         moved(n - 1, "e", "v")
@@ -514,26 +530,31 @@ def rank_program(g, core, T, topo):
         edge(n)
         ts(T.offc[:], T.tb[:, 0:104].indirect(T.lbl[:, 0:1]), T.sc[:, 1:2], None, A.add, None,
            ["tba", "tbb", "tbc", "tbd", "tb64", "lbl", "lbl2", "sc1"], ["offc"])
-        carry(n, 0)
+        carry(n)
         for e, k, dst in (("v", 0, T.bt), ("s", 1, T.bu)):
-            copy(e, dst[:, 0:128], wb.indirect(T.offb[:, 8 * k:8 * k + 8]), XW + WB + ["offb"], ["be%d" % k], down)
-        for e, k, dst in (("v", 0, T.bt), ("s", 1, T.bu)):
-            copy(e, dst[:, 128:192], wb.indirect(T.offc[:, 4 * k:4 * k + 4]), XW + WB + ["offc"], ["bl%d" % k], down)
+            copy(e, dst[:, 0:128], wb.indirect(T.offb[:, 8 * k:8 * k + 8]), XW + WB + ["offb"], ["be%d" % k] + ["bh"][k:], down)
+        for e, k in (("v", 0), ("s", 1)):
+            copy(e, T.bl[:, 64 * k:64 * k + 64], wb.indirect(T.offc[:, 4 * k:4 * k + 4]), XW + WB + ["offc"], ["bl%d" % k], down)
         moved(n, "bea", "v")
         moved(n, "cdf")
-        carry(n, 1)
-        copy("v", T.bt[64:128, 0:192], T.bu[0:64, :], ["be1", "bl1"], ["be0", "bl0"])
-        o = L * TREG[V]
+        copy("s", T.bt[64:128, 64:128], T.bu[0:64, 64:128], ["be1"], ["bh"])
+        copy("s", T.bt[64:128, 128:144], T.bu[0:64, 0:64:4], ["be1"], ["b41"])
+        copy("v", T.bt[0:64, 128:144], T.bt[0:64, 0:64:4], ["be0"], ["b40"])
+        for k in range(2):
+            copy("v", T.bt[64 * k:64 * k + 64, 144:160], T.bl[0:64, 64 * k:64 * k + 64:4], ["bl%d" % k], ["b5%d" % k])
         if t == 0:
-            spare()
+            rest()
+        o = TREG[V]
         scan(T.of[:, 1:L + 1], T.df[:], T.tn[:, o:o + L], 0.0, A.mult, A.subtract, tkeys(V) + ["df", "ofi"], ["o6"])
-        quant(T.qb[:], T.sb[:, 3 * KB:3 * KB + 128], T.bt[:], ["be0", "bl0", "btz"], ["qb"])
+        quant(T.qb[:], T.sb[:, 128:256], T.bt[:, 64:576], ["be0", "bh", "b40", "b41", "b50", "b51", "btz"], ["qb"])
         if t == 0:
             spare()
         of = slice(0, L, 3)
         o6 = T.of[:, of]
         for a in range(4):
-            tr(T.t1[32 * a:32 * a + 32, :], T.of[32 * QUAD[a]:32 * QUAD[a] + 32, of], ["o6"], ["t1%d" % a])
+            tr(T.t1[32 * a:32 * a + 32, 0:32], T.of[32 * QUAD[a]:32 * QUAD[a] + 32, of], ["o6"], ["t1%d" % a])
+        if t == 0:
+            spare()
         peer = T.cores[(rank + t + 1) % N]
         rid, pid = topo.addr(peer)[0:2]
         es = topo.engines(core, peer)
@@ -545,22 +566,23 @@ def rank_program(g, core, T, topo):
             RemoteDMATransfer(dst_ids=[DstId(rid=rid, pnc=pid)], dma_engine_mask=masks[0], remote_sem=S[arr],
                               src=T.qb[:, 0:KB].bitcast(u8), dst=ql[:, 0:KB].bitcast(u8)),
             RemoteDMATransfer(dst_ids=[DstId(rid=rid, pnc=pid)], dma_engine_mask=masks[1], remote_sem=S[arr],
-                              src=T.sb[:, 0:4 * KB], dst=sl[:, 0:4 * KB])], local_sem=S.sent)
+                              src=T.sb[:, 128 - 3 * KB:128 + KB], dst=sl[:, 0:4 * KB])], local_sem=S.sent)
         count["sent"] = count.get("sent", 0) + 2 * half
         note("g", ("sent", count["sent"]), ["qb"], [])
         count[arr] = 2 * (len(topo.engines(T.cores[(rank - t - 1) % N], core)) // 2)
         wr["land%d" % t] = (arr, count[arr])
 
         chunks = CL if last else CH
-        tt(T.a2[:], T.t1[:].indirect(T.la1[:]), T.tc[:], A.add, ["t1%d" % a for a in range(4)] + ["la1", "tc"], ["a2"])
+        tt(T.a2[:], T.t1[:, 0:32].indirect(T.la1[:]), T.tc[:], A.add, ["t1%d" % a for a in range(4)] + ["la1", "tc"], ["a2"])
         if t == 0:
             spare()
-        for a in range(4):
-            tr(T.t7[32 * a:32 * a + 32, :], T.of[96:128, of], ["o6"], ["t7%d" % a])
+        for a in range(3):
+            tr(T.t1[32 * a:32 * a + 32, 32:64], T.of[96:128, of], ["o6"], ["t7%d" % a])
         tr(T.a3[:], T.a2[:], ["a2"], ["a3"])
         if t == 0:
             spare()
-        tt(T.l2[:], T.t7[:].indirect(T.ll1[:]), T.tc[:, 0:64], A.add, ["t7%d" % a for a in range(4)] + ["ll1", "tc"], ["l2"])
+        tt(T.l2[:], T.t1[:].indirect(T.ll1[:]), T.tc[:, 0:64], A.add,
+           ["t1%d" % a for a in range(4)] + ["t7%d" % a for a in range(3)] + ["ll1a", "ll1b", "tc"], ["l2"])
         if last:
             ts(T.offz[:], T.a3[:].indirect(T.la3[:]), T.sc[:, 0:1], None, A.add, None, ["a3", "la3", "sc0"], ["offz"])
         else:
@@ -570,21 +592,23 @@ def rank_program(g, core, T, topo):
         ZP = [["zp%d%d" % (c, a) for a in range(4)] for c in range(3)]
 
         def early(e, c0, c1):
-            f0 = c0 // 56 * 16 if last else c0 // 4
+            f0 = c0 // 56 * 16 + c0 % 56 // 4 if last else c0 // 4
             copy(e, T.zz[:, 4 * c0:4 * c1], wz.indirect(T.offz[:, f0:f0 + (c1 - c0) // 4]), XW + WZ + ["offz"], ZE[c0 // 8:c1 // 8], down)
 
         def numbers():
             ts(T.g1[:], o6, float(8 * XE - 1), 0.5 - XE // 2, A.min, A.add, ["o6"], ["g1"])
             ts(T.g5[:], o6, 8.0, colv(8), A.mult, A.add, ["o6", "col"], ["g5"])
+            ts(T.g8[:], o6, 2.0, T.sc[:, 9:10], A.mult, A.add, ["o6", "sc9"], ["g8"])
             yield
             ts(T.g2[:], T.g1[:], 1.0 / XE, WHOLE, A.mult, A.add, ["g1"], ["g2"])
             ts(T.g4[:], T.g1[:], SC, T.sc[:, 5:6], A.mult, A.add, ["g1", "sc5"], ["g4"])
-            ts(T.g5[:], T.g5[:], T.sc[:, 9:10], None, A.min, None, ["g5", "sc9"], ["g5"])
+            ts(T.g8[:], T.g8[:], T.sc[:, 10:11], None, A.max, None, ["g8", "sc10"], ["g8"])
             yield
             ts(T.g3[:], T.g2[:], -WHOLE, -56.0, A.add, A.mult, ["g2"], ["g3"])
             ts(T.g7[:], T.g2[:], -WHOLE, float(C), A.add, A.mult, ["g2"], ["g7"])
             yield
             tt(T.g3[:], T.g3[:], T.g4[:], A.add, ["g3", "g4"], ["g3"])
+            tt(T.g5[:], T.g5[:], T.g8[:], A.min, ["g5", "g8"], ["g5"])
             yield
             ts(T.g1[:], T.g3[:], T.sc[:, 6:7], None, A.min, None, ["g3", "sc6"], ["g1"])
             ts(T.g2[:], T.g3[:], T.sc[:, 8:9], T.sc[:, 7:8], A.subtract, A.min, ["g3", "sc7", "sc8"], ["g2"])
@@ -602,34 +626,34 @@ def rank_program(g, core, T, topo):
             yield
         if last:
             todo[0] = numbers()
-        cuts = list(range(0, 337, 56)) if last else [0, 128, 336]
+        cuts = list(range(0, 337, 56)) + [352] if last else [0, 128, 352]
         for c0, c1 in zip(cuts, cuts[1:]):
             early("s", c0, c1)
         tr(T.l3[:], T.l2[:], ["l2"], ["l3"])
+        if t == 0:
+            pad(0)
         spare(4 if t == 0 else 1)
-        early("v", 336, 392)
-        ts(T.offl[:], T.l3[:].indirect((T.ll3 if last else T.ll2)[:]), T.sc[:, 0:1], None, A.add, None, ["l3", "ll2", "ll3", "sc0"], ["offl"])
-        spare()
 
         for b in range(4):
             mm(4 + b, 128, [(T.qg[:, 128 * b:128 * b + 128], T.sg[:, 128 * b:128 * b + 128], ql[:, 0:128], sl[:, 3 * KB:3 * KB + 128])],
                ["qg%d" % b, "land%d" % t, "pad%d" % t])
         for b in range(4):
             copy("v", T.dtl[:, 4 * KB + b:8 * KB:4], bank(4 + b, KB), ["ps%d" % (4 + b)], ["d%d_" % b])
+        ts(T.offl[:], T.l3[:].indirect((T.ll3 if last else T.ll2)[:]), T.sc[:, 0:1], None, A.add, None, ["l3", "ll3" if last else "ll2", "sc0"], ["offl"])
         spare()
         quant(T.qd[:], T.sd[:], T.dtl[:], ["d%d_" % b for b in range(4)] + ["dz0", "dz1"], ["qd"])
         for b in range(4):
             lo, hi = 16 + 128 * b, 128 * b
             mm(b, 128, [(T.qw[:, lo:lo + 128], T.sw[:, lo:lo + 128], T.qd[:, KB:KB + 128], T.sd[:, KB:KB + 128]),
                         (T.qw[:, hi:hi + 128], T.sw[:, hi:hi + 128], T.qd[:, 0:128], T.sd[:, 0:128])], WK + ["qd"])
-        spare()
-        early("v", 392, C)
-        for b in range(4):
-            if last:
-                spare()
-            copy("v", W[:, HB + b:HB + 8 * KB:4], bank(b, 2 * KB), ["ps%d" % b], ["h%d" % b], SC if t == 0 else None)
         if last:
-            spare()
+            early("v", 352, 392)
+        early("v", 392 if last else 352, C)
+        spare()
+        for b in range(4):
+            copy("v", W[:, HB + b:HB + 8 * KB:4], bank(b, 2 * KB), ["ps%d" % b], ["h%d" % b], SC if t == 0 else None)
+            if b == 3 or last and b == 1:
+                spare()
         wl = W[:, X0:HB + 8 * KB]
         LR = XW + WZ + ["w7", "offl"] + ["h%d" % b for b in range(4)]
         if t == 0:
@@ -662,7 +686,8 @@ def rank_program(g, core, T, topo):
 
         def times32(c):
             c0, c1 = chunks[c]
-            copy("s", T.z32[:, 4 * c0:4 * c1], T.zz[:, 4 * c0:4 * c1], ZE[c0 // 8:c1 // 8] + ZP[c], ["z32%d" % c], 32.0)
+            for b in range(4):
+                copy("s", T.z32[:, 4 * c0 + b:4 * c1:4], T.zz[:, 4 * c0 + b:4 * c1:4], ZE[c0 // 8:c1 // 8] + ZP[c], ["z32%d%d" % (c, b)], 32.0)
 
         def state(c):
             c0, c1 = chunks[c]
@@ -670,12 +695,14 @@ def rank_program(g, core, T, topo):
             for b in range(4):
                 out = T.x32[:, c0 // 4:c1 // 4, b:16:4] if last else W[:, X0 + 4 * c0 + b:X0 + 4 * c1:4]
                 k = 4 * (c % 2) + b
-                tt(out, bank(k, c1 - c0), T.z32[:, 4 * c0 + b:4 * c1:4], A.add, ["ps%d" % k, "z32%d" % c],
+                tt(out, bank(k, c1 - c0), T.z32[:, 4 * c0 + b:4 * c1:4], A.add, ["ps%d" % k, "z32%d%d" % (c, b)],
                    ["o%d%d" % (c, b)] if last else [XW[4 * c + b]])
 
         def scaled(es, c):
             c0, c1 = chunks[c]
             for a, e in enumerate(es):
+                if e == "-":
+                    continue
                 z0 = X0 + 4 * c0 + a * (c1 - c0)
                 copy(e, T.xk[:, c0 // 8:c1 // 8, 8 * a:8 * a + 8], W[:, z0:z0 + c1 - c0], XW[4 * c:4 * c + 4], ["xk%d%d" % (c, a)], SC)
 
@@ -683,6 +710,7 @@ def rank_program(g, core, T, topo):
             c0, c1 = chunks[c]
             keys(c, T.xk[:, c0 // 8:c1 // 8], ["xk%d%d" % (c, a) for a in range(4)])
         late("v", 0)
+        spare()
         late("s", 1)
         if not last:
             late("s", 2)
@@ -707,11 +735,12 @@ def rank_program(g, core, T, topo):
                 mm(b, c1 - c0, [(T.qw[:, lo:lo + 128], T.sw[:, lo:lo + 128], T.qz[:, c0:c1], T.sz[:, c0:c1])], WK + ["qz2"])
             scaled("ssss", 0)
             state(1)
-            scaled("ssss", 1)
+            scaled("ss--", 1)
             state(2)
             windows()
+            scaled("--vv", 1)
             rekey(0)
-            scaled("vvvv", 2)
+            scaled("vvvs", 2)
             rekey(1)
             rekey(2)
             turn(0)
@@ -729,28 +758,30 @@ def rank_program(g, core, T, topo):
     for a in range(4):
         place("v", 0, a)
     place("s", 1, 3)
-    times32(0)
     place("v", 1, 0)
-    layer(0)
     place("v", 1, 1)
+    times32(0)
+    layer(0)
     place("v", 1, 2)
+    spare()
     times32(1)
     layer(1)
+    spare()
     state(0)
     for j in range(4):
         unlay("s", 0, j)
     state(1)
-    result(0)
-    wr["qx1"] = wr["qx2"] = wr["xl00"]
+    spare()
     for j in range(4):
         unlay("v" if j < 3 else "s", 1, j)
-    copy("s", T.ys[:, 0:224], bank(0, 224), ["ps0"], ["ys0"])
+    result(0)
+    wr["qx1"] = wr["qx2"] = wr["xl00"]
     result(1)
+    copy("v", T.ys[:, 0:224], bank(0, 224), ["ps0"], ["ys0"])
     copy("v", T.ys[:, 224:448], bank(4, 224), ["ps4"], ["ys1"])
     dmas("out", [("y", ["qx0"], [], T.oc[:, 0:896], T.qx[:, 0:224].bitcast(u8)),
-                 ("s", ["ys0"], [], T.y[:, 0:224], T.ys[:, 0:224]),
-                 ("y", ["qx1"], [], T.oc[:, 896:XE], T.qx[:, 224:C].bitcast(u8))]
+                 ("s", ["qx1"], [], T.oc[:, 896:XE], T.qx[:, 224:C].bitcast(u8))]
          + [("s", ["qx0", "qx1"], [], T.osc[4 * k:4 * k + 4, :], T.sx[32 * k:32 * k + 4, :]) for k in range(4)]
-         + [("y", ["ys1"], [], T.y[:, 224:C], T.ys[:, 224:C])])
+         + [("y", ["ys0"], [], T.y[:, 0:224], T.ys[:, 0:224]), ("y", ["ys1"], [], T.y[:, 224:C], T.ys[:, 224:C])])
     for k in count:
         wait("y", (k, count[k]))

@@ -1,44 +1,49 @@
+import numpy as np
 from concourse.bass import DstId, RemoteDMATransfer
 from concourse.mybir import dt, AluOpType, ActivationFunctionType
 
 A = AluOpType
 AF = ActivationFunctionType
+s_ = np.s_
 C, M, P, V, R = 448, 14, 32, 6, 3
 XE = 4 * C
 X0 = 3 * XE
 HB = 11 * XE
+KB = 32
 BIG = float(2 ** 96)
-WHOLE = float(3 * 2 ** 22)
+TS = float(2 ** 80)
 SC = 0.03125
-L = 96
-DL = 132
+G = 15
+L = 6 * G
 QUAD = [0, 2, 1, 3]
-TREG = [0, 100, 200, 300, 400, 700, 500]
-T1, TAIL = 600, 700 + L
-KB = 24
-CD, BF, F, U8, U16 = "float8_e4m3fn_x4", "bfloat16", "float32", "uint8", "uint16"
+CYCLE = 0.00083
+PACES = [(1.0, 0.2, 0.8, 1.2, 0.7, (0.0, 1.1)), (1.0, 0.23, 0.5, 0.3, 1.0, (0.0, 1.5)), (1.0, 0.2, 0.9, 0.7, 1.3, (0.0, 0.6)),
+         (1.2, 0.16, 0.8, 1.2, 0.7, (0.0, 1.1)), (1.45, 0.2, 0.8, 1.2, 0.7, (0.0, 1.1))]
+PLANS = [(slow, wake, tensor, send, fly, (early, early)) for slow in (1.0, 1.1) for wake in (0.19, 0.21, 0.23) for tensor in (0.5, 0.8)
+         for send, fly in ((1.0, 0.7), (0.6, 0.8)) for early in (1.0, 1.5)]
+CD, BF, F, U8, U16, I32 = "float8_e4m3fn_x4", "bfloat16", "float32", "uint8", "uint16", "int32"
 
 SCRATCH = {"ps": ("psum", [128, 4096], F)}
 for _n, _s, _d in [
-        ("W", [HB + 384], BF), ("x3", [P, 4 * M], BF), ("xl", [4, 4, 2, 4 * M], BF), ("xk", [56, 32], BF), ("x32", [112, 16], BF),
-        ("zz", [XE], BF), ("z32", [XE], BF), ("lt", [C], BF), ("us", [4, 128], BF), ("vs", [512], BF), ("zt", [512], BF),
-        ("one", [516], BF), ("gt", [516], BF), ("bt", [576], BF), ("bu", [128], BF), ("bl", [128], BF), ("dtl", [608], BF),
+        ("W", [HB + 8 * KB], BF), ("zz", [M, 128], BF), ("z32", [XE], BF), ("xs", [112, 16], BF), ("lt", [C], BF),
+        ("xl", [P, 4 * M], BF), ("us", [4, 128], BF), ("vs", [512], BF), ("zt", [512], BF), ("one", [256], BF), ("gt", [1024], BF),
+        ("bt", [640], BF), ("dtl", [512], BF),
         ("qx", [C], CD), ("sx", [C], U8), ("qz", [C], CD), ("sz", [C], U8), ("qu", [128], CD), ("su", [128], U8),
-        ("qv", [128], CD), ("sv", [128], U8), ("qw", [528], CD), ("sw", [528], U8), ("qg", [512], CD), ("sg", [512], U8),
-        ("qb", [128], CD), ("sb", [256], U8), ("qn", [128], CD), ("qd", [152], CD), ("sd", [152], U8),
-        ("ql0", [152], CD), ("sl0", [224], U8), ("ql1", [152], CD), ("sl1", [224], U8), ("ql2", [152], CD), ("sl2", [224], U8),
-        ("kt", [C], F), ("ys", [C], F), ("rb", [2 * L], F), ("kb", [2 * L], F), ("sq", [2 * L], F), ("yy", [66], F),
-        ("dk", [200], F), ("dl", [2 * DL], F), ("dr", [L], F), ("df", [L], F), ("ff", [33], F), ("gg", [64], F), ("uu", [32], F),
-        ("tn", [TAIL + 32], F), ("dd", [L], F), ("lb", [V * L + 32], F), ("of", [L + 1], F), ("wt", [V], F),
-        ("blk", [512], F), ("col", [512], F), ("stg", [7, 2, 16], F), ("stc", [224], F), ("g7", [32], F), ("g8", [32], F),
-        ("pat", [64], F), ("sc", [12], F), ("tq", [64], F), ("tc", [256], F), ("bx", [64], F), ("tb", [104], F), ("t1", [64], F),
-        ("a2", [256], F), ("a3", [256], F), ("l2", [64], F), ("l3", [64], F),
-        ("g1", [32], F), ("g2", [32], F), ("g3", [32], F), ("g4", [32], F), ("g5", [32], F), ("g6", [32], F),
-        ("lbx", [4], U16), ("lbs", [2], U16), ("lbl", [2], U16), ("la1", [16], U16), ("la2", [8], U16), ("la3", [8], U16),
-        ("ll1", [4], U16), ("ll2", [2], U16), ("ll3", [2], U16),
-        ("offb", [16], U16), ("offc", [16], U16), ("offz", [128], U16), ("offl", [32], U16)]:
+        ("qv", [128], CD), ("sv", [128], U8), ("qw", [528], CD), ("sw", [528], U8), ("qg", [256], CD), ("sg", [256], U8),
+        ("qb", [256], CD), ("sb", [384], U8), ("qn", [128], CD), ("qd", [160], CD), ("sd", [160], U8),
+        ("kt", [C], F), ("ys", [C], F), ("rb", [2 * L], F), ("kb", [2 * L], F), ("sq", [2 * L], F), ("dk", [2 * L], F), ("dr", [L - 3], F),
+        ("gy", [2 * L + 60], F), ("fz", [30], F), ("s1", [30], F), ("s0", [30], F), ("tl", [240], F),
+        ("ti", [30], F), ("lb", [V * L + 50], F), ("tf", [32], F), ("wt", [V], F),
+        ("blk", [320], F), ("col", [320], F), ("pat", [48], F), ("sc", [16], F), ("mk", [64], F),
+        ("bx", [32], F), ("tb", [96], F), ("ex", [128], F), ("a3", [10, 2, 8], F), ("stg", [7, 4], F),
+        ("g1", [32], I32), ("g2", [32], F), ("g3", [32], F), ("g4", [32], F), ("g5", [32], F), ("g6", [32], F),
+        ("lbx", [2], U16), ("lbs", [4], U16), ("lex", [8], U16), ("offb", [32], U16), ("offz", [112], U16), ("offl", [28], U16)]:
     SCRATCH[_n] = ("sbuf", [128] + _s, _d)
-SEMAPHORES = ["v", "s", "t", "g", "lx", "lu", "lw", "lv", "w1", "w2", "sent", "arr0", "arr1", "arr2", "og", "out"]
+SEMAPHORES = ["v", "s", "t", "g", "lx", "lu", "lw", "lv", "lp", "w0", "w1", "w2", "sent0", "sent1", "og", "out", "end"]
+for _n in ["%d%d" % (_t, _k) for _t in range(R) for _k in range(2)]:
+    SCRATCH["ql" + _n] = ("sbuf", [128, KB + 128], CD)
+    SCRATCH["sl" + _n] = ("sbuf", [128, 256], U8)
+    SEMAPHORES.append("arr" + _n)
 
 
 def rank_program(g, core, T, topo):
@@ -48,740 +53,610 @@ def rank_program(g, core, T, topo):
     N = len(T.cores)
     S = T.sem
     eng = {"v": g.vector, "s": g.scalar, "t": g.tensor, "g": g, "y": g.sync}
-    count = {}
-    known = {e: {} for e in eng}
-    clock = {}
-    wr, rd = {}, {}
-
-    def wait(e, tok):
-        if known[e].get(tok[0], 0) >= tok[1]:
-            return
-        eng[e].wait_ge(S[tok[0]], tok[1])
-        for k, c in clock.get(tok, {}).items():
-            if known[e].get(k, 0) < c:
-                known[e][k] = c
-        known[e][tok[0]] = tok[1]
-
-    def order(e, reads, writes):
-        need = {}
-        for k in list(reads) + list(writes):
-            toks = [wr[k]] if k in wr else []
-            if k in writes:
-                toks = toks + rd.get(k, [])
-            elif k.startswith("ps"):
-                toks = toks + [t for t in rd.get(k, []) if t[0] != e]
-            for t in toks:
-                need[t[0]] = max(need.get(t[0], 0), t[1])
-        for k in sorted(need, key=lambda k: k != e):
-            wait(e, (k, need[k]))
-
-    def note(e, tok, reads, writes):
-        clock[tok] = dict(known[e])
-        for k in reads:
-            rd.setdefault(k, []).append(tok)
-        for k in writes:
-            wr[k] = tok
-            rd[k] = []
-
-    def do(e, reads, writes, call):
-        order(e, reads, writes)
-        count[e] = count.get(e, 0) + 1
-        call().then_inc(S[e], 1)
-        note(e, (e, count[e]), reads, writes)
-
-    def dmas(sem, items):
-        tok = (sem, count.get(sem, 0) + 16 * len(items))
-        count[sem] = tok[1]
-        seen = {}
-        for e, reads, writes, out, in_ in items:
-            order(e, reads, writes)
-            eng[e].dma_start(out, in_).then_inc(S[sem], 16)
-            for k, c in known[e].items():
-                seen[k] = max(seen.get(k, 0), c)
-        for e, reads, writes, out, in_ in items:
-            note(e, tok, reads, writes)
-        clock[tok] = seen
-
     vec, act, pe = g.vector, g.scalar, g.tensor
-    W, ps = T.W, T.ps
     u8 = dt.uint8
 
-    def bank(b, n):
-        return ps[:, 512 * b:512 * b + n]
+    jobs = []
+    wrote = {}
+    seen = {}
+    count = {}
+    rows = set()
 
-    def alone():
-        wait("g", ("g", count["g"]))
+    def at(name, idx=s_[:], raw=False):
+        idx = idx if isinstance(idx, tuple) else (idx,)
+        shape = SCRATCH[name][1]
+        lo, hi, _ = idx[0].indices(128)
+        cols = np.arange(int(np.prod(shape[1:]))).reshape(shape[1:])[idx[1:]].ravel()
+        cycles = len(cols) * (0.5 if SCRATCH[name][2] in (BF, U16) else 1.0)
+        if name == "ps":
+            cols, lo, hi = np.arange(cols[0] // 512 * 512, cols[0] // 512 * 512 + 512), 0, 128
+        mask = np.zeros((8, int(np.prod(shape[1:]))), bool)
+        mask[np.ix_(range(lo // 16, -(-hi // 16)), cols)] = True
+        ap = T[name][idx if len(idx) > 1 else idx[0]]
+        return (ap.bitcast(u8) if raw else ap, [(name, mask)], cycles, (lo, hi))
 
-    def iota(out, pattern, base, cm, key):
-        do("g", [], [key], lambda: g.iota(out, pattern, base, cm, allow_small_or_imprecise_dtypes=True))
+    def hbm(ap):
+        return (ap, [], 0, None)
 
-    def copy(e, out, in_, reads, writes, scale=None):
-        if e == "s":
-            if scale is None:
-                do(e, reads, writes, lambda: act.activation(out, in_, AF.Copy))
+    def pick(win, off):
+        return (win[0].indirect(off[0]), win[1] + off[1], 64 + 50 * off[2], None)
+
+    def job(e, outs, ins, call, hold, more=0.0, token=None):
+        ins = [v for v in ins if isinstance(v, tuple)]
+        reads = [r for v in ins for r in v[1]]
+        writes = [r for v in outs for r in v[1]]
+        deps = set()
+        for name, mask in reads + writes:
+            if name in wrote:
+                deps.update(int(k) for k in np.unique(wrote[name][mask]) if k >= 0)
+            if name == "ps":
+                deps.update(k for k, m in seen.get(name, []) if jobs[k]["e"] != e and (m & mask).any())
+        for name, mask in writes:
+            deps.update(k for k, m in seen.get(name, []) if (m & mask).any())
+            seen[name] = [(k, m & ~mask) for k, m in seen.get(name, []) if (m & ~mask).any()]
+            wrote.setdefault(name, np.full(mask.shape, -1, np.int32))[mask] = len(jobs)
+        for name, mask in reads:
+            seen.setdefault(name, []).append((len(jobs), mask))
+        deps.discard(len(jobs))
+        jobs.append({"e": e, "call": call, "deps": deps, "hold": hold, "more": more, "token": token, "mates": [len(jobs)]})
+
+    def do(e, outs, ins, call, hold=None):
+        if hold is None:
+            cycles = max(v[2] for v in outs + ins if isinstance(v, tuple))
+            if e == "s" and ins[0][3]:
+                cycles = max(outs[0][2], ins[0][2]) * (2 if SCRATCH[outs[0][1][0][0]][2] == SCRATCH[ins[0][1][0][0]][2] == BF else 1)
+            hold = max(78 if e == "s" else 64, cycles) * CYCLE
+        job(e, outs, ins, call, hold)
+
+    def dmas(sem, items, more):
+        count[sem] = count.get(sem, 0) + 16 * len(items)
+        mates = list(range(len(jobs), len(jobs) + len(items)))
+        for e, out, in_ in items:
+            job(e, [out], [in_], lambda e=e, out=out, in_=in_: eng[e].dma_start(out[0], in_[0]).then_inc(S[sem], 16), 0.05, more, (sem, count[sem]))
+            jobs[-1]["mates"] = mates
+
+    def issue():
+        n = len(jobs)
+        users = [{} for _ in jobs]
+        prev = {}
+        for k, j in enumerate(jobs):
+            j["deps"] = set(m for d in j["deps"] for m in jobs[d]["mates"] if m < k)
+            if (j["e"] in "gy" or k in rows) and j["e"] in prev:
+                users[prev[j["e"]]][k] = False
+            prev[j["e"]] = k
+            for d in j["deps"]:
+                users[d][k] = True
+
+        def times(pace):
+            slow, wake, tensor, send, fly, early = pace
+            hold = [send if j["more"] == "sent" else j["hold"] * {"t": tensor, "y": 1.0}.get(j["e"], slow) for j in jobs]
+            more = [{"sent": fly, "late": fly, "early": fly + early[0], "first": fly + early[1]}.get(j["more"], j["more"]) for j in jobs]
+            return hold, more, wake
+
+        def plan(pace):
+            hold, more, wake = times(pace)
+            way, left = [0.0] * n, [0] * n
+            for k in range(n - 1, -1, -1):
+                way[k] = hold[k] + max([more[k]] + [way[u] + (more[k] + wake) * waits for u, waits in users[k].items()])
+                for u in users[k]:
+                    left[u] += 1
+            ready, free, order = [0.0] * n, {e: 0.0 for e in eng}, []
+            pool = [k for k in range(n) if not left[k]]
+            while pool:
+                e = jobs[min(pool, key=lambda k: max(ready[k], free[jobs[k]["e"]]))]["e"]
+                mine = [k for k in pool if jobs[k]["e"] == e]
+                now = max(free[e], min(ready[k] for k in mine))
+                k = max((k for k in mine if ready[k] <= now), key=lambda k: way[k])
+                for h in mine:
+                    if now < ready[h] < now + hold[k] and now + hold[k] + way[h] > max(ready[h] + way[h], ready[h] + hold[h] + way[k]):
+                        k, now = h, ready[h]
+                pool.remove(k)
+                order.append(k)
+                free[e] = now + hold[k]
+                for u, waits in users[k].items():
+                    ready[u] = max(ready[u], free[e] + (more[k] + wake) * waits)
+                    left[u] -= 1
+                    if not left[u]:
+                        pool.append(u)
+            return order
+
+        def lasts(order, pace):
+            hold, more, wake = times(pace)
+            ready, free = [0.0] * n, {e: 0.0 for e in eng}
+            for k in order:
+                e = jobs[k]["e"]
+                free[e] = max(free[e], ready[k]) + hold[k]
+                for u, waits in users[k].items():
+                    ready[u] = max(ready[u], free[e] + (more[k] + wake) * waits)
+            return max(free.values())
+        known = {e: {} for e in eng}
+        clock = {}
+        for k in min((plan(p) for p in PLANS), key=lambda order: sum(lasts(order, p) / p[0] for p in PACES)):
+            j = jobs[k]
+            e = j["e"]
+            need = {}
+            for d in j["deps"]:
+                sem, c = jobs[d]["token"]
+                need[sem] = max(need.get(sem, 0), c)
+            for sem in sorted(need, key=lambda x: x != e):
+                if known[e].get(sem, 0) < need[sem]:
+                    eng[e].wait_ge(S[sem], need[sem])
+                    for x, c in clock.get((sem, need[sem]), {}).items():
+                        known[e][x] = max(known[e].get(x, 0), c)
+                    known[e][sem] = need[sem]
+            if j["token"] is None:
+                count[e] = count.get(e, 0) + 1
+                j["token"] = (e, count[e])
+                j["call"]().then_inc(S[e], 1)
+                clock[j["token"]] = dict(known[e])
             else:
-                do(e, reads, writes, lambda: act.activation(out, in_, AF.Identity, scale=scale))
-        elif scale is None:
-            do(e, reads, writes, lambda: vec.tensor_copy(out, in_))
-        else:
-            do(e, reads, writes, lambda: vec.tensor_scalar(out, in_, scale, None, A.mult))
+                j["call"]()
+        for sem in count:
+            if known["y"].get(sem, 0) < count[sem]:
+                g.sync.wait_ge(S[sem], count[sem])
 
-    def ts(out, in0, s1, s2, op0, op1, reads, writes):
+    def arg(v):
+        return v[0] if isinstance(v, tuple) else v
+
+    def iota(out, pattern, base=0, cm=0):
+        do("g", [out], [], lambda: g.iota(out[0], pattern, base, cm, allow_small_or_imprecise_dtypes=True),
+           0.13 + 2 * CYCLE * int(np.prod([c for _, c in pattern])))
+
+    def copy(e, out, in_, scale=None, bias=None, func=AF.Identity):
+        if e == "v":
+            if scale is None:
+                do(e, [out], [in_], lambda: vec.tensor_copy(out[0], in_[0]))
+            else:
+                do(e, [out], [in_], lambda: vec.tensor_scalar(out[0], in_[0], scale, None, A.mult))
+        elif scale is None and bias is None:
+            do(e, [out], [in_], lambda: act.activation(out[0], in_[0], AF.Copy))
+        else:
+            do(e, [out], [in_, scale, bias], lambda: act.activation(
+                out[0], in_[0], func, bias=0.0 if bias is None else arg(bias), scale=1.0 if scale is None else arg(scale)))
+
+    def ts(out, in0, s1, op0, s2=None, op1=None):
         if s2 is None:
-            do("v", reads, writes, lambda: vec.tensor_scalar(out, in0, s1, None, op0))
+            do("v", [out], [in0, s1], lambda: vec.tensor_scalar(out[0], in0[0], arg(s1), None, op0))
         else:
-            do("v", reads, writes, lambda: vec.tensor_scalar(out, in0, s1, s2, op0, op1))
+            do("v", [out], [in0, s1, s2], lambda: vec.tensor_scalar(out[0], in0[0], arg(s1), arg(s2), op0, op1))
 
-    def tt(out, in0, in1, op, reads, writes):
-        do("v", reads, writes, lambda: vec.tensor_tensor(out, in0, in1, op))
+    def tt(out, in0, in1, op):
+        do("v", [out], [in0, in1], lambda: vec.tensor_tensor(out[0], in0[0], in1[0], op))
 
-    def tr(out, in_, reads, writes):
-        do("v", reads, writes, lambda: vec.transpose(out, in_))
+    def tr(out, in_):
+        do("v", [out], [in_], lambda: vec.transpose(out[0], in_[0]))
 
-    def scan(out, d0, d1, init, op0, op1, reads, writes):
-        do("v", reads, writes, lambda: vec.tensor_tensor_scan(out, d0, d1, init, op0, op1))
+    def scan(out, d0, d1, init, op=A.max):
+        do("v", [out], [d0, d1], lambda: vec.tensor_tensor_scan(out[0], d0[0], d1[0], init, A.add, op))
 
-    def quant(q, s, in_, reads, writes):
-        do("v", reads, writes, lambda: vec.quantize_mx(q, s, in_))
+    def quant(q, s, a, b, in_, sa=None):
+        qv, sv = at(q, s_[:, a:b]), at(s, s_[:, a:b] if sa is None else s_[:, sa:sa + b - a])
+        do("v", [qv, sv], [in_], lambda: vec.quantize_mx(qv[0], sv[0], in_[0]), 0.012 + 0.00088 * (b - a))
 
-    def fill(ap, val, key, after=()):
-        do("v", list(after), [key], lambda: vec.memset(ap, val))
+    def fill(out, val):
+        do("v", [out], [], lambda: vec.memset(out[0], val))
 
-    def mm(b, n, pairs, reads):
-        order("t", reads, ["ps%d" % b])
-        for i, (lq, ls, rq, rs) in enumerate(pairs):
-            ins = pe.matmul_mx(bank(b, n), lq, ls, rq, rs, i == 0, i == len(pairs) - 1)
-        count["t"] = count.get("t", 0) + 1
-        ins.then_inc(S.t, 1)
-        note("t", ("t", count["t"]), reads, ["ps%d" % b])
+    def put(out, n, val):
+        copy("s", out, at("zt", s_[out[3][0]:out[3][1], 0:n]), bias=val)
 
-    CH = [(0, 128), (128, 320), (320, 448)]
-    CL = [(0, 224), (224, 448)]
-    XW = ["x%d%d" % (c, b) for c in range(3) for b in range(4)]
-    WZ = ["w%d" % d for d in (1, 2, 3, 4, 5, 6)]
-    WB = WZ[0:5] + ["w-1", "w-2", "w-3"]
+    def bank(b, a, n, step=1):
+        return at("ps", s_[:, 512 * b + a:512 * b + n:step])
+
+    def side(q, s, a, n, sa=None):
+        return at(q, s_[:, a:a + n]), at(s, s_[:, a:a + n] if sa is None else s_[:, sa:sa + n])
+
+    def mm(b, n, pairs):
+        out = bank(b, 0, n)
+        do("t", [out], [v for l, r in pairs for v in l + r], lambda: [
+            pe.matmul_mx(out[0], l[0][0], l[1][0], r[0][0], r[1][0], i == 0, i == len(pairs) - 1) for i, (l, r) in enumerate(pairs)][-1],
+           len(pairs) * (n + 16) * CYCLE)
+
+    def w(a, b, step=1, lo=0, hi=128):
+        return at("W", s_[lo:hi, a:b:step])
 
     def windows():
-        def shift(d):
-            lo, hi = (0, 128 - 16 * d) if d >= 0 else (-16 * d, 64)
-            s0 = X0 + d * XE
-            return ("y", XW, ["w%d" % d], W[lo:hi, s0:s0 + XE], W[lo + 16 * d:hi + 16 * d, X0:X0 + XE])
-        dmas("w1", [shift(d) for d in (1, 2, 3, -1, 4, -2, 5, -3)])
-        dmas("w2", [shift(d) for d in (6, 7)])
+        for sem, ds, more in (("w0", (1, -1, -2, -3), 2.0), ("w1", (2, 3, 4, 5), 3.5), ("w2", (6, 7), 4.0)):
+            items = []
+            for d in ds:
+                lo, hi = (0, 128 - 16 * d) if d >= 0 else (-16 * d, 64)
+                items.append(("y", w(X0 + d * XE, X0 + d * XE + XE, 1, lo, hi), w(X0, X0 + XE, 1, lo + 16 * d, hi + 16 * d)))
+            dmas(sem, items, more)
 
-    dmas("lx", [("y", [], ["x3"], T.x3[:], T.x[:])])
-    dmas("lu", [("y", [], ["us%d" % k], T.us[:, k:k + 3:2, :], T.u[:, 256 * k:256 * k + 256]) for k in range(2)])
-    WK = ["qw", "sw", "qw0", "sw0"]
+    dmas("lx", [("y", at("xl"), hbm(T.x[:]))], 1.6)
+    dmas("lu", [("y", at("us", s_[:, k:k + 3:2, :]), hbm(T.u[:, 256 * k:256 * k + 256])) for k in range(2)], 2.2)
 
     def blk(k, a=0, b=32):
-        return T.blk[:, 32 * k + a:32 * k + b]
-    w0 = 9 * XE + 4 * KB
-    BK = ["blk%d" % k for k in range(19)]
-    iota(blk(0), [[16, 4], [2 * XE, 4], [-4 * KB, 2]], w0, 0, BK[0])
-    iota(blk(1), [[0, 2], [1, 4], [0, 4]], 0, 0, BK[1])
-    iota(blk(2, 0, 16), [[64, 2], [-512, 2], [128, 4]], 512, 1, BK[2])
-    iota(blk(2, 16, 32), [[64, 2], [-512, 2], [128, 4]], 528, 1, BK[16])
-    iota(blk(3), [[16, 2], [0, 16]], 0, 1, BK[3])
-    iota(blk(4), [[0, 4], [64, 2], [128, 4]], 0, 0, BK[4])
-    iota(blk(5), [[4, 4], [2 * XE, 4], [-4 * KB, 2]], w0, 0, BK[5])
-    iota(T.pat[:, 0:16], [[4, 8], [0, 2]], 0, 0, "pat0")
+        return at("blk", s_[:, 32 * k + a:32 * k + b])
 
-    def more():
-        iota(blk(6, 0, 16), [[128, 2], [16, 2], [0, 4]], 0, 1, BK[6])
-        iota(blk(6, 16, 32), [[128, 2], [16, 2], [0, 4]], 0, 1, BK[17])
-        iota(blk(7), [[-16, 2], [1, 8], [32, 2]], 17, 0, BK[7])
-        iota(blk(8), [[8 - 128, 4], [2 - 16 * XE, 4], [1 + 32 * KB, 2]], 8 * C - 8 * w0, 0, BK[8])
-        iota(blk(9, 0, 16), [[8, 2], [1, 2], [0, 4]], 0, 0, BK[9])
-        iota(blk(9, 16, 32), [[8, 2], [1, 2], [0, 4]], 0, 0, BK[18])
-        iota(blk(10), [[1, 32]], 0, 0, BK[10])
-        iota(blk(11), [[-16, 2], [1, 16]], 17, 0, BK[11])
-        iota(blk(12), [[-16, 2], [1, 16]], 17, 0, BK[12])
-        iota(blk(13), [[0, 4], [2, 4], [0, 2]], 0, 0, BK[13])
-        iota(blk(14), [[8 - 32, 4], [128 - 8, 4], [0, 2]], 0, 0, BK[14])
-        iota(blk(15), [[8, 4], [128, 4], [4, 2]], 0, 0, BK[15])
-        iota(T.pat[:, 16:32], [[2, 4], [16, 2], [0, 2]], 0, 0, "pat1")
-        iota(T.pat[:, 32:40], [[32, 2], [64, 4]], 0, 0, "pat2")
-        for c0, c1 in CH:
-            iota(T.stg[:, c0 // 64:c1 // 64, 0, :], [[64, 4], [1, (c1 - c0) // 32], [32, 2]], 17 + c0 // 32, 0, "stg%d" % c0)
+    def col(k, lo=0, hi=128):
+        return at("col", s_[lo:hi, 32 * k:32 * k + 1])
 
-    def rest():
-        sk = ["stg%d" % c0 for c0, c1 in CH]
-        do("s", sk, ["stga"], lambda: act.activation(T.stg[0:96, :, 1, :], T.stg[0:96, :, 0, :], AF.Identity, bias=-16.0))
-        copy("s", T.stg[96:128, :, 1, :], T.stg[96:128, :, 0, :], sk, ["stgb"])
-        copy("s", T.blk[96:128, 400:416], T.blk[96:128, 384:400], [BK[12]], [BK[12]])
-        put(T.dtl[:, 0:4 * KB], 4 * KB, 0.0, "dz0")
-        put(T.dtl[:, 8 * KB:608], 608 - 8 * KB, 0.0, "dz1")
-    T0 = ["t0"] + ["t0%d%d" % (a, k) for a in range(4) for k in range(2)]
+    def sc(k, lo=0, hi=128):
+        return at("sc", s_[lo:hi, k:k + 1])
+    iota(at("ti"), [[-XE, 2], [128, G]], XE - 128, 4)
+    iota(blk(4), [[16, 4], [2 * XE, 4], [-4 * KB, 2]], 9 * XE + 4 * KB - 4 * 96, 4)
+    iota(blk(0), [[-XE, 2], [0, 4], [1, 4]], 0, -XE // 16)
+    iota(blk(1), [[0, 2], [L, 4], [0, 4]], L - 1)
+    for h in range(2):
+        iota(blk(2, 16 * h, 16 * h + 16), [[0, 2], [64, 2], [128, 4]], 16 * h, 1)
+        iota(blk(9, 16 * h, 16 * h + 16), [[0, 2], [64, 2], [128, 4]], 528 * h, 1)
+    iota(blk(3), [[0, 2], [1, 4], [0, 4]])
+    iota(blk(5), [[0, 4], [1, 2], [0, 4]])
+    iota(blk(6), [[1, 2], [0, 16]])
+    iota(blk(7), [[0, 2], [1, 2], [0, 8]])
+    iota(blk(8), [[1, 32]])
+    iota(at("pat", s_[:, 4:10]), [[4, 3], [-G, 2]], G + 1)
+    iota(at("pat", s_[:, 10:12]), [[-G, 2]], G + 13)
+    iota(at("pat", s_[:, 16:48]), [[0, 2], [1, 2], [0, 8]])
+    iota(at("one"), [[0, 256]], 1)
+    for b in range(4):
+        out = at("gt", s_[:, 256 * b:256 * b + 256])
+        do("g", [out], [at("one")], lambda out=out, b=b: g.affine_select(out[0], T.one[:], [[1, 256]], A.is_equal, 0.0, -b, -4), 0.6)
+    iota(at("bt", s_[:, 256:640]), [[0, 384]])
 
-    def put(ap, n, val, key, after=()):
-        do("s", ["zt"] + list(after), [key], lambda: act.activation(ap, T.zt[:, 0:n], AF.Identity, bias=val))
-    fill(T.zt[:], 0.0, "zt")
-    fill(T.tn[:, 0:L], 0.0, "t0z")
-    fill(T.dk[:], 0.0, "dk")
-    fill(T.dl[:], 1.0, "dl")
-    fill(T.dr[:], 0.0, "dr")
-    fill(T.df[:], 1.0, "df")
-    fill(T.tn[:, TAIL:TAIL + 32], 0.0, "tail")
-    fill(T.dd[:], 1.0, "dd")
-    fill(T.rb[:, 0:L], -BIG, "r0")
-    fill(T.kb[:, 0:L], -BIG, "k0")
-    fill(T.yy[:], 0.0, "yi")
-    fill(T.sq[96:128, :], -BIG, "si")
-    fill(T.one[:], 1.0, "one")
+    fill(at("zt"), 0.0)
+    fill(at("dr"), 0.0)
+    fill(at("dk"), 0.0)
+    fill(at("gy"), 0.0)
+    fill(at("tl"), -BIG)
+    fill(at("sq"), -BIG)
+    fill(at("rb", s_[:, 2:2 * L:45]), -BIG)
+    fill(at("kb", s_[:, 2:L:45]), -BIG)
+    fill(at("tb", s_[64:128]), 0.0)
+    quant("qn", "sb", 0, 128, at("zt"))
+    put(at("dr", s_[:, 42:43]), 1, -BIG)
+    put(at("dk", s_[:, 0:2 * L:3]), 60, -BIG)
+    put(at("gy", s_[:, 0:2 * L + 60:L + 30]), 2, -BIG)
     for k in range(2):
-        put(T.tn[:, 48 * k + 3:48 * k + 42:3], 13, -128.0, "t0" if k else "t0y", ["t0z"])
-    put(T.ff[:], 33, 0.0, "f")
-    put(T.of[:, 0:1], 1, 0.0, "ofi")
-    for k in range(2):
-        put(T.dk[:, 100 * k:100 * k + L:3], 32, -BIG, "dk%d" % k, ["dk"])
-    for k in range(2):
-        put(T.dl[:, DL * k:DL * k + 1], 1, 0.0, "dl%d" % k, ["dl"])
-        for c in (46, 47):
-            put(T.dl[:, DL * k + c:DL * k + L:48], 2, -1.0, "dm%d%d" % (k, c))
-    put(T.dr[:, 0:L:48], 2, -BIG, "dr")
-    put(T.df[:, 0:L:48], 2, 0.0, "df")
-    put(T.tn[:, T1:T1 + L], L, 0.0, "pz")
-    put(T.dd[:, 0:L:3], 32, 0.0, "dd")
-    put(T.tn[:, TAIL + 4:TAIL + 32:4], 7, 1.0, "tail")
-    for k in range(2):
-        put(T.tn[:, T1 + 48 * k + 3:T1 + 48 * k + 42:3], 13, -32.0, "py%d" % k, ["pz"])
-    put(T.tn[:, TAIL + 16:TAIL + 17], 1, -3.0, "tail")
-    wr["dk"] = wr["dl"] = wr["tail"]
-    order("g", ["t0z"], [])
+        put(at("gy", s_[:, (L + 30) * k + 1:(L + 30) * k + L + 3:3]), 31, BIG / 2)
+    put(at("lb", s_[0:32, V * L + 34:V * L + 50]), 16, 0.0)
+
     for a in range(4):
         q0 = 32 * QUAD[a]
-        if a == 1:
-            alone()
-        iota(T.tn[q0:q0 + 32, 0:L:48], [[XE, 2]], -(2 * a + 1) * XE, -4, T0[1 + 2 * a])
-        iota(T.tn[q0:q0 + 32, 42:L:48], [[-XE, 2]], (2 * a + 1) * XE + 128 * (M - 1), 4, T0[2 + 2 * a])
-    alone()
-    iota(T.tc[:], [[0, 64], [1, 4]], 0, 0, "tc")
-    iota(T.tq[:, 0:32], [[0, 8], [1, 4]], 0, 0, "tq0")
-    iota(T.tq[:, 32:64], [[0, 2], [1, 4], [0, 4]], 0, 0, "tq1")
-    iota(T.bt[:, 160:576], [[0, 416]], 0, 0, "btz")
-    more()
-    do("g", ["one"], ["gt"], lambda: g.affine_select(T.gt[:], T.one[:], [[1, 516]], A.is_equal, 0.0, -3, -4))
-    for k in range(2):
-        for h in range(2):
-            wr["z%d%d" % (k, h)], wr["st%d%d" % (k, h)], wr["y%d%d" % (k, h)] = wr["dk"], wr["dl"], wr["yi"]
-            wr["r%d%d" % (0, h)], wr["k%d%d" % (0, h)] = wr["r0"], wr["k0"]
-        for c in "ACa":
-            wr["s%d%s" % (k, c)] = wr["si"]
+        put(sc(0, q0, q0 + 32), 1, (2 * a * XE - 4 * q0) * TS)
+    put(sc(2, 0, 96), 1, 1 / TS)
+    put(sc(2, 96, 128), 1, 0.0)
+    put(sc(3, 96, 128), 1, 0.0)
+    put(sc(4, 0, 64), 1, 1 / TS)
+    put(sc(4, 64, 128), 1, 0.0)
+    put(sc(5, 64, 128), 1, float(X0))
+    copy("s", at("tl", s_[:, 0:L:3]), at("ti"), TS, sc(0))
 
-    def colv(k):
-        return T.col[:, 32 * k:32 * k + 1]
+    def columns():
+        put(at("dtl", s_[:, 4 * KB:512]), 512 - 4 * KB, 0.0)
+        quant("qd", "sd", 0, 128, at("zt"))
+        for n, k, m in ((0, 0, 2), (2, 19, 1), (3, 18, 1), (4, 17, 1), (5, 16, 1)):
+            copy("s", at("wt", s_[96:128, n:n + m]), at("col", s_[96:128, 128 + k:128 + k + m]), TS, BIG / 2)
+        copy("s", sc(3, 0, 96), col(0, 0, 96))
+        copy("s", sc(5, 0, 64), col(0, 0, 64), bias=X0 - BIG / 2 / TS)
+        for k in range(2):
+            copy("s", sc(6 + k), col(6 + k), -BIG)
+            copy("s", at("mk", s_[:, 32 * k:32 * k + 32]), at("pat", s_[:, 16:48]), BIG, sc(6 + k), AF.Abs)
 
-    def pad(t):
-        quant(T["ql%d" % t][:, KB:KB + 128], T["sl%d" % t][:, 4 * KB:4 * KB + 128], T.zt[:, 0:512], ["zt"], ["pad%d" % t])
+    def lists(n):
+        if n:
+            ts(at("lbx"), at("zt", s_[:, 0:2]), col(1), A.add, 2.0 * L - 1, A.min)
+            ts(at("lbs", s_[:, 0:1]), col(2), 0.0625, A.mult, 31.0, A.min)
+            ts(at("lbs", s_[:, 2:3]), col(9), 0.0625, A.mult, 63.0, A.min)
+            return
+        ts(at("lex", s_[:, 0:6]), at("pat", s_[:, 4:10]), col(3), A.add)
+        ts(at("lex", s_[:, 6:8]), at("pat", s_[:, 10:12]), col(5), A.add)
 
-    def lists():
-        fill(T.lbs[64:128, 0:1], 64, "lbs2")
-        fill(T.lbl[64:128, 0:1], 64, "lbl2")
-        fill(T.lbx[:, 2:4], 4 * L + 93, "lbx2")
-        quant(T.qn[:], T.sb[:, 0:128], T.zt[:], ["zt"], ["qb"])
-        yield
-        tr(T.col[:, 0:192], T.blk[:, 0:192], BK[0:6] + BK[16:17], ["cola"])
-        yield
-        ts(T.wt[96:128, 0:4], T.pat[96:128, 0:8:2], T.col[96:128, 0:1], None, A.add, None, ["pat0", "cola"], ["wt"])
-        ts(T.wt[96:128, 4:6], T.pat[96:128, 8:12:2], 4.0, T.col[96:128, 160:161], A.mult, A.add, ["pat0", "cola"], ["wt5"])
-        ts(T.sc[:, 2:3], colv(1), float(L), 93.0, A.mult, A.add, ["cola"], ["sc2"])
-        ts(T.sc[0:64, 3:4], T.col[0:64, 96:97], T.col[0:64, 128:129], None, A.add, None, ["cola"], ["sc3"])
-        yield
-        ts(T.sc[:, 0:1], colv(3), -112.0, None, A.mult, None, ["cola"], ["sc0"])
-        ts(T.sc[:, 1:2], colv(3), -112.0, float(X0), A.mult, A.add, ["cola"], ["sc1"])
-        ts(T.tb[:, 64:65], colv(3), 112.0, None, A.mult, None, ["cola"], ["tb64"])
-        yield
-        ts(T.lbs[0:64, 0:1], T.col[0:64, 64:65], 0.0625, None, A.mult, None, ["cola"], ["lbs"])
-        ts(T.lbx[:, 0:2], T.pat[:, 0:2], T.sc[:, 2:3], None, A.add, None, ["pat0", "sc2"], ["lbx"])
-        yield
-        ts(T.lbl[0:64, 0:1], T.sc[0:64, 3:4], 0.0625, 72.0, A.mult, A.add, ["sc3"], ["lbl"])
-        yield
-        tr(T.col[:, 192:352], T.blk[:, 192:352], BK[6:11] + BK[17:19], ["col"])
-        yield
-        ts(T.la1[:], T.pat[:, 16:32], colv(9), None, A.add, None, ["pat1", "col"], ["la1"])
-        ts(T.ll1[:], T.pat[:, 0:4], 64.0, colv(6), A.mult, A.add, ["pat0", "col"], ["ll1"])
-        ts(T.ll2[:], T.pat[:, 0:4:2], 2.0, colv(7), A.mult, A.add, ["pat0", "col"], ["ll2"])
-        yield
-        tr(T.stc[:], T.stg[:], ["stga", "stgb"], ["stc"])
-        yield
-        ts(T.ll1[96:128, :], T.ll1[96:128, :], 0.0625, None, A.mult, None, ["ll1"], ["ll1b"])
-        ts(T.ll1[0:96, :], T.ll1[0:96, :], 0.0625, 32.0, A.mult, A.add, ["ll1"], ["ll1a"])
-        ts(T.ll2[:], T.ll2[:], 63.0, None, A.min, None, ["ll2"], ["ll2"])
-        copy("v", T.la2[:, 0:7], T.stc[:, 0:224:32], ["stc"], ["la2"])
-        yield
-        for b in range(4):
-            quant(T.qg[:, 128 * b:128 * b + 128], T.sg[:, 128 * b:128 * b + 128], T.gt[:, 3 - b:515 - b], ["gt"], ["qg%d" % b])
-            yield
-        yield
-        tr(T.col[:, 352:512], T.blk[:, 352:512], BK[11:16], ["colc"])
-        yield
-        o = T1
-        ts(T.tn[:, o:o + L:48], T.tn[:, 0:L:48], colv(14), None, A.subtract, None, T0 + ["colc", "pz"], ["pa"])
-        ts(T.tn[:, o + 42:o + L:48], T.tn[:, 42:L:48], colv(14), -288.0, A.add, A.add, T0 + ["colc", "pz"], ["pb"])
-        ts(T.sc[:, 4:5], colv(13), 32.0, None, A.mult, None, ["colc"], ["sc4"])
-        yield
-        ts(T.tn[:, o + 12:o + L:48], T.tn[:, o + 13:o + L:48], T.sc[:, 4:5], -416.0, A.subtract, A.add, ["sc4", "py0", "py1"], ["pc"])
-        ts(T.tn[:, o + 30:o + L:48], T.tn[:, o + 31:o + L:48], T.sc[:, 4:5], -608.0, A.add, A.add, ["sc4", "py0", "py1"], ["pd"])
-        yield
-        ts(T.la3[:], T.pat[:, 32:40], colv(12), 255.0, A.add, A.min, ["pat2", "colc"], ["la3"])
-        ts(T.ll3[:], T.pat[:, 0:4:2], 8.0, colv(11), A.mult, A.add, ["pat0", "colc"], ["ll3"])
-        yield
-        ts(T.sc[:, 5:6], colv(10), float(32 * M), colv(15), A.mult, A.subtract, ["col", "colc"], ["sc5"])
-        ts(T.sc[:, 6:7], colv(10), float(M), 3.0, A.mult, A.add, ["col"], ["sc6"])
-        yield
-        quant(T.qv[:], T.sv[:], T.vs[:], ["vs"], ["qv"])
-        yield
-        ts(T.ll3[:], T.ll3[:], 63.0, None, A.min, None, ["ll3"], ["ll3"])
-        ts(T.sc[:, 5:6], T.sc[:, 5:6], XE // 2 - 0.5, SC, A.add, A.mult, ["sc5"], ["sc5"])
-        yield
-        ts(T.sc[:, 7:8], colv(10), float(M), 9.0, A.mult, A.add, ["col"], ["sc7"])
-        ts(T.sc[:, 8:9], colv(13), 12.0, None, A.add, None, ["colc"], ["sc8"])
-        yield
-        ts(T.sc[:, 9:10], colv(5), -2.0, colv(10), A.mult, A.add, ["col", "cola"], ["sc9"])
-        ts(T.sc[:, 10:11], colv(10), float(8 * C + 4 * P), None, A.add, None, ["col"], ["sc10"])
-        yield
-        ts(T.sc[:, 9:10], T.sc[:, 9:10], float(8 * C), None, A.add, None, ["sc9"], ["sc9"])
-        yield
-    todo = [lists()]
+    U = side("qu", "su", 0, 128)
+    RUNS = [(0, 4), (8, 14), (4, 8)]
 
-    def spare(k=1):
-        for _ in range(k):
-            next(todo[0], None)
+    def own(c):
+        a, b = RUNS[c]
+        quant("qx", "sx", 32 * a, 32 * b, w(X0 + 128 * a, X0 + 128 * b))
 
-    def keys(c, src, reads):
-        c0, c1 = CH[c]
-        quant(T.qx[:, c0:c1], T.sx[:, c0:c1], src, reads, ["qx%d" % c])
-        if "qu" in wr:
-            score(c)
-
-    def score(c):
-        c0, c1 = CH[c]
-        mm(4 + c, c1 - c0, [(T.qu[:], T.su[:], T.qx[:, c0:c1], T.sx[:, c0:c1])], ["qu", "qx%d" % c])
+    def keys(c):
+        a, b = RUNS[c]
+        mm(4 + c, 32 * (b - a), [(U, side("qx", "sx", 32 * a, 32 * (b - a)))])
 
     def turn(c):
-        c0, c1 = CH[c]
-        tr(T.kt[:, c0:c1], bank(4 + c, c1 - c0), ["ps%d" % (4 + c)], ["kt%d" % c])
-
-    XJ = ["xj%d" % j for j in range(M)]
-
-    def lay(e, j):
-        copy(e, W[:, X0 + 128 * j:X0 + 128 * j + 128], T.x3[:, :, 4 * j:4 * j + 4], ["x3"], [XJ[j]])
-
-    def first(c):
-        c0, c1 = CH[c]
-        keys(c, W[:, X0 + 4 * c0:X0 + 4 * c1], XJ[c0 // 32:c1 // 32])
-    for j in range(9, M):
-        lay("s", j)
-    for j in range(9):
-        lay("v", j)
-    XW0, XW[:] = list(XW), XJ
+        a, b = RUNS[c]
+        tr(at("kt", s_[:, 32 * a:32 * b]), bank(4 + c, 0, 32 * (b - a)))
+    for e, js in (("s", range(4, 9)), ("v", range(0, 4)), ("v", range(9, M))):
+        for j in js:
+            copy(e, w(X0 + 128 * j, X0 + 128 * j + 128), at("xl", s_[:, :, 4 * j:4 * j + 4]))
     windows()
-    dmas("lw", [("y", [], ["qw"], T.qw[:, 16:528].bitcast(u8), T.wc[:]),
-                ("y", [], ["sw"], T.sw[:, 16:528], T.ws[:]),
-                ("y", [], ["qw0"], T.qw[:, 0:16].bitcast(u8), T.wc[:, 0:64]),
-                ("y", [], ["sw0"], T.sw[:, 0:16], T.ws[:, 0:16])])
-    dmas("lv", [("y", [], ["vs"], T.vs[:], T.v[:])])
-    first(0)
-    first(1)
-    quant(T.qu[:], T.su[:], T.us[:], ["us0", "us1"], ["qu"])
-    score(0)
-    score(1)
-    first(2)
-    spare(2)
-    turn(0)
-    turn(1)
-    turn(2)
-    spare()
+    dmas("lw", [("y", at("qw", s_[:, 16:528], True), hbm(T.wc[:])), ("y", at("sw", s_[:, 16:528]), hbm(T.ws[:])),
+                ("y", at("qw", s_[:, 0:16], True), hbm(T.wc[:, 0:64])), ("y", at("sw", s_[:, 0:16]), hbm(T.ws[:, 0:16]))], 5.0)
+    for k in range(2):
+        quant("ql0%d" % k, "sl0%d" % k, KB, KB + 128, at("zt"), 128)
+    own(0)
+    own(1)
+    quant("qu", "su", 0, 128, at("us"))
+    own(2)
+    for c in range(3):
+        keys(c)
+    for a, b in ((0, 160), (160, 224), (224, 320)):
+        tr(at("col", s_[:, a:b]), at("blk", s_[:, a:b]))
+    columns()
+    lists(0)
+    lists(1)
+    for i in range(2):
+        quant("qg", "sg", 128 * i, 128 * i + 128, at("gt", s_[:, 512 * i:512 * i + 512]))
+    for c in range(3):
+        turn(c)
 
     for t in range(R):
         last = t == R - 1
-        down = None if t == 0 else SC
-        KT = ["kt0", "kt1", "kt2"]
-        treg = [T1 if t else 0] + TREG[1:]
 
-        def two(k, n):
-            return ["%s%d%d" % (k, n % 2, h) for h in range(2)]
+        def run(name, n, a, b, step=1, size=L, lo=0, hi=128):
+            o = size * (n % 2)
+            return at(name, s_[lo:hi, o + a:o + b:step])
 
-        def tkeys(n):
+        def gates(n, a, b, step=1, lo=0, hi=128):
+            return run("gy", n, a, b, step, L + 30, lo, hi)
+
+        def largest(n):
             if n:
-                return ["t%d" % n] + ["t%d%s" % (n, k) for k in "abcdef"]
-            return ["py0", "py1", "pa", "pb", "pc", "pd"] if t else T0
-
-        def run(buf, n, h, a, b, step=1, size=L):
-            o = size * (n % 2) + 48 * (1 - h)
-            return buf[:, o + a:o + b:step]
-
-        def gate(n, h, kind):
-            r, m = run(T.rb, n, h, 2, 48, 3), run(T.rb, n, h, 44, 45)
-            key, rk = ["%s%d%d" % (kind, n % 2, h)], ["r%d%d" % (n % 2, h)]
-            if kind == "y":
-                o = 33 * (n % 2) + 17 - 16 * h
-                ts(T.yy[:, o:o + 16], r, m, -BIG, A.is_lt, A.mult, rk, key)
-            elif kind == "z":
-                ts(run(T.dk, n, h, 4, 50, 3, 100), r, m, -BIG, A.is_ge, A.mult, rk, key)
+                scan(run("rb", n, 3, L), at("dr"), run("sq", n - 1, 3, L), -BIG)
             else:
-                ts(run(T.dl, n, h, 3, 46, 3, DL), run(T.rb, n, h, 2, 45, 3), m, None, A.is_ge, None, rk, key)
+                for s in range(2):
+                    scan(run("rb", 0, 45 * s + 5, 45 * s + 45, 3), at("dr", s_[:, 0:M]), at("kt", s_[:, 16 - 16 * s:C:32]), -BIG)
 
-        def latch(n, hs):
-            a, b = (0, L) if len(hs) == 2 else (0, 48) if hs[0] else (48, L + 32)
-            o, d = treg[n], DL * (n % 2)
-            skip = "" if len(hs) == 2 else "ab" if hs[0] else "cdef"
-            scan(T.lb[:, L * n + a:L * n + b], T.dl[:, d + a:d + b], T.tn[:, o + a:o + b], 0.0, A.mult, A.add,
-                 ["st%d%d" % (n % 2, h) for h in hs] + [k for k in tkeys(n) if k[-1] not in skip] + ["tail"],
-                 ["l%d%d" % (n, h) for h in hs])
-
-        def hot(n):
-            if n < V - 1:
-                o = 33 * (n % 2)
-                tt(T.ff[:, 0:32], T.yy[:, o + 1:o + 33], T.yy[:, o:o + 32], A.is_gt, two("y", n), ["f"])
-            else:
-                o = DL * (n % 2)
-                tt(T.ff[:, 0:32], T.dl[:, o + 3:o + 97:3], T.dl[:, o:o + 94:3], A.is_gt, two("st", n), ["f"])
-
-        def edge(n):
-            tt(T.gg[:, 32 * (n % 2):32 * (n % 2) + 32], T.ff[:, 0:32], T.ff[:, 1:33], A.subtract, ["f"], ["g%d_" % (n % 2)])
-
-        def carry(n):
-            o, o1 = treg[n], treg[n + 1]
+        def held(n):
             if n:
-                scan(T.tn[:, o1 - 2:o1 + L - 2], T.dd[:], T.tn[:, o:o + L], 0.0, A.mult, A.add, tkeys(n) + ["dd"], tkeys(n + 1))
-            elif t < 2:
-                copy("v", T.tn[:, o1:o1 + L:3], T.tn[:, o:o + L:3], tkeys(0), ["t1"])
+                scan(run("kb", n, 0, L), run("dk", n - 1, 0, L), run("sq", n - 1, 0, L), -BIG)
+            else:
+                for s in range(2):
+                    copy("s", run("kb", 0, 45 * s + 5, 45 * s + 45, 3), at("kt", s_[:, 16 - 16 * s:C:32]))
 
-        def moved(n, which, e="s"):
-            o1, l0, g0 = TREG[n + 1], L * n, 32 * (n % 2)
-            jobs = {"a": (0, 1, 0, 128, T.lb[:, l0 + 45:l0 + 46], 1), "b": (0, 2, 0, 128, T.lb[:, l0 + 94:l0 + 95], 0),
-                    "c": (1, 1, 0, 64, T.lb[64:128, l0 + 93:l0 + 94], 0), "d": (1, 1, 64, 96, T.lb[32:64, l0 + 93:l0 + 94], 0),
-                    "e": (1, 2, 0, 128, T.lb[:, l0 + 46:l0 + 47], 1), "f": (1, 1, 96, 128, T.wt[96:128, n:n + 1], None)}
-            for k in which:
-                h, slot, lo, hi, col, src = jobs[k]
-                a = o1 + 48 * (1 - h)
-                copy(e, T.tn[lo:hi, a + slot:a + 48:3], T.gg[lo:hi, g0 + 16 - 16 * h:g0 + 32 - 16 * h],
-                     ["g%d_" % (n % 2), ("wt5" if n > 3 else "wt") if src is None else "l%d%d" % (n, src)], ["t%d%s" % (n + 1, k)], col)
+        def before(n, s):
+            ts(gates(n, 45 * s + 3, 45 * s + 48, 3), run("rb", n, 45 * s + 2, 45 * s + 45, 3), run("rb", n, 45 * s + 44, 45 * s + 45),
+               A.is_lt, -BIG, A.mult)
+
+        def after(n, s):
+            ts(gates(n, 45 * s + 5, 45 * s + 48, 3), run("rb", n, 45 * s + 2, 45 * s + 45, 3), run("rb", n, 45 * s + 44, 45 * s + 45),
+               A.is_ge, -BIG / 2, A.mult)
+
+        def strike(n, k):
+            tt(run("sq", n, k, L, 3), run("kb", n, 2, L, 3), gates(n, 5 * k - 5, L + 3 * k - 3, 3), A.add)
 
         def enter(n):
-            o, y0 = L * (n % 2), 33 * (n % 2) + 17
-            for k, h, lo, hi, col, src in (("b", 1, 0, 64, T.rb[64:128, o + 92:o + 93], 0), ("c", 1, 64, 96, T.rb[32:64, o + 92:o + 93], 0),
-                                           ("a", 0, 0, 128, T.rb[:, o + 44:o + 45], 1)):
-                a = o + 48 * (1 - h)
-                out, in_ = T.sq[lo:hi, a:a + 48:3], T.yy[lo:hi, y0 - 16 * h:y0 - 16 * h + 16]
-                do("s", ["y%d%d" % (n % 2, h), "r%d%d" % (n % 2, src)], ["s%d%s" % (n % 2, k)],
-                   lambda: act.activation(out, in_, AF.Identity, bias=col))
+            for s, lo, hi, fr in ((0, 0, 64, 64), (0, 64, 96, 32), (1, 0, 128, 0)):
+                copy("s", run("sq", n, 45 * s + 3, 45 * s + 45, 3, L, lo, hi), gates(n, 45 * s + 6, 45 * s + 48, 3, lo, hi),
+                     bias=run("rb", n, 89 - 45 * s, 90 - 45 * s, 1, L, fr, fr + hi - lo))
+            copy("s", run("dk", n, 4, L, 3), gates(n, 5, L, 3))
 
-        for n in range(V):
-            o, oq, pr = L * (n % 2), L * (1 - n % 2), n % 2
-            SK = ["s%d%s" % (1 - pr, k) for k in "abcAC"] + ["si"]
-            if n == 0:
-                for h in (1, 0):
-                    scan(run(T.rb, 0, h, 5, 45, 3), T.dr[:, 1:15], T.kt[:, 16 * h:C:32], -BIG, A.add, A.max, KT + ["dr"], ["r0%d" % h])
-                for h in range(2):
-                    copy("s", run(T.kb, 0, h, 5, 45, 3), T.kt[:, 16 * h:C:32], KT, ["k0%d" % h])
-                if t:
-                    pad(t)
-                else:
-                    spare()
-            else:
-                scan(T.rb[:, o:o + L], T.dr[:], T.sq[:, oq:oq + L], -BIG, A.add, A.max, SK + ["dr"], two("r", n))
-                latch(n - 1, [0, 1])
-                if n < V - 1:
-                    scan(T.kb[:, o:o + L], T.dk[:, 100 * (1 - pr):100 * (1 - pr) + L], T.sq[:, oq:oq + L], -BIG, A.add, A.max,
-                         SK + two("z", n - 1), two("k", n))
-            if n == V - 1:
-                break
-            if n:
-                moved(n - 1, "acd")
-            gate(n, 1, "y")
-            gate(n, 0, "y")
+        def origin(n, a, b, step=1):
+            o = 120 if n else 0
+            return at("tl", s_[:, o + a:o + b:step])
+
+        def leave(n, a=0, b=L):
+            scan(at("lb", s_[:, L * n + a:L * n + b]), gates(n, a, b), origin(n, a, b), 0.0)
+
+        def mark(n):
+            tt(at("fz"), gates(n, 0, L, 3), gates(n, 3, L + 3, 3), A.subtract)
+
+        def come(n):
+            tt(at("s1"), origin(n, 0, L, 3), at("fz"), A.subtract)
+            for s, lo, hi, fr in ((0, 96, 128, None), (1, 0, 128, 0), (0, 0, 64, 64), (0, 64, 96, 32)):
+                c = L * n + 89 - 45 * s
+                copy("s", at("s0", s_[lo:hi, G * s:G * s + G]), at("fz", s_[lo:hi, G * s:G * s + G]), 0.5,
+                     at("wt", s_[96:128, n:n + 1]) if fr is None else at("lb", s_[fr:fr + hi - lo, c:c + 1]))
+
+        def merge(n, a=0, b=2 * G):
+            tt(origin(n + 1, 3 * a, 3 * b, 3), at("s1", s_[:, a:b]), at("s0", s_[:, a:b]), A.min)
+
+        def final(a):
+            q0 = 32 * QUAD[a]
+            tt(at("tf", s_[32 * a:32 * a + 32, 0:30]), at("s1", s_[q0:q0 + 32]), at("s0", s_[q0:q0 + 32]), A.min)
+
+        def drawn(k, in_):
+            for a in range(2):
+                tr(at("tb", s_[32 * a:32 * a + 32, 32 * k:32 * k + 32]), in_)
+
+        for n in range(V - 1):
+            largest(n)
+            held(n)
+            for gate in (before, after):
+                for s in range(2):
+                    gate(n, s)
+            rows.update(range(len(jobs) - 3, len(jobs)))
             enter(n)
-            gate(n, 0, "z")
-            gate(n, 1, "z")
-            if n:
-                moved(n - 1, "be", "v")
-            else:
-                spare()
-            hot(n)
-            kk = T.kb[:, o + 2:o + L:3]
-            tt(T.sq[:, o + 1:o + L:3], kk, T.yy[:, 33 * pr:33 * pr + 32], A.add, two("k", n) + two("y", n), ["s%dA" % pr])
-            tt(T.sq[:, o + 2:o + L:3], kk, T.dk[:, 100 * pr + 4:100 * pr + 98:3], A.add, two("k", n) + two("z", n), ["s%dC" % pr])
-            copy("s", T.dl[:, DL * pr + 3:DL * pr + 94:3], T.dk[:, 100 * pr + 4:100 * pr + 95:3], two("z", n), two("st", n), -1.0 / BIG)
-            if n == 0:
-                spare()
-            carry(n)
-            edge(n)
-            moved(n, "f")
+            strike(n, 1)
+            strike(n, 2)
+            mark(n)
+            leave(n)
+            come(n)
+            if n < V - 2:
+                merge(n)
         n = V - 1
-        wb = W[:, 0:9 * XE]
-        moved(n - 1, "acd")
-        gate(n, 0, "st")
-        moved(n - 1, "b", "v")
-        tt(T.bx[:], T.lb[:, 0:L * n].indirect(T.lbx[:]), T.tq[:], A.add,
-           [k % m for m in range(n) for k in ("l%d0", "l%d1")] + ["lbx", "lbx2", "tq0", "tq1"], ["bx"])
-        gate(n, 1, "st")
-        latch(n, [0])
-        moved(n - 1, "e", "v")
-        tr(T.tb[0:32, 0:64], T.bx[0:32, :], ["bx"], ["tba"])
-        tr(T.tb[32:64, 0:64], T.bx[0:32, :], ["bx"], ["tbb"])
-        hot(n)
-        tr(T.tb[0:32, 72:104], T.lb[0:32, V * L:V * L + 32], ["l50"], ["tbc"])
-        tr(T.tb[32:64, 72:104], T.lb[0:32, V * L:V * L + 32], ["l50"], ["tbd"])
-        latch(n, [1])
-        ts(T.offb[:], T.tb[:, 0:65].indirect(T.lbs[:, 0:1]), T.sc[:, 1:2], None, A.add, None,
-           ["tba", "tbb", "tb64", "lbs", "lbs2", "sc1"], ["offb"])
-        edge(n)
-        ts(T.offc[:], T.tb[:, 0:104].indirect(T.lbl[:, 0:1]), T.sc[:, 1:2], None, A.add, None,
-           ["tba", "tbb", "tbc", "tbd", "tb64", "lbl", "lbl2", "sc1"], ["offc"])
-        carry(n)
-        for e, k, dst in (("v", 0, T.bt), ("s", 1, T.bu)):
-            copy(e, dst[:, 0:128], wb.indirect(T.offb[:, 8 * k:8 * k + 8]), XW + WB + ["offb"], ["be%d" % k] + ["bh"][k:], down)
-        for e, k in (("v", 0), ("s", 1)):
-            copy(e, T.bl[:, 64 * k:64 * k + 64], wb.indirect(T.offc[:, 4 * k:4 * k + 4]), XW + WB + ["offc"], ["bl%d" % k], down)
-        moved(n, "bea", "v")
-        moved(n, "cdf")
-        copy("s", T.bt[64:128, 64:128], T.bu[0:64, 64:128], ["be1"], ["bh"])
-        copy("s", T.bt[64:128, 128:144], T.bu[0:64, 0:64:4], ["be1"], ["b41"])
-        copy("v", T.bt[0:64, 128:144], T.bt[0:64, 0:64:4], ["be0"], ["b40"])
-        for k in range(2):
-            copy("v", T.bt[64 * k:64 * k + 64, 144:160], T.bl[0:64, 64 * k:64 * k + 64:4], ["bl%d" % k], ["b5%d" % k])
-        if t == 0:
-            rest()
-        o = TREG[V]
-        scan(T.of[:, 1:L + 1], T.df[:], T.tn[:, o:o + L], 0.0, A.mult, A.subtract, tkeys(V) + ["df", "ofi"], ["o6"])
-        quant(T.qb[:], T.sb[:, 128:256], T.bt[:, 64:576], ["be0", "bh", "b40", "b41", "b50", "b51", "btz"], ["qb"])
-        if t == 0:
-            spare()
-        of = slice(0, L, 3)
-        o6 = T.of[:, of]
+        o = L * n
+        largest(n)
+        copy("v", at("bx"), pick(at("lb", s_[:, 0:2 * L]), at("lbx")))
+        for k in range(3):
+            copy("s", at("lb", s_[0:32, o + 112 + 4 * k:o + 116 + 4 * k]), at("zt", s_[0:32, 0:4]), bias=at("lb", s_[0:32, o - L * k - 1:o - L * k]))
+        for s in range(2):
+            before(n, s)
+            after(n, s)
+        merge(n - 1, 0, G)
+        merge(n - 1, G, 2 * G)
+        leave(n, 48, L + 22)
+        mark(n)
+        leave(n, 0, 45)
+        come(n)
         for a in range(4):
-            tr(T.t1[32 * a:32 * a + 32, 0:32], T.of[32 * QUAD[a]:32 * QUAD[a] + 32, of], ["o6"], ["t1%d" % a])
-        if t == 0:
-            spare()
+            final(a)
+
+        drawn(0, at("bx", s_[0:32]))
+        drawn(1, at("lb", s_[0:32, o + 108:o + 140]))
+        drawn(2, at("lb", s_[0:32, o + 92:o + 124]))
+        wb = w(0, 9 * XE)
         peer = T.cores[(rank + t + 1) % N]
         rid, pid = topo.addr(peer)[0:2]
         es = topo.engines(core, peer)
         half = len(es) // 2
         masks = [sum(1 << k for k in es[:half]), sum(1 << k for k in es[half:])]
-        ql, sl, arr = T["ql%d" % t], T["sl%d" % t], "arr%d" % t
-        order("g", ["qb"], [])
-        g.remote_dma_fused([
-            RemoteDMATransfer(dst_ids=[DstId(rid=rid, pnc=pid)], dma_engine_mask=masks[0], remote_sem=S[arr],
-                              src=T.qb[:, 0:KB].bitcast(u8), dst=ql[:, 0:KB].bitcast(u8)),
-            RemoteDMATransfer(dst_ids=[DstId(rid=rid, pnc=pid)], dma_engine_mask=masks[1], remote_sem=S[arr],
-                              src=T.sb[:, 128 - 3 * KB:128 + KB], dst=sl[:, 0:4 * KB])], local_sem=S.sent)
-        count["sent"] = count.get("sent", 0) + 2 * half
-        note("g", ("sent", count["sent"]), ["qb"], [])
-        count[arr] = 2 * (len(topo.engines(T.cores[(rank - t - 1) % N], core)) // 2)
-        wr["land%d" % t] = (arr, count[arr])
+        for k in range(2):
+            ts(at("offb", s_[:, 16 * k:16 * k + 16]), pick(at("tb", s_[:, 32 * k:64 * k + 32]), at("lbs", s_[:, 2 * k:2 * k + 1])),
+               sc(4), A.mult, sc(5), A.add)
+            if k:
+                for h in range(2):
+                    copy("sv"[h], at("bt", s_[:, 64 * h:64 * h + 64]), pick(wb, at("offb", s_[:, 16 + 4 * h:20 + 4 * h])))
+            else:
+                copy("s", at("bt", s_[:, 128:256]), pick(w(0, 5 * XE), at("offb", s_[:, 0:8])))
+            quant("qb", "sb", 128 * k, 128 * k + 128, at("bt", s_[:, 128 - 128 * k:640 - 128 * k]), 128 * k + 128)
+            ql, sl, arr, sent = "ql%d%d" % (t, k), "sl%d%d" % (t, k), "arr%d%d" % (t, k), "sent%d" % k
+            src = [at("qb", s_[:, 128 * k:128 * k + KB], True), at("sb", s_[:, 128 * k + KB:128 * k + 128 + KB])]
+            dst = [at(ql, s_[:, 0:KB], True), at(sl, s_[:, 0:128])]
+            writes = [RemoteDMATransfer(dst_ids=[DstId(rid=rid, pnc=pid)], dma_engine_mask=masks[i], remote_sem=S[arr],
+                                        src=src[i][0], dst=dst[i][0]) for i in range(2)]
+            count[sent] = count.get(sent, 0) + 2 * half
+            job("g", [], src, lambda writes=writes, sent=sent: g.remote_dma_fused(writes, local_sem=S[sent]), 0.0, "sent", (sent, count[sent]))
+            count[arr] = 2 * (len(topo.engines(T.cores[(rank - t - 1) % N], core)) // 2)
+            job("g", dst, [], lambda: None, 0.0, "late" if k else "early" if t else "first", (arr, count[arr]))
+            for i in range(2):
+                mm(4 * k + i, 128, [(side("qg", "sg", 128 * i, 128), side(ql, sl, 0, 128, 128 - KB))])
+                for b in range(2):
+                    for h in range(2):
+                        o = 512 * (4 * k + i) + 16 * h
+                        copy("vs"[i], at("dtl", s_[64 * h:64 * h + 64, 64 * k + 2 * i + b:64 * k + 64:4]),
+                             at("ps", s_[64 * b:64 * b + 64, o:o + 16]))
+        tt(at("ex", s_[:, 96:128]), pick(at("tf", s_[:, 0:30]), at("lex", s_[:, 6:8])), at("mk", s_[:, 32 * last:32 * last + 32]), A.subtract)
+        copy("s", at("ex", s_[:, 0:96]), pick(at("tf", s_[:, 0:30]), at("lex", s_[:, 0:6])))
 
-        chunks = CL if last else CH
-        tt(T.a2[:], T.t1[:, 0:32].indirect(T.la1[:]), T.tc[:], A.add, ["t1%d" % a for a in range(4)] + ["la1", "tc"], ["a2"])
-        if t == 0:
-            spare()
-        for a in range(3):
-            tr(T.t1[32 * a:32 * a + 32, 32:64], T.of[96:128, of], ["o6"], ["t7%d" % a])
-        tr(T.a3[:], T.a2[:], ["a2"], ["a3"])
-        if t == 0:
-            spare()
-        tt(T.l2[:], T.t1[:].indirect(T.ll1[:]), T.tc[:, 0:64], A.add,
-           ["t1%d" % a for a in range(4)] + ["t7%d" % a for a in range(3)] + ["ll1a", "ll1b", "tc"], ["l2"])
+        r0 = 1 if last else 0
+        tr(at("a3", s_[:, 2 * r0:2 * r0 + 8]), at("ex"))
         if last:
-            ts(T.offz[:], T.a3[:].indirect(T.la3[:]), T.sc[:, 0:1], None, A.add, None, ["a3", "la3", "sc0"], ["offz"])
+            tt(at("a3", s_[:, 1]), at("a3", s_[:, 8:10, 0]), at("a3", s_[:, 8:10, 1]), A.max)
+            ts(at("offz", s_[:, 0:48]), at("a3", s_[:, 2:7:2]), sc(2), A.mult, sc(3), A.add)
+            ts(at("offz", s_[:, 48:112]), at("a3", s_[:, 1:8:2]), sc(2), A.mult, sc(3), A.add)
         else:
-            ts(T.offz[:, 0:112], T.a3[:].indirect(T.la2[:, 0:7]), T.sc[:, 0:1], None, A.add, None, ["a3", "la2", "sc0"], ["offz"])
-        wz = W[:, X0:X0 + 7 * XE]
-        ZE = ["ze%d" % k for k in range(56)]
-        ZP = [["zp%d%d" % (c, a) for a in range(4)] for c in range(3)]
+            tt(at("a3", s_[:, 6]), at("a3", s_[:, 6]), at("a3", s_[:, 7]), A.max)
+            ts(at("offz", s_[:, 0:96]), at("a3", s_[:, 0:6]), sc(2), A.mult, sc(3), A.add)
+            ts(at("offz", s_[:, 96:112]), at("a3", s_[:, 6]), sc(2), A.mult, sc(3), A.add)
+        for a in range(4):
+            copy("s", at("stg", s_[32 * a:32 * a + 32]), at("a3", s_[96:128, r0:r0 + 7, :, 2 * a:2 * a + 2]))
+        wz = w(X0, X0 + 7 * XE)
 
-        def early(e, c0, c1):
-            f0 = c0 // 56 * 16 + c0 % 56 // 4 if last else c0 // 4
-            copy(e, T.zz[:, 4 * c0:4 * c1], wz.indirect(T.offz[:, f0:f0 + (c1 - c0) // 4]), XW + WZ + ["offz"], ZE[c0 // 8:c1 // 8], down)
-
-        def numbers():
-            ts(T.g1[:], o6, float(8 * XE - 1), 0.5 - XE // 2, A.min, A.add, ["o6"], ["g1"])
-            ts(T.g5[:], o6, 8.0, colv(8), A.mult, A.add, ["o6", "col"], ["g5"])
-            ts(T.g8[:], o6, 2.0, T.sc[:, 9:10], A.mult, A.add, ["o6", "sc9"], ["g8"])
-            yield
-            ts(T.g2[:], T.g1[:], 1.0 / XE, WHOLE, A.mult, A.add, ["g1"], ["g2"])
-            ts(T.g4[:], T.g1[:], SC, T.sc[:, 5:6], A.mult, A.add, ["g1", "sc5"], ["g4"])
-            ts(T.g8[:], T.g8[:], T.sc[:, 10:11], None, A.max, None, ["g8", "sc10"], ["g8"])
-            yield
-            ts(T.g3[:], T.g2[:], -WHOLE, -56.0, A.add, A.mult, ["g2"], ["g3"])
-            ts(T.g7[:], T.g2[:], -WHOLE, float(C), A.add, A.mult, ["g2"], ["g7"])
-            yield
-            tt(T.g3[:], T.g3[:], T.g4[:], A.add, ["g3", "g4"], ["g3"])
-            tt(T.g5[:], T.g5[:], T.g8[:], A.min, ["g5", "g8"], ["g5"])
-            yield
-            ts(T.g1[:], T.g3[:], T.sc[:, 6:7], None, A.min, None, ["g3", "sc6"], ["g1"])
-            ts(T.g2[:], T.g3[:], T.sc[:, 8:9], T.sc[:, 7:8], A.subtract, A.min, ["g3", "sc7", "sc8"], ["g2"])
-            ts(T.g4[:], T.g3[:], -30.0, None, A.add, None, ["g3"], ["g4"])
-            yield
-            tt(T.g1[:], T.g1[:], T.g2[:], A.max, ["g1", "g2"], ["g1"])
-            yield
-            tt(T.g1[:], T.g1[:], T.g4[:], A.max, ["g1", "g4"], ["g1"])
-            yield
-            tt(T.g1[:], T.g1[:], T.g7[:], A.add, ["g1", "g7"], ["g1"])
-            yield
-            tt(T.g6[:], T.g1[:], T.g5[:], A.max, ["g1", "g5"], ["g6"])
-            dmas("og", [("y", ["g6"], [], T.og[2 * a + h:2 * a + h + 1, :], T.g6[32 * QUAD[a]:32 * QUAD[a] + 32, 17 - 16 * h:31 - 16 * h])
-                        for a in range(4) for h in range(2)])
-            yield
+        def early(e, a, b):
+            for r in range(a, b):
+                copy(e, at("zz", s_[:, r]), pick(wz, at("offz", s_[:, 8 * r:8 * r + 8])))
+        early("s", 0, 9)
+        early("v", 9, 14)
         if last:
-            todo[0] = numbers()
-        cuts = list(range(0, 337, 56)) + [352] if last else [0, 128, 352]
-        for c0, c1 in zip(cuts, cuts[1:]):
-            early("s", c0, c1)
-        tr(T.l3[:], T.l2[:], ["l2"], ["l3"])
-        if t == 0:
-            pad(0)
-        spare(4 if t == 0 else 1)
-
-        for b in range(4):
-            mm(4 + b, 128, [(T.qg[:, 128 * b:128 * b + 128], T.sg[:, 128 * b:128 * b + 128], ql[:, 0:128], sl[:, 3 * KB:3 * KB + 128])],
-               ["qg%d" % b, "land%d" % t, "pad%d" % t])
-        for b in range(4):
-            copy("v", T.dtl[:, 4 * KB + b:8 * KB:4], bank(4 + b, KB), ["ps%d" % (4 + b)], ["d%d_" % b])
-        ts(T.offl[:], T.l3[:].indirect((T.ll3 if last else T.ll2)[:]), T.sc[:, 0:1], None, A.add, None, ["l3", "ll3" if last else "ll2", "sc0"], ["offl"])
-        spare()
-        quant(T.qd[:], T.sd[:], T.dtl[:], ["d%d_" % b for b in range(4)] + ["dz0", "dz1"], ["qd"])
-        for b in range(4):
-            lo, hi = 16 + 128 * b, 128 * b
-            mm(b, 128, [(T.qw[:, lo:lo + 128], T.sw[:, lo:lo + 128], T.qd[:, KB:KB + 128], T.sd[:, KB:KB + 128]),
-                        (T.qw[:, hi:hi + 128], T.sw[:, hi:hi + 128], T.qd[:, 0:128], T.sd[:, 0:128])], WK + ["qd"])
-        if last:
-            early("v", 352, 392)
-        early("v", 392 if last else 352, C)
-        spare()
-        for b in range(4):
-            copy("v", W[:, HB + b:HB + 8 * KB:4], bank(b, 2 * KB), ["ps%d" % b], ["h%d" % b], SC if t == 0 else None)
-            if b == 3 or last and b == 1:
-                spare()
-        wl = W[:, X0:HB + 8 * KB]
-        LR = XW + WZ + ["w7", "offl"] + ["h%d" % b for b in range(4)]
-        if t == 0:
-            XW[:] = XW0
-            for k in XW:
-                wr[k] = wr["h3"]
-                rd[k] = []
-            OLD = XJ
+            ts(at("offl", s_[:, 0:12]), at("stg", s_[:, 1:6:2]), 1 / TS, A.mult, col(0), A.add)
+            ts(at("offl", s_[:, 12:28]), at("stg", s_[:, 0:7:2]), 1 / TS, A.mult, col(0), A.add)
         else:
-            OLD = []
+            ts(at("offl"), at("stg"), 1 / TS, A.mult, col(0), A.add)
 
-        def late(e, c):
-            c0, c1 = chunks[c]
-            f0 = 16 * c if last else c0 // 16
-            copy(e, T.lt[:, c0:c1], wl.indirect(T.offl[:, f0:f0 + (c1 - c0) // 16]), LR, ["lt%d" % c], down)
+        quant("qd", "sd", KB, KB + 128, at("dtl"))
+        if t == 0:
+            job("y", [], [at("qd")], lambda: None, 0.0, 0.0, ("lx", 0))
+            dmas("lp", [x for r in range(1, R) for k in range(2) for x in (
+                ("y", at("ql%d%d" % (r, k), s_[:, KB:128], True), at("qn", s_[:, 0:128 - KB], True)),
+                ("y", at("sl%d%d" % (r, k), s_[:, 128:256 - KB]), at("sb", s_[:, 0:128 - KB])))], 3.0)
+            dmas("lv", [("y", at("vs"), hbm(T.v[:]))], 3.0)
+        for b in range(4):
+            mm(b, 128, [(side("qw", "sw", 16 + 128 * b, 128), side("qd", "sd", KB, 128)),
+                        (side("qw", "sw", 128 * b, 128), side("qd", "sd", 0, 128))])
+        for b in range(4):
+            copy("vvsv"[b], w(HB + b, HB + 8 * KB, 4), bank(b, 0, 2 * KB), SC)
 
-        def place(e, c, a):
-            c0, c1 = chunks[c]
-            z0 = 4 * c0 + a * (c1 - c0)
-            copy(e, T.zz[96:128, z0:z0 + c1 - c0], T.lt[32 * a:32 * a + 32, c0:c1], ["lt%d" % c] + ZE[c0 // 8:c1 // 8], [ZP[c][a]])
+        chunks = [(0, 4), (4, 10), (10, 14)] if last else RUNS
+        wl = w(X0, HB + 8 * KB)
 
-        def layer(c):
-            c0, c1 = chunks[c]
-            zk = ZE[c0 // 8:c1 // 8] + ZP[c]
-            quant(T.qz[:, c0:c1], T.sz[:, c0:c1], T.zz[:, 4 * c0:4 * c1], zk, ["qz%d" % c])
-            for b in range(4):
-                lo = 16 + 128 * b
-                mm(4 * (c % 2) + b, c1 - c0, [(T.qw[:, lo:lo + 128], T.sw[:, lo:lo + 128], T.qz[:, c0:c1], T.sz[:, c0:c1])],
-                   WK + ["qz%d" % c])
+        def late(es, c):
+            a, b = chunks[c]
+            for k, e in enumerate(es):
+                a1, b1 = a + k * (b - a) // len(es), a + (k + 1) * (b - a) // len(es)
+                copy(e, at("lt", s_[:, 32 * a1:32 * b1]), pick(wl, at("offl", s_[:, 2 * a1:2 * b1])))
+
+        def place(es, c):
+            a, b = chunks[c]
+            for k, e in enumerate(es):
+                if e != "-":
+                    copy(e, at("zz", s_[96:128, a:b, 32 * k:32 * k + 32]), at("lt", s_[32 * k:32 * k + 32, 32 * a:32 * b]))
+
+        def codes(c):
+            a, b = chunks[c]
+            quant("qz", "sz", 32 * a, 32 * b, at("zz", s_[:, a:b]))
+            for k in range(4):
+                mm(4 * (c % 2) + k, 32 * (b - a), [(side("qw", "sw", 16 + 128 * k, 128), side("qz", "sz", 32 * a, 32 * (b - a)))])
 
         def times32(c):
-            c0, c1 = chunks[c]
-            for b in range(4):
-                copy("s", T.z32[:, 4 * c0 + b:4 * c1:4], T.zz[:, 4 * c0 + b:4 * c1:4], ZE[c0 // 8:c1 // 8] + ZP[c], ["z32%d%d" % (c, b)], 32.0)
+            a, b = chunks[c]
+            for k in range(4):
+                copy("s", at("z32", s_[:, 128 * a + k:128 * b:4]), at("zz", s_[:, a:b, k:128:4]), 32.0)
 
         def state(c):
-            c0, c1 = chunks[c]
-            order("v", [], OLD)
-            for b in range(4):
-                out = T.x32[:, c0 // 4:c1 // 4, b:16:4] if last else W[:, X0 + 4 * c0 + b:X0 + 4 * c1:4]
-                k = 4 * (c % 2) + b
-                tt(out, bank(k, c1 - c0), T.z32[:, 4 * c0 + b:4 * c1:4], A.add, ["ps%d" % k, "z32%d%d" % (c, b)],
-                   ["o%d%d" % (c, b)] if last else [XW[4 * c + b]])
+            a, b = chunks[c]
+            for k in range(4):
+                tt(at("xs", s_[:, 8 * a:8 * b, k:16:4]), bank(4 * (c % 2) + k, 0, 32 * (b - a)), at("z32", s_[:, 128 * a + k:128 * b:4]), A.add)
 
-        def scaled(es, c):
-            c0, c1 = chunks[c]
-            for a, e in enumerate(es):
-                if e == "-":
-                    continue
-                z0 = X0 + 4 * c0 + a * (c1 - c0)
-                copy(e, T.xk[:, c0 // 8:c1 // 8, 8 * a:8 * a + 8], W[:, z0:z0 + c1 - c0], XW[4 * c:4 * c + 4], ["xk%d%d" % (c, a)], SC)
-
-        def rekey(c):
-            c0, c1 = chunks[c]
-            keys(c, T.xk[:, c0 // 8:c1 // 8], ["xk%d%d" % (c, a) for a in range(4)])
-        late("v", 0)
-        spare()
-        late("s", 1)
+        def scaled(e, j):
+            o = X0 + 128 * j
+            if j < 12:
+                copy(e, w(o, o + 128), at("xs", s_[:, j // 4 * 32:j // 4 * 32 + 32, j % 4 * 4:j % 4 * 4 + 4]), SC)
+            else:
+                for x in range(2):
+                    k = 8 * x + 4 * (j - 12)
+                    copy(e, w(o + 64 * x, o + 64 * x + 64), at("xs", s_[:, 96:112, k:k + 4]), SC)
+        for c in range(len(chunks)):
+            late(("vs", "sv", "s")[c], c)
+            place(("vvvs", "vvvv", "vvvv")[c], c)
+            codes(c)
+            times32(c)
+            state(c)
         if not last:
-            late("s", 2)
-            for a in range(4):
-                place("v", 0, a)
-            for a in range(4):
-                place("v" if a < 2 else "s", 1, a)
-            for a in range(2):
-                place("v", 2, a)
-            times32(0)
-            layer(0)
-            for a in range(2, 4):
-                place("v", 2, a)
-            times32(1)
-            layer(1)
-            times32(2)
-            c0, c1 = chunks[2]
-            quant(T.qz[:, c0:c1], T.sz[:, c0:c1], T.zz[:, 4 * c0:4 * c1], ZE[c0 // 8:c1 // 8] + ZP[2], ["qz2"])
-            state(0)
-            for b in range(4):
-                lo = 16 + 128 * b
-                mm(b, c1 - c0, [(T.qw[:, lo:lo + 128], T.sw[:, lo:lo + 128], T.qz[:, c0:c1], T.sz[:, c0:c1])], WK + ["qz2"])
-            scaled("ssss", 0)
-            state(1)
-            scaled("ss--", 1)
-            state(2)
+            for j in (0, 1, 2, 3, 10, 11, 12, 13, 6):
+                scaled("s", j)
+            first = len(jobs)
+            own(0)
+            for j in (8, 9, 4, 5, 7):
+                scaled("v", j)
+            own(1)
+            own(2)
+            rows.update(range(first, len(jobs)))
             windows()
-            scaled("--vv", 1)
-            rekey(0)
-            scaled("vvvs", 2)
-            rekey(1)
-            rekey(2)
-            turn(0)
-            turn(1)
-            turn(2)
+            for c in range(3):
+                keys(c)
+            if t == 0:
+                copy("s", sc(8), col(8), -1.0 / C, -6.5 / M)
+                copy("s", sc(9), col(8), M - SC)
+                copy("s", sc(10), col(4), -8.0, col(8))
+                copy("s", sc(11), col(4), 8.0, col(8))
+                copy("s", sc(10), sc(10), bias=8.0 * C)
+                copy("s", sc(11), sc(11), bias=8.0 * C + 21 * P)
+            else:
+                quant("qv", "sv", 0, 128, at("vs"))
+            for c in range(3):
+                turn(c)
 
-    def unlay(e, c, j):
-        copy(e, T.xl[:, 2 * c + j // 2, :, j % 2, :], T.x32[:, 56 * c:56 * c + 56, 4 * j:4 * j + 4],
-             ["o%d%d" % (c, b) for b in range(4)], ["xl%d%d" % (c, j)], SC)
+    def small(name):
+        return at(name, s_[:, 0:30])
+    copy("s", small("g3"), small("tf"), 1 / (128 * TS))
+    copy("s", small("g4"), small("tf"), 8 / TS, sc(10))
+    copy("s", small("g6"), small("tf"), -8 / TS, sc(11))
+    ts(small("g1"), small("tf"), 1 / (XE * TS), A.mult, sc(8), A.add)
 
-    def result(c):
-        c0 = 224 * c
-        quant(T.qx[:, c0:c0 + 224], T.sx[:, c0:c0 + 224], T.xl[:, 2 * c:2 * c + 2], ["xl%d%d" % (c, j) for j in range(4)], ["qx0", "qx1", "qx2"][c:])
-        mm(4 * c, 224, [(T.qv[:], T.sv[:], T.qx[:, c0:c0 + 224], T.sx[:, c0:c0 + 224])], ["qv", "qx%d" % c])
-    for a in range(4):
-        place("v", 0, a)
-    place("s", 1, 3)
-    place("v", 1, 0)
-    place("v", 1, 1)
-    times32(0)
-    layer(0)
-    place("v", 1, 2)
-    spare()
-    times32(1)
-    layer(1)
-    spare()
-    state(0)
-    for j in range(4):
-        unlay("s", 0, j)
-    state(1)
-    spare()
-    for j in range(4):
-        unlay("v" if j < 3 else "s", 1, j)
-    result(0)
-    wr["qx1"] = wr["qx2"] = wr["xl00"]
-    result(1)
-    copy("v", T.ys[:, 0:224], bank(0, 224), ["ps0"], ["ys0"])
-    copy("v", T.ys[:, 224:448], bank(4, 224), ["ps4"], ["ys1"])
-    dmas("out", [("y", ["qx0"], [], T.oc[:, 0:896], T.qx[:, 0:224].bitcast(u8)),
-                 ("s", ["qx1"], [], T.oc[:, 896:XE], T.qx[:, 224:C].bitcast(u8))]
-         + [("s", ["qx0", "qx1"], [], T.osc[4 * k:4 * k + 4, :], T.sx[32 * k:32 * k + 4, :]) for k in range(4)]
-         + [("y", ["ys0"], [], T.y[:, 0:224], T.ys[:, 0:224]), ("y", ["ys1"], [], T.y[:, 224:C], T.ys[:, 224:C])])
-    for k in count:
-        wait("y", (k, count[k]))
+    def unlay(es, p0, n, u0):
+        for k in range(3):
+            copy(es[k], at("xl", s_[:, p0:p0 + n, 16 * k:16 * k + 16]), at("xs", s_[:, u0 + n * k:u0 + n * k + n]), SC)
+        for q in range(p0 // 8, (p0 + n) // 8):
+            copy(es[3], at("xl", s_[:, 8 * q:8 * q + 8, 48:56]), at("xs", s_[:, 48 + q // 2 * 8:56 + q // 2 * 8, q % 2 * 8:q % 2 * 8 + 8]), SC)
+
+    def result(e, c):
+        quant("qx", "sx", 224 * c, 224 * c + 224, at("xl", s_[:, 16 * c:16 * c + 16]))
+        mm(4 + c, 224, [(side("qv", "sv", 0, 128), side("qx", "sx", 224 * c, 224))])
+        copy(e, at("ys", s_[:, 224 * c:224 * c + 224]), bank(4 + c, 0, 224))
+    ts(small("g2"), small("g1"), float(C - M), A.mult, sc(9), A.add)
+    tt(small("g2"), small("g2"), small("g3"), A.add)
+    ts(small("g2"), small("g2"), 8.0 * C - 1, A.min)
+    tt(small("g4"), small("g4"), small("g6"), A.min)
+    tt(small("g5"), small("g2"), small("g4"), A.max)
+    dmas("og", [("y", hbm(T.og[1 - s:8:2, :]), at("g5", s_[:, G * s + 1:G * s + G])) for s in range(2)], 3.0)
+    unlay("ssss", 0, 16, 0)
+    unlay("vvsv", 16, 16, 64)
+    for c in range(2):
+        result("sv"[c], c)
+    dmas("out", [("y", hbm(T.oc[:, 0:896]), at("qx", s_[:, 0:224], True)),
+                 ("s", hbm(T.y[:, 0:224]), at("ys", s_[:, 0:224]))], 1.0)
+    dmas("end", [("y", hbm(T.oc[:, 896:XE]), at("qx", s_[:, 224:C], True))]
+         + [("y", hbm(T.osc[4 * k:4 * k + 4, :]), at("sx", s_[32 * k:32 * k + 4])) for k in range(4)]
+         + [("y", hbm(T.y[:, 224:C]), at("ys", s_[:, 224:C]))], 1.0)
+    issue()

@@ -11,38 +11,46 @@ X0 = 3 * XE
 HB = 11 * XE
 KB = 32
 BIG = float(2 ** 96)
-TS = float(2 ** 80)
+TS = 2.0 ** -16
 SC = 0.03125
-G = 15
+G = 16
 L = 6 * G
+APART = 0
+LT = L + 24
 QUAD = [0, 2, 1, 3]
+EIGHTS = [(0, 4, 0, 0), (4, 7, 2, 1), (7, 11, 1, 0), (11, 14, 3, 1)]
 CYCLE = 0.00083
-PACES = [(1.0, 0.2, 0.8, 1.2, 0.7, (0.0, 1.1)), (1.0, 0.23, 0.5, 0.3, 1.0, (0.0, 1.5)), (1.0, 0.2, 0.9, 0.7, 1.3, (0.0, 0.6)),
-         (1.2, 0.16, 0.8, 1.2, 0.7, (0.0, 1.1)), (1.45, 0.2, 0.8, 1.2, 0.7, (0.0, 1.1))]
-PLANS = [(slow, wake, tensor, send, fly, (early, early)) for slow in (1.0, 1.1) for wake in (0.19, 0.21, 0.23) for tensor in (0.5, 0.8)
+PACES = [(1.0, 0.21, 0.8, 1.56, 1.2, 0.25, 2.0), (1.0, 0.2, 0.6, 1.2, 0.5, 0.7, 1.6), (1.1, 0.22, 0.9, 2.0, 1.0, 0.9, 2.6),
+         (1.25, 0.21, 0.7, 1.56, 0.6, 1.1, 1.6), (1.25, 0.18, 0.9, 1.2, 1.3, 0.4, 2.0), (1.45, 0.21, 0.7, 1.8, 0.9, 0.5, 2.0),
+         (1.5, 0.21, 0.9, 1.5, 0.7, 0.8, 2.0)]
+PLANS = [(slow, wake, tensor, 1.56, send, fly, early) for slow in (1.0, 1.1) for wake in (0.19, 0.21, 0.23) for tensor in (0.5, 0.8)
          for send, fly in ((1.0, 0.7), (0.6, 0.8)) for early in (1.0, 1.5)]
+TRIES, SLACK = 70000, 0.004
+SPAN = 50
+PASSES, BIAS = 5, 0.02
+CHOSEN = []
 CD, BF, F, U8, U16, I32 = "float8_e4m3fn_x4", "bfloat16", "float32", "uint8", "uint16", "int32"
 
 SCRATCH = {"ps": ("psum", [128, 4096], F)}
 for _n, _s, _d in [
         ("W", [HB + 8 * KB], BF), ("zz", [M, 128], BF), ("z32", [XE], BF), ("xs", [112, 16], BF), ("lt", [C], BF),
-        ("xl", [P, 4 * M], BF), ("us", [4, 128], BF), ("vs", [512], BF), ("zt", [512], BF), ("one", [256], BF), ("gt", [1024], BF),
+        ("xl", [P, 4 * M], BF), ("xo", [P, 4 * M], BF), ("us", [4, 128], BF), ("vs", [512], BF), ("zt", [512], BF), ("one", [256], BF), ("gt", [1024], BF),
         ("bt", [640], BF), ("dtl", [512], BF),
-        ("qx", [C], CD), ("sx", [C], U8), ("qz", [C], CD), ("sz", [C], U8), ("qu", [128], CD), ("su", [128], U8),
+        ("qx", [C], CD), ("sx", [C], U8), ("qz", [512], CD), ("sz", [512], U8), ("qu", [128], CD), ("su", [128], U8),
         ("qv", [128], CD), ("sv", [128], U8), ("qw", [528], CD), ("sw", [528], U8), ("qg", [256], CD), ("sg", [256], U8),
         ("qb", [256], CD), ("sb", [384], U8), ("qn", [128], CD), ("qd", [160], CD), ("sd", [160], U8),
-        ("kt", [C], F), ("ys", [C], F), ("rb", [2 * L], F), ("kb", [2 * L], F), ("sq", [2 * L], F), ("dk", [2 * L], F), ("dr", [L - 3], F),
-        ("gy", [2 * L + 60], F), ("fz", [30], F), ("s1", [30], F), ("s0", [30], F), ("tl", [240], F),
-        ("ti", [30], F), ("lb", [V * L + 50], F), ("tf", [32], F), ("wt", [V], F),
+        ("kt", [C], F), ("ys", [C], F), ("rb", [2 * L], F), ("sq", [4 * L], F), ("nx", [2], F), ("ob", [30], F),
+        ("gy", [2 * LT], F), ("em", [4 * L], F), ("tl", [3 * LT], F),
+        ("ti", [32], F), ("lb", [V * L], F), ("lq", [96], F), ("tf", [30], F), ("wt", [V], F),
         ("blk", [320], F), ("col", [320], F), ("pat", [48], F), ("sc", [16], F), ("mk", [64], F),
-        ("bx", [32], F), ("tb", [96], F), ("ex", [128], F), ("a3", [10, 2, 8], F), ("stg", [7, 4], F),
+        ("bx", [2, 16], F), ("tb", [96], F), ("ex", [128], F), ("a3", [10, 2, 8], F), ("stg", [8, 2, 2], F),
         ("g1", [32], I32), ("g2", [32], F), ("g3", [32], F), ("g4", [32], F), ("g5", [32], F), ("g6", [32], F),
-        ("lbx", [2], U16), ("lbs", [4], U16), ("lex", [8], U16), ("offb", [32], U16), ("offz", [112], U16), ("offl", [28], U16)]:
+        ("lbs", [4], U16), ("lex", [8], U16), ("offb", [32], U16), ("offz", [112], U16), ("offl", [28], U16)]:
     SCRATCH[_n] = ("sbuf", [128] + _s, _d)
 SEMAPHORES = ["v", "s", "t", "g", "lx", "lu", "lw", "lv", "lp", "w0", "w1", "w2", "sent0", "sent1", "og", "out", "end"]
-for _n in ["%d%d" % (_t, _k) for _t in range(R) for _k in range(2)]:
+for _n in ("00", "01", "11", "21"):
     SCRATCH["ql" + _n] = ("sbuf", [128, KB + 128], CD)
-    SCRATCH["sl" + _n] = ("sbuf", [128, 256], U8)
+    SCRATCH["sl" + _n] = ("sbuf", [128, 320], U8)
     SEMAPHORES.append("arr" + _n)
 
 
@@ -79,9 +87,12 @@ def rank_program(g, core, T, topo):
         return (ap, [], 0, None)
 
     def pick(win, off):
-        return (win[0].indirect(off[0]), win[1] + off[1], 64 + 50 * off[2], None)
+        return (win[0].indirect(off[0]), win[1] + off[1], 32 * off[2], None)
 
-    def job(e, outs, ins, call, hold, more=0.0, token=None):
+    def job(e, outs, ins, call, hold, more=0.0, token=None, picks=0):
+        if jobs and jobs[-1].get("open"):
+            jobs[-1]["can"][e] = (call, hold)
+            return
         ins = [v for v in ins if isinstance(v, tuple)]
         reads = [r for v in ins for r in v[1]]
         writes = [r for v in outs for r in v[1]]
@@ -98,15 +109,26 @@ def rank_program(g, core, T, topo):
         for name, mask in reads:
             seen.setdefault(name, []).append((len(jobs), mask))
         deps.discard(len(jobs))
-        jobs.append({"e": e, "call": call, "deps": deps, "hold": hold, "more": more, "token": token, "mates": [len(jobs)]})
+        jobs.append({"e": e, "can": {e: (call, hold)}, "deps": deps, "picks": picks, "more": more, "token": token, "mates": [len(jobs)]})
 
     def do(e, outs, ins, call, hold=None):
-        if hold is None:
-            cycles = max(v[2] for v in outs + ins if isinstance(v, tuple))
-            if e == "s" and ins[0][3]:
-                cycles = max(outs[0][2], ins[0][2]) * (2 if SCRATCH[outs[0][1][0][0]][2] == SCRATCH[ins[0][1][0][0]][2] == BF else 1)
+        picks = 0
+        if hold is None and ins and ins[0][3] is None:
+            hold, picks = 0.065 if e == "s" else 0.05, ins[0][2]
+        elif hold is None:
+            views = [v for v in outs + ins if isinstance(v, tuple)]
+            wide = [v for v in views if v[2] > 1]
+            narrow = e == "v" and all(SCRATCH[v[1][0][0]][2] in (BF, U16) for v in wide)
+            cycles = max(v[2] * (2 if SCRATCH[v[1][0][0]][2] in (BF, U16) and not narrow else 1) for v in views)
             hold = max(78 if e == "s" else 64, cycles) * CYCLE
-        job(e, outs, ins, call, hold)
+        job(e, outs, ins, call, hold, picks=picks)
+
+    def either(*ways):
+        ways[0]()
+        jobs[-1]["open"] = True
+        for way in ways[1:]:
+            way()
+        jobs[-1]["open"] = False
 
     def dmas(sem, items, more):
         count[sem] = count.get(sem, 0) + 16 * len(items)
@@ -121,20 +143,23 @@ def rank_program(g, core, T, topo):
         prev = {}
         for k, j in enumerate(jobs):
             j["deps"] = set(m for d in j["deps"] for m in jobs[d]["mates"] if m < k)
-            if (j["e"] in "gy" or k in rows) and j["e"] in prev:
-                users[prev[j["e"]]][k] = False
-            prev[j["e"]] = k
+            if j["e"] in "gy" and len(j["can"]) == 1:
+                if j["e"] in prev:
+                    users[prev[j["e"]]][k] = False
+                prev[j["e"]] = k
             for d in j["deps"]:
                 users[d][k] = True
 
         def times(pace):
-            slow, wake, tensor, send, fly, early = pace
-            hold = [send if j["more"] == "sent" else j["hold"] * {"t": tensor, "y": 1.0}.get(j["e"], slow) for j in jobs]
-            more = [{"sent": fly, "late": fly, "early": fly + early[0], "first": fly + early[1]}.get(j["more"], j["more"]) for j in jobs]
-            return hold, more, wake
+            slow, wake, tensor, gather, send, fly, first = pace
+            hold = [{e: send + h if j["more"] == "sent" else (h + gather * CYCLE * j["picks"]) * {"t": tensor, "y": 1.0}.get(e, slow)
+                     for e, (_, h) in j["can"].items()} for j in jobs]
+            more = [{"sent": fly, "late": fly, "early": fly + 0.4, "first": fly + first}.get(j["more"], j["more"]) + wake for j in jobs]
+            return hold, more
 
         def plan(pace):
-            hold, more, wake = times(pace)
+            hold, more = times(pace)
+            hold, wake = [h[j["e"]] for h, j in zip(hold, jobs)], 0.0
             way, left = [0.0] * n, [0] * n
             for k in range(n - 1, -1, -1):
                 way[k] = hold[k] + max([more[k]] + [way[u] + (more[k] + wake) * waits for u, waits in users[k].items()])
@@ -160,20 +185,178 @@ def rank_program(g, core, T, topo):
                         pool.append(u)
             return order
 
-        def lasts(order, pace):
-            hold, more, wake = times(pace)
-            ready, free = [0.0] * n, {e: 0.0 for e in eng}
-            for k in order:
-                e = jobs[k]["e"]
-                free[e] = max(free[e], ready[k]) + hold[k]
-                for u, waits in users[k].items():
-                    ready[u] = max(ready[u], free[e] + (more[k] + wake) * waits)
-            return max(free.values())
+        def refine():
+            timed = [times(p) for p in PACES]
+            hold = [{e: np.array([h[k][e] for h, _ in timed]) for e in jobs[k]["can"]} for k in range(n)]
+            more = np.array([m for _, m in timed]).T
+            weight = np.array([1 / p[0] for p in PACES])
+            hard, behind = [], []
+            for j in jobs:
+                far = 0
+                for d in j["deps"]:
+                    far |= behind[d]
+                hard.append(sorted(d for d in j["deps"] if not far >> d & 1))
+                behind.append(far | sum(1 << d for d in j["deps"] if not far >> d & 1))
+            soft = [[] for _ in jobs]
+            for d in range(n):
+                for k, waits in users[d].items():
+                    if not waits:
+                        soft[k].append(d)
+            zero = np.zeros(len(PACES))
+
+            def lasts(order, on, end, done, start, chain=(), room=0.0, until=n):
+                free, moved = {}, set()
+                for k in reversed(order[:start]):
+                    free.setdefault(on[k], end[k])
+                    if len(free) == len(eng):
+                        break
+                for i in range(start, n):
+                    k = order[i]
+                    t = free.get(on[k], zero)
+                    for d in hard[k]:
+                        t = np.maximum(t, done[d])
+                    t = t + hold[k][on[k]]
+                    if i > start + 70 and k in chain:
+                        by = t - end[k]
+                        if by @ weight > room:
+                            return np.inf
+                        end[order[i:]] += by
+                        done[order[i:]] += by
+                        break
+                    if until < n:
+                        if max(map(abs, (t - end[k]).tolist())) > 1e-9:
+                            moved.add(on[k])
+                            until = max([until] + [where[u] + 1 for u in users[k]])
+                        else:
+                            moved.discard(on[k])
+                            if i > until and not moved:
+                                break
+                    free[on[k]] = end[k] = t
+                    done[k] = t + more[k]
+                return float(done.max(axis=0) @ weight)
+
+            def places():
+                where, ahead, last = {k: i for i, k in enumerate(order)}, {}, {}
+                for k in order:
+                    ahead[k] = last.get(on[k])
+                    last[on[k]] = k
+                return where, ahead
+
+            def chains():
+                stood, common = [], None
+                for p in range(len(PACES)):
+                    k, chain = int(done[:, p].argmax()), set()
+                    while k is not None:
+                        chain.add(k)
+                        d = max(hard[k], key=lambda x: done[x, p], default=None)
+                        if d is not None and done[d, p] > end[k, p] - hold[k][on[k]][p] - 1e-9:
+                            k = d
+                        else:
+                            if ahead[k] is not None:
+                                stood.append(k)
+                            k = ahead[k]
+                    common = chain if common is None else common & chain
+                return stood, common
+            on = [j["e"] for j in jobs]
+            end, done = np.zeros((n, len(PACES))), np.zeros((n, len(PACES)))
+
+            def fit(k, t0, p, busy, queues, first, bias):
+                found = []
+                for e in queues:
+                    t, h, row = t0, hold[k][e][p], busy[e]
+                    i = len(row)
+                    while i and row[i - 1][1] > t0:
+                        i -= 1
+                    while i < len(row) and row[i][0] < t + h - 1e-9:
+                        t, i = max(t, row[i][1]), i + 1
+                    found.append((t + h + bias * (e != first), t, h, i, e))
+                _, t, h, i, e = min(found)
+                busy[e].insert(i, (t, t + h))
+                return t + h, e
+
+            def pack(rank, p, on, back):
+                busy, ends, to = {e: [] for e in eng}, [0.0] * n, [None] * n
+                for k in rank:
+                    if back:
+                        t0 = max([more[k, p]] + [ends[u] + more[k, p] * waits for u, waits in users[k].items()])
+                    else:
+                        t0 = max([0.0] + [ends[d] + more[d, p] for d in hard[k]] + [ends[d] for d in soft[k]])
+                    ends[k], to[k] = fit(k, t0, p, busy, [on[k]] if on else jobs[k]["can"], jobs[k]["e"], BIAS)
+                if back:
+                    return sorted(range(n), key=lambda k: (-ends[k], k)), to
+                return sorted(range(n), key=lambda k: (ends[k] - hold[k][to[k]][p], k)), to, sorted(range(n), key=lambda k: (-ends[k], -k))
+            best = min((lasts(order, on, end, done, 0), order, on) for order in map(plan, PLANS))
+            for p, pace in enumerate(PACES):
+                for free in (False, True):
+                    rank, to = plan(pace), on
+                    for _ in range(PASSES):
+                        order, to, rank = pack(rank, p, None if free else to, False)
+                        best = min(best, (lasts(order, to, end, done, 0), order, to))
+                        rank, to = pack(rank, p, to, True)
+            now, order, on = best
+            lasts(order, on, end, done, 0)
+            rng = np.random.default_rng(0)
+            where, ahead = places()
+            stood, common = chains()
+            taken = 0
+            for i in range(TRIES):
+                room = -SLACK * (1 - i / TRIES) * float(np.log(rng.random() + 1e-12))
+                k = stood[int(rng.integers(len(stood)))]
+                h = ahead[k]
+                if h is None:
+                    continue
+                new, to = list(order), list(on)
+                move = int(rng.integers(6))
+                if move > 3:
+                    at_ = max(0, where[k] - int(rng.integers(SPAN)))
+                    p, part = int(rng.integers(len(PACES))), order[at_:at_ + SPAN]
+                    shake = 0.25 * rng.random()
+                    key = {x: end[x, p] - hold[x][on[x]][p] + shake * rng.standard_normal() for x in part}
+                    for x in part:
+                        key[x] = max([key[x]] + [key[d] + 1e-6 for d in hard[x] + soft[x] if d in key])
+                    busy, ends = {e: [] for e in eng}, {}
+                    for x in reversed(order[:at_]):
+                        if not busy[on[x]]:
+                            busy[on[x]].append((0.0, end[x, p]))
+                    for x in sorted(part, key=key.get):
+                        t0 = max([0.0] + [ends[d] + more[d, p] if d in key else done[d, p] for d in hard[x]] + [ends[d] for d in soft[x] if d in key])
+                        ends[x], to[x] = fit(x, t0, p, busy, jobs[x]["can"], on[x], 0.3 * rng.random())
+                    new[at_:at_ + SPAN] = sorted(part, key=lambda x: (ends[x] - hold[x][to[x]][p], key[x]))
+                elif move == 0:
+                    for _ in range(int(rng.integers(3))):
+                        h = ahead[h] if ahead[h] is not None else h
+                    at_ = max([where[h]] + [where[d] + 1 for d in hard[k] + soft[k]])
+                    new.insert(at_, new.pop(where[k]))
+                elif move == 1:
+                    at_ = min([where[k] + int(rng.integers(12))] + [where[u] - 1 for u in users[h]] + [n - 1])
+                    new.insert(at_, new.pop(where[h]))
+                    at_ = where[h]
+                else:
+                    x = (k, h)[move - 2]
+                    others = [e for e in jobs[x]["can"] if e != on[x]]
+                    if not others:
+                        continue
+                    to[x], at_ = others[int(rng.integers(len(others)))], where[x]
+                end2, done2 = end.copy(), done.copy()
+                t = lasts(new, to, end2, done2, at_, common, room + 1e-9, where[k] + SPAN + 1)
+                if t <= now + room + 1e-9:
+                    order, on, end, done = new, to, end2, done2
+                    where, ahead = places()
+                    now, taken = t, taken + 1
+                    if taken % 20 == 0 or now < best[0] - 0.05:
+                        now = lasts(order, on, end, done, 0)
+                        stood, common = chains()
+                        if now < best[0]:
+                            best = (now, order, on)
+            return best[1:]
+        if not CHOSEN:
+            CHOSEN.extend(refine())
         known = {e: {} for e in eng}
         clock = {}
-        for k in min((plan(p) for p in PLANS), key=lambda order: sum(lasts(order, p) / p[0] for p in PACES)):
+        for k in CHOSEN[0]:
             j = jobs[k]
-            e = j["e"]
+            e = CHOSEN[1][k]
+            j["call"] = j["can"][e][0]
             need = {}
             for d in j["deps"]:
                 sem, c = jobs[d]["token"]
@@ -202,12 +385,21 @@ def rank_program(g, core, T, topo):
         do("g", [out], [], lambda: g.iota(out[0], pattern, base, cm, allow_small_or_imprecise_dtypes=True),
            0.13 + 2 * CYCLE * int(np.prod([c for _, c in pattern])))
 
-    def copy(e, out, in_, scale=None, bias=None, func=AF.Identity):
-        if e == "v":
-            if scale is None:
+    def copy(e, out, in_, scale=None, bias=None, func=AF.Identity, only=False):
+        if func == AF.Identity and not only:
+            either(*[lambda x=x: copy(x, out, in_, scale, bias, func, True) for x in dict.fromkeys(e + "vs")])
+        elif e == "g":
+            n = int(out[1][0][1].sum(axis=1).max())
+            do(e, [out], [in_], lambda: g.affine_select(out[0], in_[0], [[0, n]], A.is_gt, 0.0, 1, 0), 0.17 + 2 * CYCLE * n)
+        elif e == "v":
+            if scale is None and bias is None:
                 do(e, [out], [in_], lambda: vec.tensor_copy(out[0], in_[0]))
+            elif bias is None:
+                ts(out, in_, scale, A.mult)
+            elif scale is None:
+                ts(out, in_, bias, A.add)
             else:
-                do(e, [out], [in_], lambda: vec.tensor_scalar(out[0], in_[0], scale, None, A.mult))
+                ts(out, in_, scale, A.mult, bias, A.add)
         elif scale is None and bias is None:
             do(e, [out], [in_], lambda: act.activation(out[0], in_[0], AF.Copy))
         else:
@@ -226,8 +418,8 @@ def rank_program(g, core, T, topo):
     def tr(out, in_):
         do("v", [out], [in_], lambda: vec.transpose(out[0], in_[0]))
 
-    def scan(out, d0, d1, init, op=A.max):
-        do("v", [out], [d0, d1], lambda: vec.tensor_tensor_scan(out[0], d0[0], d1[0], init, A.add, op))
+    def scan(out, d0, d1, init, op0=A.add, op1=A.max):
+        do("v", [out], [d0, d1], lambda: vec.tensor_tensor_scan(out[0], d0[0], d1[0], init, op0, op1))
 
     def quant(q, s, a, b, in_, sa=None):
         qv, sv = at(q, s_[:, a:b]), at(s, s_[:, a:b] if sa is None else s_[:, sa:sa + b - a])
@@ -262,7 +454,7 @@ def rank_program(g, core, T, topo):
                 items.append(("y", w(X0 + d * XE, X0 + d * XE + XE, 1, lo, hi), w(X0, X0 + XE, 1, lo + 16 * d, hi + 16 * d)))
             dmas(sem, items, more)
 
-    dmas("lx", [("y", at("xl"), hbm(T.x[:]))], 1.6)
+    dmas("lx", [(e, at("xl", s_[64 * k:64 * k + 64]), hbm(T.x[64 * k:64 * k + 64, :])) for k, e in enumerate("ys")], 1.6)
     dmas("lu", [("y", at("us", s_[:, k:k + 3:2, :]), hbm(T.u[:, 256 * k:256 * k + 256])) for k in range(2)], 2.2)
 
     def blk(k, a=0, b=32):
@@ -276,7 +468,7 @@ def rank_program(g, core, T, topo):
     iota(at("ti"), [[-XE, 2], [128, G]], XE - 128, 4)
     iota(blk(4), [[16, 4], [2 * XE, 4], [-4 * KB, 2]], 9 * XE + 4 * KB - 4 * 96, 4)
     iota(blk(0), [[-XE, 2], [0, 4], [1, 4]], 0, -XE // 16)
-    iota(blk(1), [[0, 2], [L, 4], [0, 4]], L - 1)
+    iota(blk(1), [[0, 32]])
     for h in range(2):
         iota(blk(2, 16 * h, 16 * h + 16), [[0, 2], [64, 2], [128, 4]], 16 * h, 1)
         iota(blk(9, 16 * h, 16 * h + 16), [[0, 2], [64, 2], [128, 4]], 528 * h, 1)
@@ -285,8 +477,8 @@ def rank_program(g, core, T, topo):
     iota(blk(6), [[1, 2], [0, 16]])
     iota(blk(7), [[0, 2], [1, 2], [0, 8]])
     iota(blk(8), [[1, 32]])
-    iota(at("pat", s_[:, 4:10]), [[4, 3], [-G, 2]], G + 1)
-    iota(at("pat", s_[:, 10:12]), [[-G, 2]], G + 13)
+    iota(at("pat", s_[:, 4:10]), [[4, 3], [-G, 2]], G)
+    iota(at("pat", s_[:, 10:12]), [[-G, 2]], G + 12)
     iota(at("pat", s_[:, 16:48]), [[0, 2], [1, 2], [0, 8]])
     iota(at("one"), [[0, 256]], 1)
     for b in range(4):
@@ -295,21 +487,18 @@ def rank_program(g, core, T, topo):
     iota(at("bt", s_[:, 256:640]), [[0, 384]])
 
     fill(at("zt"), 0.0)
-    fill(at("dr"), 0.0)
-    fill(at("dk"), 0.0)
     fill(at("gy"), 0.0)
-    fill(at("tl"), -BIG)
-    fill(at("sq"), -BIG)
-    fill(at("rb", s_[:, 2:2 * L:45]), -BIG)
-    fill(at("kb", s_[:, 2:L:45]), -BIG)
+    fill(at("tl"), 0.0)
+    fill(at("sq", s_[:, 0:4 * L:2]), -BIG)
     fill(at("tb", s_[64:128]), 0.0)
     quant("qn", "sb", 0, 128, at("zt"))
-    put(at("dr", s_[:, 42:43]), 1, -BIG)
-    put(at("dk", s_[:, 0:2 * L:3]), 60, -BIG)
-    put(at("gy", s_[:, 0:2 * L + 60:L + 30]), 2, -BIG)
+    for name, k, val in (("sq", 3, 0.0), ("em", 0, 0.0)):
+        put(at(name, s_[:, k:4 * L:6]), 64, val)
+    put(at("rb"), 2 * L, -BIG / 4)
+    put(at("gy", s_[:, 48:2 * LT:LT]), 2, -BIG)
     for k in range(2):
-        put(at("gy", s_[:, (L + 30) * k + 1:(L + 30) * k + L + 3:3]), 31, BIG / 2)
-    put(at("lb", s_[0:32, V * L + 34:V * L + 50]), 16, 0.0)
+        put(at("gy", s_[:, LT * k + 46:LT * k + 95:48]), 2, -1.0)
+    put(at("lq", s_[0:64, 80:96]), 16, 0.0)
 
     for a in range(4):
         q0 = 32 * QUAD[a]
@@ -320,22 +509,22 @@ def rank_program(g, core, T, topo):
     put(sc(4, 0, 64), 1, 1 / TS)
     put(sc(4, 64, 128), 1, 0.0)
     put(sc(5, 64, 128), 1, float(X0))
-    copy("s", at("tl", s_[:, 0:L:3]), at("ti"), TS, sc(0))
+    for s in range(2):
+        copy("s", at("tl", s_[:, 48 * s + 3:48 * s + 45:3]), at("ti", s_[:, G * s + 1:G * s + 15]), TS, sc(0))
 
     def columns():
         put(at("dtl", s_[:, 4 * KB:512]), 512 - 4 * KB, 0.0)
         quant("qd", "sd", 0, 128, at("zt"))
         for n, k, m in ((0, 0, 2), (2, 19, 1), (3, 18, 1), (4, 17, 1), (5, 16, 1)):
-            copy("s", at("wt", s_[96:128, n:n + m]), at("col", s_[96:128, 128 + k:128 + k + m]), TS, BIG / 2)
+            copy("s", at("wt", s_[96:128, n:n + m]), at("col", s_[96:128, 128 + k:128 + k + m]), TS)
         copy("s", sc(3, 0, 96), col(0, 0, 96))
-        copy("s", sc(5, 0, 64), col(0, 0, 64), bias=X0 - BIG / 2 / TS)
+        copy("s", sc(5, 0, 64), col(0, 0, 64), bias=float(X0))
         for k in range(2):
             copy("s", sc(6 + k), col(6 + k), -BIG)
             copy("s", at("mk", s_[:, 32 * k:32 * k + 32]), at("pat", s_[:, 16:48]), BIG, sc(6 + k), AF.Abs)
 
     def lists(n):
         if n:
-            ts(at("lbx"), at("zt", s_[:, 0:2]), col(1), A.add, 2.0 * L - 1, A.min)
             ts(at("lbs", s_[:, 0:1]), col(2), 0.0625, A.mult, 31.0, A.min)
             ts(at("lbs", s_[:, 2:3]), col(9), 0.0625, A.mult, 63.0, A.min)
             return
@@ -388,62 +577,81 @@ def rank_program(g, core, T, topo):
             return at(name, s_[lo:hi, o + a:o + b:step])
 
         def gates(n, a, b, step=1, lo=0, hi=128):
-            return run("gy", n, a, b, step, L + 30, lo, hi)
+            return run("gy", n, a, b, step, LT, lo, hi)
+
+        def one(name, n, k, lo=0, hi=128):
+            return run(name, n, k, k + 1, 1, L, lo, hi)
+
+        def six(name, n, a, b, step=6, lo=0, hi=128):
+            return run(name, n, a, b, step, 2 * L, lo, hi)
+
+        def top(n, s, lo=0, hi=128):
+            return one("rb", n, 48 * s + 44, lo, hi)
 
         def largest(n):
             if n:
-                scan(run("rb", n, 3, L), at("dr"), run("sq", n - 1, 3, L), -BIG)
-            else:
-                for s in range(2):
-                    scan(run("rb", 0, 45 * s + 5, 45 * s + 45, 3), at("dr", s_[:, 0:M]), at("kt", s_[:, 16 - 16 * s:C:32]), -BIG)
-
-        def held(n):
-            if n:
-                scan(run("kb", n, 0, L), run("dk", n - 1, 0, L), run("sq", n - 1, 0, L), -BIG)
-            else:
-                for s in range(2):
-                    copy("s", run("kb", 0, 45 * s + 5, 45 * s + 45, 3), at("kt", s_[:, 16 - 16 * s:C:32]))
+                for a, b in ((3, 95),) if n <= APART else ((51, 95), (3, 45)):
+                    scan(run("rb", n, a, b), run("rb", n - 1, a, b), six("sq", n - 1, 2 * a, 2 * b, 2), -BIG / 4, A.min, A.max)
+                return
+            put(run("rb", 0, 3, L, 3), 31, BIG)
+            for s in (1, 0):
+                scan(run("rb", 0, 48 * s + 5, 48 * s + 45, 3), at("zt", s_[:, 0:M]), at("kt", s_[:, 16 - 16 * s:C:32]), -BIG)
+                copy("s", six("sq", 0, L * s + 6, L * s + 90), at("kt", s_[:, 16 - 16 * s:C:32]))
 
         def before(n, s):
-            ts(gates(n, 45 * s + 3, 45 * s + 48, 3), run("rb", n, 45 * s + 2, 45 * s + 45, 3), run("rb", n, 45 * s + 44, 45 * s + 45),
-               A.is_lt, -BIG, A.mult)
+            ts(gates(n, 48 * s + 3, 48 * s + 48, 3), run("rb", n, 48 * s + 2, 48 * s + 45, 3), top(n, s), A.is_lt, -BIG, A.mult)
 
-        def after(n, s):
-            ts(gates(n, 45 * s + 5, 45 * s + 48, 3), run("rb", n, 45 * s + 2, 45 * s + 45, 3), run("rb", n, 45 * s + 44, 45 * s + 45),
-               A.is_ge, -BIG / 2, A.mult)
+        def lift(n, s):
+            out, in_ = gates(n, 48 * s + 5, 48 * s + 45, 3), run("rb", n, 48 * s + 2, 48 * s + 42, 3)
+            either(lambda: copy("s", out, in_, -1.0, top(n, s), AF.Sign), lambda: ts(out, in_, top(n, s), A.is_lt))
 
-        def strike(n, k):
-            tt(run("sq", n, k, L, 3), run("kb", n, 2, L, 3), gates(n, 5 * k - 5, L + 3 * k - 3, 3), A.add)
+        def cut(n):
+            end = 93 if n else 96
+            for a, b in ((3, end),) if n < APART else ((51, end), (3, 45)):
+                tt(run("rb", n, a + 1, b, 3), run("rb", n, a - 1, b - 3, 3), gates(n, a + 3, b + 3, 3), A.subtract)
 
         def enter(n):
-            for s, lo, hi, fr in ((0, 0, 64, 64), (0, 64, 96, 32), (1, 0, 128, 0)):
-                copy("s", run("sq", n, 45 * s + 3, 45 * s + 45, 3, L, lo, hi), gates(n, 45 * s + 6, 45 * s + 48, 3, lo, hi),
-                     bias=run("rb", n, 89 - 45 * s, 90 - 45 * s, 1, L, fr, fr + hi - lo))
-            copy("s", run("dk", n, 4, L, 3), gates(n, 5, L, 3))
+            for lo, hi, fr in ((0, 64, 64), (64, 96, 32)):
+                copy("s", six("sq", n, 8, 90, 6, lo, hi), at("zt", s_[lo:hi, 0:M]), bias=one("rb", n, 94 if n else 92, fr, fr + hi - lo))
+            if n:
+                ts(six("sq", n, 104, 190), at("zt", s_[:, 0:M + 1]), top(n, 0), A.add, six("sq", n - 1, 8, 9), A.max)
+            else:
+                copy("v", six("sq", n, 104, 190), at("zt", s_[:, 0:M + 1]), bias=top(n, 0))
 
-        def origin(n, a, b, step=1):
-            o = 120 if n else 0
-            return at("tl", s_[:, o + a:o + b:step])
+        def held(n):
+            copy("s", at("nx"), six("sq", n, 8, 105, L), -1.0)
+            for s in range(2):
+                out, in_, new = six("sq", n, L * s + 9, L * s + 90), six("em", n, L * s + 9, L * s + 90), six("sq", n, L * s + 8, L * s + 9)
+                either(lambda: copy("s", out, in_, at("nx", s_[:, s:s + 1]), new, only=True), lambda: ts(out, in_, 0.5, A.is_lt, new, A.mult))
+            scan(six("sq", n + 1, 3, 183, 3), six("em", n, 6, 186, 3), six("sq", n, 6, 186, 3), 0.0, A.mult, A.add)
 
-        def leave(n, a=0, b=L):
-            scan(at("lb", s_[:, L * n + a:L * n + b]), gates(n, a, b), origin(n, a, b), 0.0)
+        def origin(n, a, b, step=1, lo=0, hi=128):
+            o = LT * (2 - n % 2) if n else 0
+            return at("tl", s_[lo:hi, o + a:o + b:step])
+
+        def left(n, s, lo=0, hi=32):
+            return at("lb", s_[lo:hi, L * n + 48 * s + 46:L * n + 48 * s + 47])
+
+        def leave(n):
+            scan(at("lb", s_[:, L * n + 3:L * n + 95]), gates(n, 3, 95), origin(n, 3, 95), 0.0)
 
         def mark(n):
-            tt(at("fz"), gates(n, 0, L, 3), gates(n, 3, L + 3, 3), A.subtract)
+            tt(six("em", n, 9, 186), gates(n, 3, 93, 3), gates(n, 6, 96, 3), A.is_equal)
+
+        def stay(n):
+            if n:
+                tt(at("ob"), origin(n, 3, 93, 3), origin(n, 4, 93, 3), A.add)
+            tt(origin(n + 1, 3, 93, 3), at("ob") if n else origin(0, 3, 93, 3), six("em", n, 9, 186), A.mult)
 
         def come(n):
-            tt(at("s1"), origin(n, 0, L, 3), at("fz"), A.subtract)
             for s, lo, hi, fr in ((0, 96, 128, None), (1, 0, 128, 0), (0, 0, 64, 64), (0, 64, 96, 32)):
-                c = L * n + 89 - 45 * s
-                copy("s", at("s0", s_[lo:hi, G * s:G * s + G]), at("fz", s_[lo:hi, G * s:G * s + G]), 0.5,
-                     at("wt", s_[96:128, n:n + 1]) if fr is None else at("lb", s_[fr:fr + hi - lo, c:c + 1]))
-
-        def merge(n, a=0, b=2 * G):
-            tt(origin(n + 1, 3 * a, 3 * b, 3), at("s1", s_[:, a:b]), at("s0", s_[:, a:b]), A.min)
+                out, in_ = origin(n + 1, 48 * s + 4, 48 * s + 45, 3, lo, hi), six("em", n, L * s + 9, L * s + 90, 6, lo, hi)
+                new = at("wt", s_[96:128, n:n + 1]) if fr is None else left(n, 1 - s, fr, fr + hi - lo)
+                either(lambda: copy("s", out, in_, -1.0, new, AF.Relu), lambda: ts(out, in_, 0.5, A.is_lt, new, A.mult))
 
         def final(a):
             q0 = 32 * QUAD[a]
-            tt(at("tf", s_[32 * a:32 * a + 32, 0:30]), at("s1", s_[q0:q0 + 32]), at("s0", s_[q0:q0 + 32]), A.min)
+            tt(at("tf", s_[32 * a:32 * a + 32]), origin(V, 3, 93, 3, q0, q0 + 32), origin(V, 4, 93, 3, q0, q0 + 32), A.add)
 
         def drawn(k, in_):
             for a in range(2):
@@ -451,40 +659,40 @@ def rank_program(g, core, T, topo):
 
         for n in range(V - 1):
             largest(n)
-            held(n)
-            for gate in (before, after):
-                for s in range(2):
-                    gate(n, s)
-            rows.update(range(len(jobs) - 3, len(jobs)))
+            for s in range(2):
+                before(n, s)
             enter(n)
-            strike(n, 1)
-            strike(n, 2)
+            for s in range(2):
+                lift(n, s)
+            cut(n)
             mark(n)
             leave(n)
+            stay(n)
             come(n)
             if n < V - 2:
-                merge(n)
+                held(n)
         n = V - 1
-        o = L * n
-        largest(n)
-        copy("v", at("bx"), pick(at("lb", s_[:, 0:2 * L]), at("lbx")))
+        for k, (a, b) in enumerate(((0, 4), (4, 16))):
+            copy("s", at("bx", s_[0:32, :, a:b]), at("zt", s_[0:32, 0:2 * (b - a)]), bias=left(k, 1))
         for k in range(3):
-            copy("s", at("lb", s_[0:32, o + 112 + 4 * k:o + 116 + 4 * k]), at("zt", s_[0:32, 0:4]), bias=at("lb", s_[0:32, o - L * k - 1:o - L * k]))
-        for s in range(2):
+            for a in range(2):
+                copy("s", at("lq", s_[32 * a:32 * a + 32, 68 + 4 * k:72 + 4 * k]), at("zt", s_[0:32, 0:4]), bias=left(n - 1 - k, 1))
+        largest(n)
+        for s in (1, 0):
             before(n, s)
-            after(n, s)
-        merge(n - 1, 0, G)
-        merge(n - 1, G, 2 * G)
-        leave(n, 48, L + 22)
+            lift(n, s)
+        for a in range(2):
+            scan(at("lq", s_[32 * a:32 * a + 32, 0:68]), gates(n, 51, 119, 1, 0, 32), origin(n, 51, 119, 1, 0, 32), 0.0)
         mark(n)
-        leave(n, 0, 45)
+        leave(n)
+        stay(n)
         come(n)
         for a in range(4):
             final(a)
 
         drawn(0, at("bx", s_[0:32]))
-        drawn(1, at("lb", s_[0:32, o + 108:o + 140]))
-        drawn(2, at("lb", s_[0:32, o + 92:o + 124]))
+        tr(at("tb", s_[0:64, 32:64]), at("lq", s_[0:64, 64:96]))
+        tr(at("tb", s_[0:64, 64:96]), at("lq", s_[0:64, 48:80]))
         wb = w(0, 9 * XE)
         peer = T.cores[(rank + t + 1) % N]
         rid, pid = topo.addr(peer)[0:2]
@@ -494,43 +702,47 @@ def rank_program(g, core, T, topo):
         for k in range(2):
             ts(at("offb", s_[:, 16 * k:16 * k + 16]), pick(at("tb", s_[:, 32 * k:64 * k + 32]), at("lbs", s_[:, 2 * k:2 * k + 1])),
                sc(4), A.mult, sc(5), A.add)
-            if k:
+            if k or t:
                 for h in range(2):
-                    copy("sv"[h], at("bt", s_[:, 64 * h:64 * h + 64]), pick(wb, at("offb", s_[:, 16 + 4 * h:20 + 4 * h])))
+                    o = 128 * h + 64 * k if t else 64 * h
+                    copy("sv"[h * k], at("bt", s_[:, o:o + 64]), pick(wb if k else w(0, 5 * XE), at("offb", s_[:, 16 * k + 4 * h:16 * k + 4 * h + 4])))
             else:
                 copy("s", at("bt", s_[:, 128:256]), pick(w(0, 5 * XE), at("offb", s_[:, 0:8])))
+            if t and not k:
+                continue
+            n = 2 * KB if t else KB
             quant("qb", "sb", 128 * k, 128 * k + 128, at("bt", s_[:, 128 - 128 * k:640 - 128 * k]), 128 * k + 128)
             ql, sl, arr, sent = "ql%d%d" % (t, k), "sl%d%d" % (t, k), "arr%d%d" % (t, k), "sent%d" % k
-            src = [at("qb", s_[:, 128 * k:128 * k + KB], True), at("sb", s_[:, 128 * k + KB:128 * k + 128 + KB])]
-            dst = [at(ql, s_[:, 0:KB], True), at(sl, s_[:, 0:128])]
+            src = [at("qb", s_[:, 128 * k:128 * k + n], True), at("sb", s_[:, 128 * k + 128 - 3 * n:128 * k + 128 + n])]
+            dst = [at(ql, s_[:, 0:n], True), at(sl, s_[:, 0:4 * n])]
             writes = [RemoteDMATransfer(dst_ids=[DstId(rid=rid, pnc=pid)], dma_engine_mask=masks[i], remote_sem=S[arr],
                                         src=src[i][0], dst=dst[i][0]) for i in range(2)]
             count[sent] = count.get(sent, 0) + 2 * half
-            job("g", [], src, lambda writes=writes, sent=sent: g.remote_dma_fused(writes, local_sem=S[sent]), 0.0, "sent", (sent, count[sent]))
+            job("g", [], src, lambda writes=writes, sent=sent: g.remote_dma_fused(writes, local_sem=S[sent]), 0.4 - 0.4 * k, "sent", (sent, count[sent]))
             count[arr] = 2 * (len(topo.engines(T.cores[(rank - t - 1) % N], core)) // 2)
             job("g", dst, [], lambda: None, 0.0, "late" if k else "early" if t else "first", (arr, count[arr]))
             for i in range(2):
-                mm(4 * k + i, 128, [(side("qg", "sg", 128 * i, 128), side(ql, sl, 0, 128, 128 - KB))])
+                mm(4 * k + i, 128, [(side("qg", "sg", 128 * i, 128), side(ql, sl, 0, 128, 3 * n))])
                 for b in range(2):
                     for h in range(2):
-                        o = 512 * (4 * k + i) + 16 * h
-                        copy("vs"[i], at("dtl", s_[64 * h:64 * h + 64, 64 * k + 2 * i + b:64 * k + 64:4]),
-                             at("ps", s_[64 * b:64 * b + 64, o:o + 16]))
-        tt(at("ex", s_[:, 96:128]), pick(at("tf", s_[:, 0:30]), at("lex", s_[:, 6:8])), at("mk", s_[:, 32 * last:32 * last + 32]), A.subtract)
-        copy("s", at("ex", s_[:, 0:96]), pick(at("tf", s_[:, 0:30]), at("lex", s_[:, 0:6])))
+                        o = 512 * (4 * k + i) + n // 2 * h
+                        copy("vs"[i], at("dtl", s_[64 * h:64 * h + 64, 64 * k + 64 - 2 * n + 2 * i + b:64 * k + 64:4]),
+                             at("ps", s_[64 * b:64 * b + 64, o:o + n // 2]), only=True)
+        tt(at("ex", s_[:, 96:128]), pick(at("tf"), at("lex", s_[:, 6:8])), at("mk", s_[:, 32 * last:32 * last + 32]), A.subtract)
+        copy("s", at("ex", s_[:, 0:96]), pick(at("tf"), at("lex", s_[:, 0:6])))
 
         r0 = 1 if last else 0
         tr(at("a3", s_[:, 2 * r0:2 * r0 + 8]), at("ex"))
         if last:
-            tt(at("a3", s_[:, 1]), at("a3", s_[:, 8:10, 0]), at("a3", s_[:, 8:10, 1]), A.max)
-            ts(at("offz", s_[:, 0:48]), at("a3", s_[:, 2:7:2]), sc(2), A.mult, sc(3), A.add)
-            ts(at("offz", s_[:, 48:112]), at("a3", s_[:, 1:8:2]), sc(2), A.mult, sc(3), A.add)
+            tt(at("a3", s_[:, 0:2, 0]), at("a3", s_[:, 8:10, 0]), at("a3", s_[:, 8:10, 1]), A.max)
+            for a, b, k, x in EIGHTS:
+                ts(at("offz", s_[:, 8 * a:8 * b]), at("a3", s_[:, k:k + 2 * (b - a) - 1:2, x]), sc(2), A.mult, sc(3), A.add)
         else:
             tt(at("a3", s_[:, 6]), at("a3", s_[:, 6]), at("a3", s_[:, 7]), A.max)
             ts(at("offz", s_[:, 0:96]), at("a3", s_[:, 0:6]), sc(2), A.mult, sc(3), A.add)
             ts(at("offz", s_[:, 96:112]), at("a3", s_[:, 6]), sc(2), A.mult, sc(3), A.add)
         for a in range(4):
-            copy("s", at("stg", s_[32 * a:32 * a + 32]), at("a3", s_[96:128, r0:r0 + 7, :, 2 * a:2 * a + 2]))
+            copy("gs", at("stg", s_[32 * a:32 * a + 32, 0:7 + r0]), at("a3", s_[96:128, 0:7 + r0, :, 2 * a:2 * a + 2]))
         wz = w(X0, X0 + 7 * XE)
 
         def early(e, a, b):
@@ -539,17 +751,17 @@ def rank_program(g, core, T, topo):
         early("s", 0, 9)
         early("v", 9, 14)
         if last:
-            ts(at("offl", s_[:, 0:12]), at("stg", s_[:, 1:6:2]), 1 / TS, A.mult, col(0), A.add)
-            ts(at("offl", s_[:, 12:28]), at("stg", s_[:, 0:7:2]), 1 / TS, A.mult, col(0), A.add)
+            for a, b, k, x in EIGHTS:
+                ts(at("offl", s_[:, 2 * a:2 * b]), at("stg", s_[:, k:k + 2 * (b - a) - 1:2, x]), 1 / TS, A.mult, col(0), A.add)
         else:
-            ts(at("offl"), at("stg"), 1 / TS, A.mult, col(0), A.add)
+            ts(at("offl"), at("stg", s_[:, 0:7]), 1 / TS, A.mult, col(0), A.add)
 
         quant("qd", "sd", KB, KB + 128, at("dtl"))
         if t == 0:
             job("y", [], [at("qd")], lambda: None, 0.0, 0.0, ("lx", 0))
-            dmas("lp", [x for r in range(1, R) for k in range(2) for x in (
-                ("y", at("ql%d%d" % (r, k), s_[:, KB:128], True), at("qn", s_[:, 0:128 - KB], True)),
-                ("y", at("sl%d%d" % (r, k), s_[:, 128:256 - KB]), at("sb", s_[:, 0:128 - KB])))], 3.0)
+            dmas("lp", [x for r in range(1, R) for x in (
+                ("y", at("ql%d1" % r, s_[:, 64:128], True), at("qn", s_[:, 0:64], True)),
+                ("y", at("sl%d1" % r, s_[:, 256:320]), at("sb", s_[:, 0:64])))], 3.0)
             dmas("lv", [("y", at("vs"), hbm(T.v[:]))], 3.0)
         for b in range(4):
             mm(b, 128, [(side("qw", "sw", 16 + 128 * b, 128), side("qd", "sd", KB, 128)),
@@ -569,14 +781,15 @@ def rank_program(g, core, T, topo):
         def place(es, c):
             a, b = chunks[c]
             for k, e in enumerate(es):
-                if e != "-":
-                    copy(e, at("zz", s_[96:128, a:b, 32 * k:32 * k + 32]), at("lt", s_[32 * k:32 * k + 32, 32 * a:32 * b]))
+                copy(e + "g", at("zz", s_[96:128, a:b, 32 * k:32 * k + 32]), at("lt", s_[32 * k:32 * k + 32, 32 * a:32 * b]))
 
         def codes(c):
             a, b = chunks[c]
-            quant("qz", "sz", 32 * a, 32 * b, at("zz", s_[:, a:b]))
+            a = min(a, b - 4)
+            o = 32 * a
+            quant("qz", "sz", o, o + 32 * (b - a), at("zz", s_[:, a:b]))
             for k in range(4):
-                mm(4 * (c % 2) + k, 32 * (b - a), [(side("qw", "sw", 16 + 128 * k, 128), side("qz", "sz", 32 * a, 32 * (b - a)))])
+                mm(4 * (c % 2) + k, 32 * (b - a), [(side("qw", "sw", 16 + 128 * k, 128), side("qz", "sz", o, 32 * (b - a)))])
 
         def times32(c):
             a, b = chunks[c]
@@ -586,7 +799,8 @@ def rank_program(g, core, T, topo):
         def state(c):
             a, b = chunks[c]
             for k in range(4):
-                tt(at("xs", s_[:, 8 * a:8 * b, k:16:4]), bank(4 * (c % 2) + k, 0, 32 * (b - a)), at("z32", s_[:, 128 * a + k:128 * b:4]), A.add)
+                n = max(128, 32 * (b - a))
+                tt(at("xs", s_[:, 8 * a:8 * b, k:16:4]), bank(4 * (c % 2) + k, n - 32 * (b - a), n), at("z32", s_[:, 128 * a + k:128 * b:4]), A.add)
 
         def scaled(e, j):
             o = X0 + 128 * j
@@ -598,7 +812,7 @@ def rank_program(g, core, T, topo):
                     copy(e, w(o + 64 * x, o + 64 * x + 64), at("xs", s_[:, 96:112, k:k + 4]), SC)
         for c in range(len(chunks)):
             late(("vs", "sv", "s")[c], c)
-            place(("vvvs", "vvvv", "vvvv")[c], c)
+            place("vvvv" if c else "vvvs", c)
             codes(c)
             times32(c)
             state(c)
@@ -611,7 +825,7 @@ def rank_program(g, core, T, topo):
                 scaled("v", j)
             own(1)
             own(2)
-            rows.update(range(first, len(jobs)))
+            rows.update(range(first + 1, len(jobs)))
             windows()
             for c in range(3):
                 keys(c)
@@ -634,29 +848,31 @@ def rank_program(g, core, T, topo):
     copy("s", small("g6"), small("tf"), -8 / TS, sc(11))
     ts(small("g1"), small("tf"), 1 / (XE * TS), A.mult, sc(8), A.add)
 
-    def unlay(es, p0, n, u0):
+    def unlay(es, q):
         for k in range(3):
-            copy(es[k], at("xl", s_[:, p0:p0 + n, 16 * k:16 * k + 16]), at("xs", s_[:, u0 + n * k:u0 + n * k + n]), SC)
-        for q in range(p0 // 8, (p0 + n) // 8):
-            copy(es[3], at("xl", s_[:, 8 * q:8 * q + 8, 48:56]), at("xs", s_[:, 48 + q // 2 * 8:56 + q // 2 * 8, q % 2 * 8:q % 2 * 8 + 8]), SC)
+            u = 8 * (EIGHTS[q][1] - 3 + k)
+            copy(es[k], at("xo", s_[:, 8 * q:8 * q + 8, 16 * k:16 * k + 16]), at("xs", s_[:, u:u + 8]), SC)
+        u = 56 * (q // 2)
+        copy(es[3], at("xo", s_[:, 8 * q:8 * q + 8, 48:56]), at("xs", s_[:, u:u + 8, q % 2 * 8:q % 2 * 8 + 8]), SC)
 
     def result(e, c):
-        quant("qx", "sx", 224 * c, 224 * c + 224, at("xl", s_[:, 16 * c:16 * c + 16]))
-        mm(4 + c, 224, [(side("qv", "sv", 0, 128), side("qx", "sx", 224 * c, 224))])
-        copy(e, at("ys", s_[:, 224 * c:224 * c + 224]), bank(4 + c, 0, 224))
+        a, b = ENDS[c]
+        quant("qx", "sx", M * a, M * b, at("xo", s_[:, a:b]))
+        mm(c, M * (b - a), [(side("qv", "sv", 0, 128), side("qx", "sx", M * a, M * (b - a)))])
+        copy(e, at("ys", s_[:, M * a:M * b]), bank(c, 0, M * (b - a)))
+    ENDS = [(0, 16), (16, 32)]
     ts(small("g2"), small("g1"), float(C - M), A.mult, sc(9), A.add)
     tt(small("g2"), small("g2"), small("g3"), A.add)
     ts(small("g2"), small("g2"), 8.0 * C - 1, A.min)
     tt(small("g4"), small("g4"), small("g6"), A.min)
     tt(small("g5"), small("g2"), small("g4"), A.max)
-    dmas("og", [("y", hbm(T.og[1 - s:8:2, :]), at("g5", s_[:, G * s + 1:G * s + G])) for s in range(2)], 3.0)
-    unlay("ssss", 0, 16, 0)
-    unlay("vvsv", 16, 16, 64)
+    dmas("og", [("y", hbm(T.og[1 - s:8:2, :]), at("g5", s_[:, G * s:G * s + M])) for s in range(2)], 3.0)
+    for q in range(4):
+        unlay(("ssss", "ssss", "vvss", "vsvv")[q], q)
     for c in range(2):
         result("sv"[c], c)
-    dmas("out", [("y", hbm(T.oc[:, 0:896]), at("qx", s_[:, 0:224], True)),
-                 ("s", hbm(T.y[:, 0:224]), at("ys", s_[:, 0:224]))], 1.0)
-    dmas("end", [("y", hbm(T.oc[:, 896:XE]), at("qx", s_[:, 224:C], True))]
-         + [("y", hbm(T.osc[4 * k:4 * k + 4, :]), at("sx", s_[32 * k:32 * k + 4])) for k in range(4)]
-         + [("y", hbm(T.y[:, 224:C]), at("ys", s_[:, 224:C]))], 1.0)
+    oc = [("y", hbm(T.oc[:, 4 * M * a:4 * M * b]), at("qx", s_[:, M * a:M * b], True)) for a, b in ENDS]
+    ys = [(e, hbm(T.y[:, M * a:M * b]), at("ys", s_[:, M * a:M * b])) for e, (a, b) in zip("sy", ENDS)]
+    dmas("out", oc + [("y", hbm(T.osc[4 * k:4 * k + 4, :]), at("sx", s_[32 * k:32 * k + 4])) for k in range(4)], 1.6)
+    dmas("end", ys, 1.6)
     issue()

import numpy as np
from concourse.bass import DstId, RemoteDMATransfer
from concourse.mybir import dt, AluOpType, ActivationFunctionType

A = AluOpType
AF = ActivationFunctionType
s_ = np.s_
C, M, P, V, R = 448, 14, 32, 6, 3
XE = 4 * C
X0 = 3 * XE
HB = 11 * XE
KB = 32
BIG = float(2 ** 96)
TS = 2.0 ** -16
SC = 0.03125
G = 16
L = 6 * G
APART = 0
LT = L + 24
QUAD = [0, 2, 1, 3]
EIGHTS = [(0, 4, 0, 0), (4, 7, 2, 1), (7, 11, 1, 0), (11, 14, 3, 1)]
CYCLE = 0.00083
PACES = [(1.0, 0.21, 0.8, 1.56, 1.2, 0.25, 2.0), (1.0, 0.2, 0.6, 1.2, 0.5, 0.7, 1.6), (1.1, 0.22, 0.9, 2.0, 1.0, 0.9, 2.6),
         (1.25, 0.21, 0.7, 1.56, 0.6, 1.1, 1.6), (1.25, 0.18, 0.9, 1.2, 1.3, 0.4, 2.0), (1.45, 0.21, 0.7, 1.8, 0.9, 0.5, 2.0),
         (1.5, 0.21, 0.9, 1.5, 0.7, 0.8, 2.0)]
PLANS = [(slow, wake, tensor, 1.56, send, fly, early) for slow in (1.0, 1.1) for wake in (0.19, 0.21, 0.23) for tensor in (0.5, 0.8)
         for send, fly in ((1.0, 0.7), (0.6, 0.8)) for early in (1.0, 1.5)]
TRIES, SLACK = 70000, 0.004
SPAN = 50
PASSES, BIAS = 5, 0.02
CHOSEN = []
CD, BF, F, U8, U16, I32 = "float8_e4m3fn_x4", "bfloat16", "float32", "uint8", "uint16", "int32"

SCRATCH = {"ps": ("psum", [128, 4096], F)}
for _n, _s, _d in [
        ("W", [HB + 8 * KB], BF), ("zz", [M, 128], BF), ("z32", [XE], BF), ("xs", [112, 16], BF), ("lt", [C], BF),
        ("xl", [P, 4 * M], BF), ("xo", [P, 4 * M], BF), ("us", [4, 128], BF), ("vs", [512], BF), ("zt", [512], BF), ("one", [256], BF), ("gt", [1024], BF),
        ("bt", [640], BF), ("dtl", [512], BF),
        ("qx", [C], CD), ("sx", [C], U8), ("qz", [512], CD), ("sz", [512], U8), ("qu", [128], CD), ("su", [128], U8),
        ("qv", [128], CD), ("sv", [128], U8), ("qw", [528], CD), ("sw", [528], U8), ("qg", [256], CD), ("sg", [256], U8),
        ("qb", [256], CD), ("sb", [384], U8), ("qn", [128], CD), ("qd", [160], CD), ("sd", [160], U8),
        ("kt", [C], F), ("ys", [C], F), ("rb", [2 * L], F), ("sq", [4 * L], F), ("nx", [2], F), ("ob", [30], F),
        ("gy", [2 * LT], F), ("em", [4 * L], F), ("tl", [3 * LT], F),
        ("ti", [32], F), ("lb", [V * L], F), ("lq", [96], F), ("tf", [30], F), ("wt", [V], F),
        ("blk", [320], F), ("col", [320], F), ("pat", [48], F), ("sc", [16], F), ("mk", [64], F),
        ("bx", [2, 16], F), ("tb", [96], F), ("ex", [128], F), ("a3", [10, 2, 8], F), ("stg", [8, 2, 2], F),
        ("g1", [32], I32), ("g2", [32], F), ("g3", [32], F), ("g4", [32], F), ("g5", [32], F), ("g6", [32], F),
        ("lbs", [4], U16), ("lex", [8], U16), ("offb", [32], U16), ("offz", [112], U16), ("offl", [28], U16)]:
    SCRATCH[_n] = ("sbuf", [128] + _s, _d)
SEMAPHORES = ["v", "s", "t", "g", "lx", "lu", "lw", "lv", "lp", "w0", "w1", "w2", "sent0", "sent1", "og", "out", "end"]
for _n in ("00", "01", "11", "21"):
    SCRATCH["ql" + _n] = ("sbuf", [128, KB + 128], CD)
    SCRATCH["sl" + _n] = ("sbuf", [128, 320], U8)
    SEMAPHORES.append("arr" + _n)


def rank_program(g, core, T, topo):
    rank = T.rank_of(core)
    if rank is None:
        return
    N = len(T.cores)
    S = T.sem
    eng = {"v": g.vector, "s": g.scalar, "t": g.tensor, "g": g, "y": g.sync}
    vec, act, pe = g.vector, g.scalar, g.tensor
    u8 = dt.uint8

    jobs = []
    wrote = {}
    seen = {}
    count = {}
    rows = set()

    def at(name, idx=s_[:], raw=False):
        idx = idx if isinstance(idx, tuple) else (idx,)
        shape = SCRATCH[name][1]
        lo, hi, _ = idx[0].indices(128)
        cols = np.arange(int(np.prod(shape[1:]))).reshape(shape[1:])[idx[1:]].ravel()
        cycles = len(cols) * (0.5 if SCRATCH[name][2] in (BF, U16) else 1.0)
        if name == "ps":
            cols, lo, hi = np.arange(cols[0] // 512 * 512, cols[0] // 512 * 512 + 512), 0, 128
        mask = np.zeros((8, int(np.prod(shape[1:]))), bool)
        mask[np.ix_(range(lo // 16, -(-hi // 16)), cols)] = True
        ap = T[name][idx if len(idx) > 1 else idx[0]]
        return (ap.bitcast(u8) if raw else ap, [(name, mask)], cycles, (lo, hi))

    def hbm(ap):
        return (ap, [], 0, None)

    def pick(win, off):
        return (win[0].indirect(off[0]), win[1] + off[1], 32 * off[2], None)

    def job(e, outs, ins, call, hold, more=0.0, token=None, picks=0):
        if jobs and jobs[-1].get("open"):
            jobs[-1]["can"][e] = (call, hold)
            return
        ins = [v for v in ins if isinstance(v, tuple)]
        reads = [r for v in ins for r in v[1]]
        writes = [r for v in outs for r in v[1]]
        deps = set()
        for name, mask in reads + writes:
            if name in wrote:
                deps.update(int(k) for k in np.unique(wrote[name][mask]) if k >= 0)
            if name == "ps":
                deps.update(k for k, m in seen.get(name, []) if jobs[k]["e"] != e and (m & mask).any())
        for name, mask in writes:
            deps.update(k for k, m in seen.get(name, []) if (m & mask).any())
            seen[name] = [(k, m & ~mask) for k, m in seen.get(name, []) if (m & ~mask).any()]
            wrote.setdefault(name, np.full(mask.shape, -1, np.int32))[mask] = len(jobs)
        for name, mask in reads:
            seen.setdefault(name, []).append((len(jobs), mask))
        deps.discard(len(jobs))
        jobs.append({"e": e, "can": {e: (call, hold)}, "deps": deps, "picks": picks, "more": more, "token": token, "mates": [len(jobs)]})

    def do(e, outs, ins, call, hold=None):
        picks = 0
        if hold is None and ins and ins[0][3] is None:
            hold, picks = 0.065 if e == "s" else 0.05, ins[0][2]
        elif hold is None:
            views = [v for v in outs + ins if isinstance(v, tuple)]
            wide = [v for v in views if v[2] > 1]
            narrow = e == "v" and all(SCRATCH[v[1][0][0]][2] in (BF, U16) for v in wide)
            cycles = max(v[2] * (2 if SCRATCH[v[1][0][0]][2] in (BF, U16) and not narrow else 1) for v in views)
            hold = max(78 if e == "s" else 64, cycles) * CYCLE
        job(e, outs, ins, call, hold, picks=picks)

    def either(*ways):
        ways[0]()
        jobs[-1]["open"] = True
        for way in ways[1:]:
            way()
        jobs[-1]["open"] = False

    def dmas(sem, items, more):
        count[sem] = count.get(sem, 0) + 16 * len(items)
        mates = list(range(len(jobs), len(jobs) + len(items)))
        for e, out, in_ in items:
            job(e, [out], [in_], lambda e=e, out=out, in_=in_: eng[e].dma_start(out[0], in_[0]).then_inc(S[sem], 16), 0.05, more, (sem, count[sem]))
            jobs[-1]["mates"] = mates

    def issue():
        n = len(jobs)
        users = [{} for _ in jobs]
        prev = {}
        for k, j in enumerate(jobs):
            j["deps"] = set(m for d in j["deps"] for m in jobs[d]["mates"] if m < k)
            if j["e"] in "gy" and len(j["can"]) == 1:
                if j["e"] in prev:
                    users[prev[j["e"]]][k] = False
                prev[j["e"]] = k
            for d in j["deps"]:
                users[d][k] = True

        def times(pace):
            slow, wake, tensor, gather, send, fly, first = pace
            hold = [{e: send + h if j["more"] == "sent" else (h + gather * CYCLE * j["picks"]) * {"t": tensor, "y": 1.0}.get(e, slow)
                     for e, (_, h) in j["can"].items()} for j in jobs]
            more = [{"sent": fly, "late": fly, "early": fly + 0.4, "first": fly + first}.get(j["more"], j["more"]) + wake for j in jobs]
            return hold, more

        def plan(pace):
            hold, more = times(pace)
            hold, wake = [h[j["e"]] for h, j in zip(hold, jobs)], 0.0
            way, left = [0.0] * n, [0] * n
            for k in range(n - 1, -1, -1):
                way[k] = hold[k] + max([more[k]] + [way[u] + (more[k] + wake) * waits for u, waits in users[k].items()])
                for u in users[k]:
                    left[u] += 1
            ready, free, order = [0.0] * n, {e: 0.0 for e in eng}, []
            pool = [k for k in range(n) if not left[k]]
            while pool:
                e = jobs[min(pool, key=lambda k: max(ready[k], free[jobs[k]["e"]]))]["e"]
                mine = [k for k in pool if jobs[k]["e"] == e]
                now = max(free[e], min(ready[k] for k in mine))
                k = max((k for k in mine if ready[k] <= now), key=lambda k: way[k])
                for h in mine:
                    if now < ready[h] < now + hold[k] and now + hold[k] + way[h] > max(ready[h] + way[h], ready[h] + hold[h] + way[k]):
                        k, now = h, ready[h]
                pool.remove(k)
                order.append(k)
                free[e] = now + hold[k]
                for u, waits in users[k].items():
                    ready[u] = max(ready[u], free[e] + (more[k] + wake) * waits)
                    left[u] -= 1
                    if not left[u]:
                        pool.append(u)
            return order

        def refine():
            timed = [times(p) for p in PACES]
            hold = [{e: np.array([h[k][e] for h, _ in timed]) for e in jobs[k]["can"]} for k in range(n)]
            more = np.array([m for _, m in timed]).T
            weight = np.array([1 / p[0] for p in PACES])
            hard, behind = [], []
            for j in jobs:
                far = 0
                for d in j["deps"]:
                    far |= behind[d]
                hard.append(sorted(d for d in j["deps"] if not far >> d & 1))
                behind.append(far | sum(1 << d for d in j["deps"] if not far >> d & 1))
            soft = [[] for _ in jobs]
            for d in range(n):
                for k, waits in users[d].items():
                    if not waits:
                        soft[k].append(d)
            zero = np.zeros(len(PACES))

            def lasts(order, on, end, done, start, chain=(), room=0.0, until=n):
                free, moved = {}, set()
                for k in reversed(order[:start]):
                    free.setdefault(on[k], end[k])
                    if len(free) == len(eng):
                        break
                for i in range(start, n):
                    k = order[i]
                    t = free.get(on[k], zero)
                    for d in hard[k]:
                        t = np.maximum(t, done[d])
                    t = t + hold[k][on[k]]
                    if i > start + 70 and k in chain:
                        by = t - end[k]
                        if by @ weight > room:
                            return np.inf
                        end[order[i:]] += by
                        done[order[i:]] += by
                        break
                    if until < n:
                        if max(map(abs, (t - end[k]).tolist())) > 1e-9:
                            moved.add(on[k])
                            until = max([until] + [where[u] + 1 for u in users[k]])
                        else:
                            moved.discard(on[k])
                            if i > until and not moved:
                                break
                    free[on[k]] = end[k] = t
                    done[k] = t + more[k]
                return float(done.max(axis=0) @ weight)

            def places():
                where, ahead, last = {k: i for i, k in enumerate(order)}, {}, {}
                for k in order:
                    ahead[k] = last.get(on[k])
                    last[on[k]] = k
                return where, ahead

            def chains():
                stood, common = [], None
                for p in range(len(PACES)):
                    k, chain = int(done[:, p].argmax()), set()
                    while k is not None:
                        chain.add(k)
                        d = max(hard[k], key=lambda x: done[x, p], default=None)
                        if d is not None and done[d, p] > end[k, p] - hold[k][on[k]][p] - 1e-9:
                            k = d
                        else:
                            if ahead[k] is not None:
                                stood.append(k)
                            k = ahead[k]
                    common = chain if common is None else common & chain
                return stood, common
            on = [j["e"] for j in jobs]
            end, done = np.zeros((n, len(PACES))), np.zeros((n, len(PACES)))

            def fit(k, t0, p, busy, queues, first, bias):
                found = []
                for e in queues:
                    t, h, row = t0, hold[k][e][p], busy[e]
                    i = len(row)
                    while i and row[i - 1][1] > t0:
                        i -= 1
                    while i < len(row) and row[i][0] < t + h - 1e-9:
                        t, i = max(t, row[i][1]), i + 1
                    found.append((t + h + bias * (e != first), t, h, i, e))
                _, t, h, i, e = min(found)
                busy[e].insert(i, (t, t + h))
                return t + h, e

            def pack(rank, p, on, back):
                busy, ends, to = {e: [] for e in eng}, [0.0] * n, [None] * n
                for k in rank:
                    if back:
                        t0 = max([more[k, p]] + [ends[u] + more[k, p] * waits for u, waits in users[k].items()])
                    else:
                        t0 = max([0.0] + [ends[d] + more[d, p] for d in hard[k]] + [ends[d] for d in soft[k]])
                    ends[k], to[k] = fit(k, t0, p, busy, [on[k]] if on else jobs[k]["can"], jobs[k]["e"], BIAS)
                if back:
                    return sorted(range(n), key=lambda k: (-ends[k], k)), to
                return sorted(range(n), key=lambda k: (ends[k] - hold[k][to[k]][p], k)), to, sorted(range(n), key=lambda k: (-ends[k], -k))
            best = min((lasts(order, on, end, done, 0), order, on) for order in map(plan, PLANS))
            for p, pace in enumerate(PACES):
                for free in (False, True):
                    rank, to = plan(pace), on
                    for _ in range(PASSES):
                        order, to, rank = pack(rank, p, None if free else to, False)
                        best = min(best, (lasts(order, to, end, done, 0), order, to))
                        rank, to = pack(rank, p, to, True)
            now, order, on = best
            lasts(order, on, end, done, 0)
            rng = np.random.default_rng(0)
            where, ahead = places()
            stood, common = chains()
            taken = 0
            for i in range(TRIES):
                room = -SLACK * (1 - i / TRIES) * float(np.log(rng.random() + 1e-12))
                k = stood[int(rng.integers(len(stood)))]
                h = ahead[k]
                if h is None:
                    continue
                new, to = list(order), list(on)
                move = int(rng.integers(6))
                if move > 3:
                    at_ = max(0, where[k] - int(rng.integers(SPAN)))
                    p, part = int(rng.integers(len(PACES))), order[at_:at_ + SPAN]
                    shake = 0.25 * rng.random()
                    key = {x: end[x, p] - hold[x][on[x]][p] + shake * rng.standard_normal() for x in part}
                    for x in part:
                        key[x] = max([key[x]] + [key[d] + 1e-6 for d in hard[x] + soft[x] if d in key])
                    busy, ends = {e: [] for e in eng}, {}
                    for x in reversed(order[:at_]):
                        if not busy[on[x]]:
                            busy[on[x]].append((0.0, end[x, p]))
                    for x in sorted(part, key=key.get):
                        t0 = max([0.0] + [ends[d] + more[d, p] if d in key else done[d, p] for d in hard[x]] + [ends[d] for d in soft[x] if d in key])
                        ends[x], to[x] = fit(x, t0, p, busy, jobs[x]["can"], on[x], 0.3 * rng.random())
                    new[at_:at_ + SPAN] = sorted(part, key=lambda x: (ends[x] - hold[x][to[x]][p], key[x]))
                elif move == 0:
                    for _ in range(int(rng.integers(3))):
                        h = ahead[h] if ahead[h] is not None else h
                    at_ = max([where[h]] + [where[d] + 1 for d in hard[k] + soft[k]])
                    new.insert(at_, new.pop(where[k]))
                elif move == 1:
                    at_ = min([where[k] + int(rng.integers(12))] + [where[u] - 1 for u in users[h]] + [n - 1])
                    new.insert(at_, new.pop(where[h]))
                    at_ = where[h]
                else:
                    x = (k, h)[move - 2]
                    others = [e for e in jobs[x]["can"] if e != on[x]]
                    if not others:
                        continue
                    to[x], at_ = others[int(rng.integers(len(others)))], where[x]
                end2, done2 = end.copy(), done.copy()
                t = lasts(new, to, end2, done2, at_, common, room + 1e-9, where[k] + SPAN + 1)
                if t <= now + room + 1e-9:
                    order, on, end, done = new, to, end2, done2
                    where, ahead = places()
                    now, taken = t, taken + 1
                    if taken % 20 == 0 or now < best[0] - 0.05:
                        now = lasts(order, on, end, done, 0)
                        stood, common = chains()
                        if now < best[0]:
                            best = (now, order, on)
            return best[1:]
        if not CHOSEN:
            CHOSEN.extend(refine())
        known = {e: {} for e in eng}
        clock = {}
        for k in CHOSEN[0]:
            j = jobs[k]
            e = CHOSEN[1][k]
            j["call"] = j["can"][e][0]
            need = {}
            for d in j["deps"]:
                sem, c = jobs[d]["token"]
                need[sem] = max(need.get(sem, 0), c)
            for sem in sorted(need, key=lambda x: x != e):
                if known[e].get(sem, 0) < need[sem]:
                    eng[e].wait_ge(S[sem], need[sem])
                    for x, c in clock.get((sem, need[sem]), {}).items():
                        known[e][x] = max(known[e].get(x, 0), c)
                    known[e][sem] = need[sem]
            if j["token"] is None:
                count[e] = count.get(e, 0) + 1
                j["token"] = (e, count[e])
                j["call"]().then_inc(S[e], 1)
                clock[j["token"]] = dict(known[e])
            else:
                j["call"]()
        for sem in count:
            if known["y"].get(sem, 0) < count[sem]:
                g.sync.wait_ge(S[sem], count[sem])

    def arg(v):
        return v[0] if isinstance(v, tuple) else v

    def iota(out, pattern, base=0, cm=0):
        do("g", [out], [], lambda: g.iota(out[0], pattern, base, cm, allow_small_or_imprecise_dtypes=True),
           0.13 + 2 * CYCLE * int(np.prod([c for _, c in pattern])))

    def copy(e, out, in_, scale=None, bias=None, func=AF.Identity, only=False):
        if func == AF.Identity and not only:
            either(*[lambda x=x: copy(x, out, in_, scale, bias, func, True) for x in dict.fromkeys(e + "vs")])
        elif e == "g":
            n = int(out[1][0][1].sum(axis=1).max())
            do(e, [out], [in_], lambda: g.affine_select(out[0], in_[0], [[0, n]], A.is_gt, 0.0, 1, 0), 0.17 + 2 * CYCLE * n)
        elif e == "v":
            if scale is None and bias is None:
                do(e, [out], [in_], lambda: vec.tensor_copy(out[0], in_[0]))
            elif bias is None:
                ts(out, in_, scale, A.mult)
            elif scale is None:
                ts(out, in_, bias, A.add)
            else:
                ts(out, in_, scale, A.mult, bias, A.add)
        elif scale is None and bias is None:
            do(e, [out], [in_], lambda: act.activation(out[0], in_[0], AF.Copy))
        else:
            do(e, [out], [in_, scale, bias], lambda: act.activation(
                out[0], in_[0], func, bias=0.0 if bias is None else arg(bias), scale=1.0 if scale is None else arg(scale)))

    def ts(out, in0, s1, op0, s2=None, op1=None):
        if s2 is None:
            do("v", [out], [in0, s1], lambda: vec.tensor_scalar(out[0], in0[0], arg(s1), None, op0))
        else:
            do("v", [out], [in0, s1, s2], lambda: vec.tensor_scalar(out[0], in0[0], arg(s1), arg(s2), op0, op1))

    def tt(out, in0, in1, op):
        do("v", [out], [in0, in1], lambda: vec.tensor_tensor(out[0], in0[0], in1[0], op))

    def tr(out, in_):
        do("v", [out], [in_], lambda: vec.transpose(out[0], in_[0]))

    def scan(out, d0, d1, init, op0=A.add, op1=A.max):
        do("v", [out], [d0, d1], lambda: vec.tensor_tensor_scan(out[0], d0[0], d1[0], init, op0, op1))

    def quant(q, s, a, b, in_, sa=None):
        qv, sv = at(q, s_[:, a:b]), at(s, s_[:, a:b] if sa is None else s_[:, sa:sa + b - a])
        do("v", [qv, sv], [in_], lambda: vec.quantize_mx(qv[0], sv[0], in_[0]), 0.012 + 0.00088 * (b - a))

    def fill(out, val):
        do("v", [out], [], lambda: vec.memset(out[0], val))

    def put(out, n, val):
        copy("s", out, at("zt", s_[out[3][0]:out[3][1], 0:n]), bias=val)

    def bank(b, a, n, step=1):
        return at("ps", s_[:, 512 * b + a:512 * b + n:step])

    def side(q, s, a, n, sa=None):
        return at(q, s_[:, a:a + n]), at(s, s_[:, a:a + n] if sa is None else s_[:, sa:sa + n])

    def mm(b, n, pairs):
        out = bank(b, 0, n)
        do("t", [out], [v for l, r in pairs for v in l + r], lambda: [
            pe.matmul_mx(out[0], l[0][0], l[1][0], r[0][0], r[1][0], i == 0, i == len(pairs) - 1) for i, (l, r) in enumerate(pairs)][-1],
           len(pairs) * (n + 16) * CYCLE)

    def w(a, b, step=1, lo=0, hi=128):
        return at("W", s_[lo:hi, a:b:step])

    def windows():
        for sem, ds, more in (("w0", (1, -1, -2, -3), 2.0), ("w1", (2, 3, 4, 5), 3.5), ("w2", (6, 7), 4.0)):
            items = []
            for d in ds:
                lo, hi = (0, 128 - 16 * d) if d >= 0 else (-16 * d, 64)
                items.append(("y", w(X0 + d * XE, X0 + d * XE + XE, 1, lo, hi), w(X0, X0 + XE, 1, lo + 16 * d, hi + 16 * d)))
            dmas(sem, items, more)

    dmas("lx", [(e, at("xl", s_[64 * k:64 * k + 64]), hbm(T.x[64 * k:64 * k + 64, :])) for k, e in enumerate("ys")], 1.6)
    dmas("lu", [("y", at("us", s_[:, k:k + 3:2, :]), hbm(T.u[:, 256 * k:256 * k + 256])) for k in range(2)], 2.2)

    def blk(k, a=0, b=32):
        return at("blk", s_[:, 32 * k + a:32 * k + b])

    def col(k, lo=0, hi=128):
        return at("col", s_[lo:hi, 32 * k:32 * k + 1])

    def sc(k, lo=0, hi=128):
        return at("sc", s_[lo:hi, k:k + 1])
    iota(at("ti"), [[-XE, 2], [128, G]], XE - 128, 4)
    iota(blk(4), [[16, 4], [2 * XE, 4], [-4 * KB, 2]], 9 * XE + 4 * KB - 4 * 96, 4)
    iota(blk(0), [[-XE, 2], [0, 4], [1, 4]], 0, -XE // 16)
    iota(blk(1), [[0, 32]])
    for h in range(2):
        iota(blk(2, 16 * h, 16 * h + 16), [[0, 2], [64, 2], [128, 4]], 16 * h, 1)
        iota(blk(9, 16 * h, 16 * h + 16), [[0, 2], [64, 2], [128, 4]], 528 * h, 1)
    iota(blk(3), [[0, 2], [1, 4], [0, 4]])
    iota(blk(5), [[0, 4], [1, 2], [0, 4]])
    iota(blk(6), [[1, 2], [0, 16]])
    iota(blk(7), [[0, 2], [1, 2], [0, 8]])
    iota(blk(8), [[1, 32]])
    iota(at("pat", s_[:, 4:10]), [[4, 3], [-G, 2]], G)
    iota(at("pat", s_[:, 10:12]), [[-G, 2]], G + 12)
    iota(at("pat", s_[:, 16:48]), [[0, 2], [1, 2], [0, 8]])
    iota(at("one"), [[0, 256]], 1)
    for b in range(4):
        out = at("gt", s_[:, 256 * b:256 * b + 256])
        do("g", [out], [at("one")], lambda out=out, b=b: g.affine_select(out[0], T.one[:], [[1, 256]], A.is_equal, 0.0, -b, -4), 0.6)
    iota(at("bt", s_[:, 256:640]), [[0, 384]])

    fill(at("zt"), 0.0)
    fill(at("gy"), 0.0)
    fill(at("tl"), 0.0)
    fill(at("sq", s_[:, 0:4 * L:2]), -BIG)
    fill(at("tb", s_[64:128]), 0.0)
    quant("qn", "sb", 0, 128, at("zt"))
    for name, k, val in (("sq", 3, 0.0), ("em", 0, 0.0)):
        put(at(name, s_[:, k:4 * L:6]), 64, val)
    put(at("rb"), 2 * L, -BIG / 4)
    put(at("gy", s_[:, 48:2 * LT:LT]), 2, -BIG)
    for k in range(2):
        put(at("gy", s_[:, LT * k + 46:LT * k + 95:48]), 2, -1.0)
    put(at("lq", s_[0:64, 80:96]), 16, 0.0)

    for a in range(4):
        q0 = 32 * QUAD[a]
        put(sc(0, q0, q0 + 32), 1, (2 * a * XE - 4 * q0) * TS)
    put(sc(2, 0, 96), 1, 1 / TS)
    put(sc(2, 96, 128), 1, 0.0)
    put(sc(3, 96, 128), 1, 0.0)
    put(sc(4, 0, 64), 1, 1 / TS)
    put(sc(4, 64, 128), 1, 0.0)
    put(sc(5, 64, 128), 1, float(X0))
    for s in range(2):
        copy("s", at("tl", s_[:, 48 * s + 3:48 * s + 45:3]), at("ti", s_[:, G * s + 1:G * s + 15]), TS, sc(0))

    def columns():
        put(at("dtl", s_[:, 4 * KB:512]), 512 - 4 * KB, 0.0)
        quant("qd", "sd", 0, 128, at("zt"))
        for n, k, m in ((0, 0, 2), (2, 19, 1), (3, 18, 1), (4, 17, 1), (5, 16, 1)):
            copy("s", at("wt", s_[96:128, n:n + m]), at("col", s_[96:128, 128 + k:128 + k + m]), TS)
        copy("s", sc(3, 0, 96), col(0, 0, 96))
        copy("s", sc(5, 0, 64), col(0, 0, 64), bias=float(X0))
        for k in range(2):
            copy("s", sc(6 + k), col(6 + k), -BIG)
            copy("s", at("mk", s_[:, 32 * k:32 * k + 32]), at("pat", s_[:, 16:48]), BIG, sc(6 + k), AF.Abs)

    def lists(n):
        if n:
            ts(at("lbs", s_[:, 0:1]), col(2), 0.0625, A.mult, 31.0, A.min)
            ts(at("lbs", s_[:, 2:3]), col(9), 0.0625, A.mult, 63.0, A.min)
            return
        ts(at("lex", s_[:, 0:6]), at("pat", s_[:, 4:10]), col(3), A.add)
        ts(at("lex", s_[:, 6:8]), at("pat", s_[:, 10:12]), col(5), A.add)

    U = side("qu", "su", 0, 128)
    RUNS = [(0, 4), (8, 14), (4, 8)]

    def own(c):
        a, b = RUNS[c]
        quant("qx", "sx", 32 * a, 32 * b, w(X0 + 128 * a, X0 + 128 * b))

    def keys(c):
        a, b = RUNS[c]
        mm(4 + c, 32 * (b - a), [(U, side("qx", "sx", 32 * a, 32 * (b - a)))])

    def turn(c):
        a, b = RUNS[c]
        tr(at("kt", s_[:, 32 * a:32 * b]), bank(4 + c, 0, 32 * (b - a)))
    for e, js in (("s", range(4, 9)), ("v", range(0, 4)), ("v", range(9, M))):
        for j in js:
            copy(e, w(X0 + 128 * j, X0 + 128 * j + 128), at("xl", s_[:, :, 4 * j:4 * j + 4]))
    windows()
    dmas("lw", [("y", at("qw", s_[:, 16:528], True), hbm(T.wc[:])), ("y", at("sw", s_[:, 16:528]), hbm(T.ws[:])),
                ("y", at("qw", s_[:, 0:16], True), hbm(T.wc[:, 0:64])), ("y", at("sw", s_[:, 0:16]), hbm(T.ws[:, 0:16]))], 5.0)
    for k in range(2):
        quant("ql0%d" % k, "sl0%d" % k, KB, KB + 128, at("zt"), 128)
    own(0)
    own(1)
    quant("qu", "su", 0, 128, at("us"))
    own(2)
    for c in range(3):
        keys(c)
    for a, b in ((0, 160), (160, 224), (224, 320)):
        tr(at("col", s_[:, a:b]), at("blk", s_[:, a:b]))
    columns()
    lists(0)
    lists(1)
    for i in range(2):
        quant("qg", "sg", 128 * i, 128 * i + 128, at("gt", s_[:, 512 * i:512 * i + 512]))
    for c in range(3):
        turn(c)

    for t in range(R):
        last = t == R - 1

        def run(name, n, a, b, step=1, size=L, lo=0, hi=128):
            o = size * (n % 2)
            return at(name, s_[lo:hi, o + a:o + b:step])

        def gates(n, a, b, step=1, lo=0, hi=128):
            return run("gy", n, a, b, step, LT, lo, hi)

        def one(name, n, k, lo=0, hi=128):
            return run(name, n, k, k + 1, 1, L, lo, hi)

        def six(name, n, a, b, step=6, lo=0, hi=128):
            return run(name, n, a, b, step, 2 * L, lo, hi)

        def top(n, s, lo=0, hi=128):
            return one("rb", n, 48 * s + 44, lo, hi)

        def largest(n):
            if n:
                for a, b in ((3, 95),) if n <= APART else ((51, 95), (3, 45)):
                    scan(run("rb", n, a, b), run("rb", n - 1, a, b), six("sq", n - 1, 2 * a, 2 * b, 2), -BIG / 4, A.min, A.max)
                return
            put(run("rb", 0, 3, L, 3), 31, BIG)
            for s in (1, 0):
                scan(run("rb", 0, 48 * s + 5, 48 * s + 45, 3), at("zt", s_[:, 0:M]), at("kt", s_[:, 16 - 16 * s:C:32]), -BIG)
                copy("s", six("sq", 0, L * s + 6, L * s + 90), at("kt", s_[:, 16 - 16 * s:C:32]))

        def before(n, s):
            ts(gates(n, 48 * s + 3, 48 * s + 48, 3), run("rb", n, 48 * s + 2, 48 * s + 45, 3), top(n, s), A.is_lt, -BIG, A.mult)

        def lift(n, s):
            out, in_ = gates(n, 48 * s + 5, 48 * s + 45, 3), run("rb", n, 48 * s + 2, 48 * s + 42, 3)
            either(lambda: copy("s", out, in_, -1.0, top(n, s), AF.Sign), lambda: ts(out, in_, top(n, s), A.is_lt))

        def cut(n):
            end = 93 if n else 96
            for a, b in ((3, end),) if n < APART else ((51, end), (3, 45)):
                tt(run("rb", n, a + 1, b, 3), run("rb", n, a - 1, b - 3, 3), gates(n, a + 3, b + 3, 3), A.subtract)

        def enter(n):
            for lo, hi, fr in ((0, 64, 64), (64, 96, 32)):
                copy("s", six("sq", n, 8, 90, 6, lo, hi), at("zt", s_[lo:hi, 0:M]), bias=one("rb", n, 94 if n else 92, fr, fr + hi - lo))
            if n:
                ts(six("sq", n, 104, 190), at("zt", s_[:, 0:M + 1]), top(n, 0), A.add, six("sq", n - 1, 8, 9), A.max)
            else:
                copy("v", six("sq", n, 104, 190), at("zt", s_[:, 0:M + 1]), bias=top(n, 0))

        def held(n):
            copy("s", at("nx"), six("sq", n, 8, 105, L), -1.0)
            for s in range(2):
                out, in_, new = six("sq", n, L * s + 9, L * s + 90), six("em", n, L * s + 9, L * s + 90), six("sq", n, L * s + 8, L * s + 9)
                either(lambda: copy("s", out, in_, at("nx", s_[:, s:s + 1]), new, only=True), lambda: ts(out, in_, 0.5, A.is_lt, new, A.mult))
            scan(six("sq", n + 1, 3, 183, 3), six("em", n, 6, 186, 3), six("sq", n, 6, 186, 3), 0.0, A.mult, A.add)

        def origin(n, a, b, step=1, lo=0, hi=128):
            o = LT * (2 - n % 2) if n else 0
            return at("tl", s_[lo:hi, o + a:o + b:step])

        def left(n, s, lo=0, hi=32):
            return at("lb", s_[lo:hi, L * n + 48 * s + 46:L * n + 48 * s + 47])

        def leave(n):
            scan(at("lb", s_[:, L * n + 3:L * n + 95]), gates(n, 3, 95), origin(n, 3, 95), 0.0)

        def mark(n):
            tt(six("em", n, 9, 186), gates(n, 3, 93, 3), gates(n, 6, 96, 3), A.is_equal)

        def stay(n):
            if n:
                tt(at("ob"), origin(n, 3, 93, 3), origin(n, 4, 93, 3), A.add)
            tt(origin(n + 1, 3, 93, 3), at("ob") if n else origin(0, 3, 93, 3), six("em", n, 9, 186), A.mult)

        def come(n):
            for s, lo, hi, fr in ((0, 96, 128, None), (1, 0, 128, 0), (0, 0, 64, 64), (0, 64, 96, 32)):
                out, in_ = origin(n + 1, 48 * s + 4, 48 * s + 45, 3, lo, hi), six("em", n, L * s + 9, L * s + 90, 6, lo, hi)
                new = at("wt", s_[96:128, n:n + 1]) if fr is None else left(n, 1 - s, fr, fr + hi - lo)
                either(lambda: copy("s", out, in_, -1.0, new, AF.Relu), lambda: ts(out, in_, 0.5, A.is_lt, new, A.mult))

        def final(a):
            q0 = 32 * QUAD[a]
            tt(at("tf", s_[32 * a:32 * a + 32]), origin(V, 3, 93, 3, q0, q0 + 32), origin(V, 4, 93, 3, q0, q0 + 32), A.add)

        def drawn(k, in_):
            for a in range(2):
                tr(at("tb", s_[32 * a:32 * a + 32, 32 * k:32 * k + 32]), in_)

        for n in range(V - 1):
            largest(n)
            for s in range(2):
                before(n, s)
            enter(n)
            for s in range(2):
                lift(n, s)
            cut(n)
            mark(n)
            leave(n)
            stay(n)
            come(n)
            if n < V - 2:
                held(n)
        n = V - 1
        for k, (a, b) in enumerate(((0, 4), (4, 16))):
            copy("s", at("bx", s_[0:32, :, a:b]), at("zt", s_[0:32, 0:2 * (b - a)]), bias=left(k, 1))
        for k in range(3):
            for a in range(2):
                copy("s", at("lq", s_[32 * a:32 * a + 32, 68 + 4 * k:72 + 4 * k]), at("zt", s_[0:32, 0:4]), bias=left(n - 1 - k, 1))
        largest(n)
        for s in (1, 0):
            before(n, s)
            lift(n, s)
        for a in range(2):
            scan(at("lq", s_[32 * a:32 * a + 32, 0:68]), gates(n, 51, 119, 1, 0, 32), origin(n, 51, 119, 1, 0, 32), 0.0)
        mark(n)
        leave(n)
        stay(n)
        come(n)
        for a in range(4):
            final(a)

        drawn(0, at("bx", s_[0:32]))
        tr(at("tb", s_[0:64, 32:64]), at("lq", s_[0:64, 64:96]))
        tr(at("tb", s_[0:64, 64:96]), at("lq", s_[0:64, 48:80]))
        wb = w(0, 9 * XE)
        peer = T.cores[(rank + t + 1) % N]
        rid, pid = topo.addr(peer)[0:2]
        es = topo.engines(core, peer)
        half = len(es) // 2
        masks = [sum(1 << k for k in es[:half]), sum(1 << k for k in es[half:])]
        for k in range(2):
            ts(at("offb", s_[:, 16 * k:16 * k + 16]), pick(at("tb", s_[:, 32 * k:64 * k + 32]), at("lbs", s_[:, 2 * k:2 * k + 1])),
               sc(4), A.mult, sc(5), A.add)
            if k or t:
                for h in range(2):
                    o = 128 * h + 64 * k if t else 64 * h
                    copy("sv"[h * k], at("bt", s_[:, o:o + 64]), pick(wb if k else w(0, 5 * XE), at("offb", s_[:, 16 * k + 4 * h:16 * k + 4 * h + 4])))
            else:
                copy("s", at("bt", s_[:, 128:256]), pick(w(0, 5 * XE), at("offb", s_[:, 0:8])))
            if t and not k:
                continue
            n = 2 * KB if t else KB
            quant("qb", "sb", 128 * k, 128 * k + 128, at("bt", s_[:, 128 - 128 * k:640 - 128 * k]), 128 * k + 128)
            ql, sl, arr, sent = "ql%d%d" % (t, k), "sl%d%d" % (t, k), "arr%d%d" % (t, k), "sent%d" % k
            src = [at("qb", s_[:, 128 * k:128 * k + n], True), at("sb", s_[:, 128 * k + 128 - 3 * n:128 * k + 128 + n])]
            dst = [at(ql, s_[:, 0:n], True), at(sl, s_[:, 0:4 * n])]
            writes = [RemoteDMATransfer(dst_ids=[DstId(rid=rid, pnc=pid)], dma_engine_mask=masks[i], remote_sem=S[arr],
                                        src=src[i][0], dst=dst[i][0]) for i in range(2)]
            count[sent] = count.get(sent, 0) + 2 * half
            job("g", [], src, lambda writes=writes, sent=sent: g.remote_dma_fused(writes, local_sem=S[sent]), 0.4 - 0.4 * k, "sent", (sent, count[sent]))
            count[arr] = 2 * (len(topo.engines(T.cores[(rank - t - 1) % N], core)) // 2)
            job("g", dst, [], lambda: None, 0.0, "late" if k else "early" if t else "first", (arr, count[arr]))
            for i in range(2):
                mm(4 * k + i, 128, [(side("qg", "sg", 128 * i, 128), side(ql, sl, 0, 128, 3 * n))])
                for b in range(2):
                    for h in range(2):
                        o = 512 * (4 * k + i) + n // 2 * h
                        copy("vs"[i], at("dtl", s_[64 * h:64 * h + 64, 64 * k + 64 - 2 * n + 2 * i + b:64 * k + 64:4]),
                             at("ps", s_[64 * b:64 * b + 64, o:o + n // 2]), only=True)
        tt(at("ex", s_[:, 96:128]), pick(at("tf"), at("lex", s_[:, 6:8])), at("mk", s_[:, 32 * last:32 * last + 32]), A.subtract)
        copy("s", at("ex", s_[:, 0:96]), pick(at("tf"), at("lex", s_[:, 0:6])))

        r0 = 1 if last else 0
        tr(at("a3", s_[:, 2 * r0:2 * r0 + 8]), at("ex"))
        if last:
            tt(at("a3", s_[:, 0:2, 0]), at("a3", s_[:, 8:10, 0]), at("a3", s_[:, 8:10, 1]), A.max)
            for a, b, k, x in EIGHTS:
                ts(at("offz", s_[:, 8 * a:8 * b]), at("a3", s_[:, k:k + 2 * (b - a) - 1:2, x]), sc(2), A.mult, sc(3), A.add)
        else:
            tt(at("a3", s_[:, 6]), at("a3", s_[:, 6]), at("a3", s_[:, 7]), A.max)
            ts(at("offz", s_[:, 0:96]), at("a3", s_[:, 0:6]), sc(2), A.mult, sc(3), A.add)
            ts(at("offz", s_[:, 96:112]), at("a3", s_[:, 6]), sc(2), A.mult, sc(3), A.add)
        for a in range(4):
            copy("gs", at("stg", s_[32 * a:32 * a + 32, 0:7 + r0]), at("a3", s_[96:128, 0:7 + r0, :, 2 * a:2 * a + 2]))
        wz = w(X0, X0 + 7 * XE)

        def early(e, a, b):
            for r in range(a, b):
                copy(e, at("zz", s_[:, r]), pick(wz, at("offz", s_[:, 8 * r:8 * r + 8])))
        early("s", 0, 9)
        early("v", 9, 14)
        if last:
            for a, b, k, x in EIGHTS:
                ts(at("offl", s_[:, 2 * a:2 * b]), at("stg", s_[:, k:k + 2 * (b - a) - 1:2, x]), 1 / TS, A.mult, col(0), A.add)
        else:
            ts(at("offl"), at("stg", s_[:, 0:7]), 1 / TS, A.mult, col(0), A.add)

        quant("qd", "sd", KB, KB + 128, at("dtl"))
        if t == 0:
            job("y", [], [at("qd")], lambda: None, 0.0, 0.0, ("lx", 0))
            dmas("lp", [x for r in range(1, R) for x in (
                ("y", at("ql%d1" % r, s_[:, 64:128], True), at("qn", s_[:, 0:64], True)),
                ("y", at("sl%d1" % r, s_[:, 256:320]), at("sb", s_[:, 0:64])))], 3.0)
            dmas("lv", [("y", at("vs"), hbm(T.v[:]))], 3.0)
        for b in range(4):
            mm(b, 128, [(side("qw", "sw", 16 + 128 * b, 128), side("qd", "sd", KB, 128)),
                        (side("qw", "sw", 128 * b, 128), side("qd", "sd", 0, 128))])
        for b in range(4):
            copy("vvsv"[b], w(HB + b, HB + 8 * KB, 4), bank(b, 0, 2 * KB), SC)

        chunks = [(0, 4), (4, 10), (10, 14)] if last else RUNS
        wl = w(X0, HB + 8 * KB)

        def late(es, c):
            a, b = chunks[c]
            for k, e in enumerate(es):
                a1, b1 = a + k * (b - a) // len(es), a + (k + 1) * (b - a) // len(es)
                copy(e, at("lt", s_[:, 32 * a1:32 * b1]), pick(wl, at("offl", s_[:, 2 * a1:2 * b1])))

        def place(es, c):
            a, b = chunks[c]
            for k, e in enumerate(es):
                copy(e + "g", at("zz", s_[96:128, a:b, 32 * k:32 * k + 32]), at("lt", s_[32 * k:32 * k + 32, 32 * a:32 * b]))

        def codes(c):
            a, b = chunks[c]
            a = min(a, b - 4)
            o = 32 * a
            quant("qz", "sz", o, o + 32 * (b - a), at("zz", s_[:, a:b]))
            for k in range(4):
                mm(4 * (c % 2) + k, 32 * (b - a), [(side("qw", "sw", 16 + 128 * k, 128), side("qz", "sz", o, 32 * (b - a)))])

        def times32(c):
            a, b = chunks[c]
            for k in range(4):
                copy("s", at("z32", s_[:, 128 * a + k:128 * b:4]), at("zz", s_[:, a:b, k:128:4]), 32.0)

        def state(c):
            a, b = chunks[c]
            for k in range(4):
                n = max(128, 32 * (b - a))
                tt(at("xs", s_[:, 8 * a:8 * b, k:16:4]), bank(4 * (c % 2) + k, n - 32 * (b - a), n), at("z32", s_[:, 128 * a + k:128 * b:4]), A.add)

        def scaled(e, j):
            o = X0 + 128 * j
            if j < 12:
                copy(e, w(o, o + 128), at("xs", s_[:, j // 4 * 32:j // 4 * 32 + 32, j % 4 * 4:j % 4 * 4 + 4]), SC)
            else:
                for x in range(2):
                    k = 8 * x + 4 * (j - 12)
                    copy(e, w(o + 64 * x, o + 64 * x + 64), at("xs", s_[:, 96:112, k:k + 4]), SC)
        for c in range(len(chunks)):
            late(("vs", "sv", "s")[c], c)
            place("vvvv" if c else "vvvs", c)
            codes(c)
            times32(c)
            state(c)
        if not last:
            for j in (0, 1, 2, 3, 10, 11, 12, 13, 6):
                scaled("s", j)
            first = len(jobs)
            own(0)
            for j in (8, 9, 4, 5, 7):
                scaled("v", j)
            own(1)
            own(2)
            rows.update(range(first + 1, len(jobs)))
            windows()
            for c in range(3):
                keys(c)
            if t == 0:
                copy("s", sc(8), col(8), -1.0 / C, -6.5 / M)
                copy("s", sc(9), col(8), M - SC)
                copy("s", sc(10), col(4), -8.0, col(8))
                copy("s", sc(11), col(4), 8.0, col(8))
                copy("s", sc(10), sc(10), bias=8.0 * C)
                copy("s", sc(11), sc(11), bias=8.0 * C + 21 * P)
            else:
                quant("qv", "sv", 0, 128, at("vs"))
            for c in range(3):
                turn(c)

    def small(name):
        return at(name, s_[:, 0:30])
    copy("s", small("g3"), small("tf"), 1 / (128 * TS))
    copy("s", small("g4"), small("tf"), 8 / TS, sc(10))
    copy("s", small("g6"), small("tf"), -8 / TS, sc(11))
    ts(small("g1"), small("tf"), 1 / (XE * TS), A.mult, sc(8), A.add)

    def unlay(es, q):
        for k in range(3):
            u = 8 * (EIGHTS[q][1] - 3 + k)
            copy(es[k], at("xo", s_[:, 8 * q:8 * q + 8, 16 * k:16 * k + 16]), at("xs", s_[:, u:u + 8]), SC)
        u = 56 * (q // 2)
        copy(es[3], at("xo", s_[:, 8 * q:8 * q + 8, 48:56]), at("xs", s_[:, u:u + 8, q % 2 * 8:q % 2 * 8 + 8]), SC)

    def result(e, c):
        a, b = ENDS[c]
        quant("qx", "sx", M * a, M * b, at("xo", s_[:, a:b]))
        mm(c, M * (b - a), [(side("qv", "sv", 0, 128), side("qx", "sx", M * a, M * (b - a)))])
        copy(e, at("ys", s_[:, M * a:M * b]), bank(c, 0, M * (b - a)))
    ENDS = [(0, 16), (16, 32)]
    ts(small("g2"), small("g1"), float(C - M), A.mult, sc(9), A.add)
    tt(small("g2"), small("g2"), small("g3"), A.add)
    ts(small("g2"), small("g2"), 8.0 * C - 1, A.min)
    tt(small("g4"), small("g4"), small("g6"), A.min)
    tt(small("g5"), small("g2"), small("g4"), A.max)
    dmas("og", [("y", hbm(T.og[1 - s:8:2, :]), at("g5", s_[:, G * s:G * s + M])) for s in range(2)], 3.0)
    for q in range(4):
        unlay(("ssss", "ssss", "vvss", "vsvv")[q], q)
    for c in range(2):
        result("sv"[c], c)
    oc = [("y", hbm(T.oc[:, 4 * M * a:4 * M * b]), at("qx", s_[:, M * a:M * b], True)) for a, b in ENDS]
    ys = [(e, hbm(T.y[:, M * a:M * b]), at("ys", s_[:, M * a:M * b])) for e, (a, b) in zip("sy", ENDS)]
    dmas("out", oc + [("y", hbm(T.osc[4 * k:4 * k + 4, :]), at("sx", s_[32 * k:32 * k + 4])) for k in range(4)], 1.6)
    dmas("end", ys, 1.6)
    issue()
